import numpy as np
import ml_dtypes


def mxq(x, axis, fmt="e4m3"):
    dtype, down = {"e4m3": (ml_dtypes.float8_e4m3fn, 7), "e5m2": (ml_dtypes.float8_e5m2, 14)}[fmt]
    v = np.moveaxis(np.asarray(x, np.float32).astype(ml_dtypes.bfloat16).astype(np.float64), axis, -1)
    blocks = v.reshape(v.shape[:-1] + (-1, 32))
    amax = np.abs(blocks).max(-1, keepdims=True)
    byte = np.maximum(np.where(amax > 0, np.frexp(amax)[1] - 1 + 127, 0) - down, 1)
    scale = np.exp2(byte - 127.0)
    codes = (blocks / scale).astype(np.float32).astype(dtype).astype(np.float64)
    return np.moveaxis((codes * scale).reshape(v.shape), -1, axis)


WIDE = False


def mx_kscale(k):
    if not WIDE:
        return np.ones(k)
    levels = np.array([10, -10, 5, -5, 0])
    if k % 512:
        return np.exp2(np.random.permutation(np.resize(levels, k // 32))).repeat(32)
    a = np.empty((k // 512, 16))
    for p in range(k // 512):
        a[p, :8] = np.random.permutation(np.resize(levels, 8))
        for g in range(8):
            far = levels[np.abs(levels - a[p, g]) >= 10]
            a[p, g + 8] = far[np.random.randint(len(far))]
    return np.exp2(a.ravel()).repeat(32)


def f64(x):
    return np.asarray(x).astype(np.float64)


def striped(idx):
    return np.tile(idx.reshape(-1, 16).T, (8, 1)).astype(np.uint16)


def unstriped(offs):
    return offs[:16].T.reshape(-1).astype(np.int64)


E2M1 = np.array([0.0, 0.5, 1.0, 1.5, 2.0, 3.0, 4.0, 6.0, -0.0, -0.5, -1.0, -1.5, -2.0, -3.0, -4.0, -6.0])


def pack_weight(w, fmt):
    k, n = w.shape
    w = f64(np.asarray(w, np.float32).astype(ml_dtypes.bfloat16)).reshape(k // 32, 32, n)
    amax = np.abs(w).max(1)
    if fmt == "e4m3":
        byte = np.frexp(amax)[1] - 1 + 127 - 7
    else:
        mant, ex = np.frexp(amax / 6.0)
        byte = np.where(mant > 0.5, ex, ex - 1) + 127
    byte = np.clip(np.where(amax > 0, byte, 1), 1, 254)
    scaled = (w * np.exp2(127.0 - byte)[:, None, :]).reshape(k, n).astype(np.float32)
    by_word = np.ascontiguousarray(scaled.reshape(k // 512, 128, 4, n).transpose(0, 1, 3, 2))
    if fmt == "e4m3":
        words = by_word.astype(ml_dtypes.float8_e4m3fn).view(np.uint8)
    else:
        c = by_word.astype(ml_dtypes.float4_e2m1fn).view(np.uint8) & 0xF
        words = (c[..., 0::2] | (c[..., 1::2] << 4)).reshape(k // 512, 128, 2 * n)
    return np.ascontiguousarray(words), np.ascontiguousarray(byte.astype(np.uint8).reshape(k // 512, 16, n))


def unpack_weight(words, scales, fmt):
    g, _, n = scales.shape
    words = np.ascontiguousarray(words).reshape(g, 128, n, -1)
    if fmt == "e4m3":
        vals = words.view(ml_dtypes.float8_e4m3fn).astype(np.float64)
    else:
        nib = np.empty((g, 128, n, 4), np.uint8)
        nib[..., 0::2] = words & 0xF
        nib[..., 1::2] = words >> 4
        vals = E2M1[nib]
    vals = vals * np.repeat(np.exp2(scales.astype(np.float64) - 127.0), 8, axis=1)[..., None]
    return vals.transpose(0, 1, 3, 2).reshape(g * 512, n)


def gelu(v):
    return 0.5 * v * (1.0 + np.tanh(np.sqrt(2.0 / np.pi) * (v + 0.044715 * v**3)))


K, H, N, T, S = 1024, 1024, 512, 2048, 1024

def setup_inputs():
    n = np.random.standard_normal
    s = mx_kscale(K)[:, None]
    u = mx_kscale(H)[:, None]
    tab_words, tab_scales = pack_weight(n((K, T)) * s, "e4m3")
    w4_words, w4_scales = pack_weight(n((K, H)) / np.sqrt(K) / s, "e2m1")
    return {
        "tab_words": tab_words,
        "tab_scales": tab_scales,
        "offs": striped(np.random.permutation(T)[:S]),
        "w4_words": w4_words,
        "w4_scales": w4_scales,
        "peak": (np.exp(0.3 * n(H)) * u[:, 0]).astype(np.float32),
        "w2": (n((H, N)) / np.sqrt(H) / u).astype(np.float32),
        "drive": (0.5 * n(N)).astype(np.float32),
        "decay": np.random.uniform(0.5, 0.95, N).astype(np.float32),
        "gT": n((N, T)).astype(np.float32),
    }

def reference(tab_words, tab_scales, offs, w4_words, w4_scales, peak, w2, drive, decay, gT):
    v = unpack_weight(tab_words, tab_scales, "e4m3")[:, unstriped(offs)]
    w4 = unpack_weight(w4_words, w4_scales, "e2m1")
    h = f64(peak)[:, None] * np.tanh(w4.T @ v)
    y = mxq(f64(w2), 0, "e4m3").T @ mxq(h, 0, "e4m3")
    g = f64(gT)[:, unstriped(offs)]
    new = f64(decay)[:, None] * g + (y + f64(drive)[:, None])
    out = f64(gT).copy()
    out[:, unstriped(offs)] = new
    return out

@@ -1,0 +1,261 @@
+from contextlib import ExitStack
+
+import concourse.mybir as mybir
+from concourse.masks import make_identity
+
+K, H, N, T, S = 1024, 1024, 512, 2048, 1024
+FLOPS = 2 * K * H * S + 2 * H * N * S
+
+F32 = mybir.dt.float32
+BF16 = mybir.dt.bfloat16
+I32 = mybir.dt.int32
+U32 = mybir.dt.uint32
+U16 = mybir.dt.uint16
+U8 = mybir.dt.uint8
+FP8X4 = mybir.dt.float8_e4m3fn_x4
+FP4X4 = mybir.dt.float4_e2m1fn_x4
+ACT = mybir.ActivationFunctionType
+ALU = mybir.AluOpType
+
+P = 128
+BANK = 512
+HALF = 512
+SLICES = ((0, 256), (256, 256), (512, 256), (768, 256))
+
+
+def tile_list_place_cell_replay_kernel(tc, tab_words, tab_scales, offs, w4_words, w4_scales, peak, w2, drive, decay, gT, out):
+    nc = tc.nc
+    with ExitStack() as ctx:
+        keep = ctx.enter_context(tc.tile_pool(name="keep", bufs=1))
+        pre_pool = ctx.enter_context(tc.psum_pool(name="pre", bufs=6))
+        y_pool = ctx.enter_context(tc.psum_pool(name="ypsum", bufs=2))
+
+        def held(shape, dtype, name):
+            return keep.tile(shape, dtype, name=name, align_bytes=64)
+
+        offsets = keep.tile([P, S // 16], U16, name="offsets")
+        nc.sync.dma_start(offsets[:], offs)
+
+        def listed(window, start, width):
+            return window.indirect(offsets[:, start // 16 : (start + width) // 16])
+
+        tab_s = held([P, T], U8, "tab_s")
+        nc.gpsimd.memset(tab_s[:].bitcast(I32), 0)
+        w4_s_raw = held([P, 2 * H], U8, "w4_s_raw")
+        nc.vector.memset(w4_s_raw[:].bitcast(I32), 0)
+        v_s1 = held([P, S], U8, "v_s1")
+        nc.vector.memset(v_s1[:].bitcast(I32), 0)
+        for q in range(4):
+            nc.sync.dma_start(tab_s[32 * q : 32 * q + 8, :].bitcast(I32), tab_scales[:, 4 * q : 4 * q + 4, :].bitcast(I32))
+        tab_w = [held([P, T], I32, "tab_w%d" % a) for a in range(2)]
+        w4_raw = held([P, 2 * H // 2], I32, "w4_raw")
+        nc.sync.dma_start(tab_w[0][:], tab_words[0].rearrange("p t i -> p (t i)").bitcast(I32))
+        nc.sync.dma_start(w4_raw[:].rearrange("p (a c) -> p a c", a=2), w4_words.bitcast(I32).rearrange("a p c -> p a c"))
+        for q in range(4):
+            nc.sync.dma_start(
+                w4_s_raw[32 * q : 32 * q + 4, :].bitcast(I32).rearrange("p (a c) -> p a c", a=2),
+                w4_scales[:, 4 * q : 4 * q + 4, :].bitcast(I32).rearrange("a r c -> r a c"),
+            )
+        nc.sync.dma_start(tab_w[1][:], tab_words[1].rearrange("p t i -> p (t i)").bitcast(I32))
+        rows = held([P, P], F32, "rows")
+        nc.gpsimd.memset(rows[:], 0.0)
+        nc.gpsimd.dma_start(rows[8:12, :], decay.rearrange("(m p) -> m p", p=P))
+        for b in range(2):
+            nc.gpsimd.dma_start(
+                rows[4 * b : 4 * b + 4, :].rearrange("t (g e) -> t g e", e=8),
+                peak[512 * b : 512 * (b + 1)].rearrange("(g t e) -> t g e", t=4, e=8),
+            )
+        nc.gpsimd.dma_start(rows[12:16, :], drive.rearrange("(m p) -> m p", p=P))
+        identity = held([P, P], F32, "identity")
+        make_identity(nc, identity[:])
+        turned = y_pool.tile([P, BANK], F32, name="acc")
+        nc.tensor.transpose(turned[:, 0:P], rows[:], identity[:])
+        columns = held([P, 16], F32, "columns")
+        nc.scalar.copy(columns[:], turned[:, 0:16])
+        peak_col = [columns[:, 0:4], columns[:, 4:8]]
+        decay_col = columns[:, 8:12]
+        drive_col = columns[:, 12:16]
+
+        g_tile = [keep.tile([P, T], F32, name="g_tile%d" % m) for m in range(4)]
+        w2_raw = [held([P, 4, N], F32, "w2_raw%d" % b) for b in range(2)]
+
+        def load_g(m):
+            nc.sync.dma_start(g_tile[m][:], gT[P * m : P * (m + 1), :])
+
+        def load_w2(b):
+            w2_rows = w2[512 * b : 512 * (b + 1), :].rearrange("(g t e) n -> t g e n", t=4, e=8)
+            for t in range(4):
+                nc.sync.dma_start(w2_raw[b][:, t, :], w2_rows[t])
+
+        load_g(0)
+        load_w2(0)
+        load_g(1)
+        load_w2(1)
+        load_g(2)
+        load_g(3)
+
+        v_s0 = held([P, S], U8, "v_s0")
+        nc.vector.tensor_copy(v_s0[:], listed(tab_s[:], 0, S))
+        nc.scalar.dma_start(v_s1[0:112, :].bitcast(I32), v_s0[4:116, :].bitcast(I32))
+        v_s = [v_s0, v_s1]
+
+        decay_wide = [held([P, HALF], F32, "decay_wide%d" % m) for m in range(4)]
+        for m in range(4):
+            nc.scalar.copy(decay_wide[m][:], decay_col[:, m : m + 1].to_broadcast([P, HALF]))
+
+        v_w = {}
+
+        def gather_words(a, i):
+            start, width = SLICES[i]
+            v_w[a, i] = held([P, width], U32, "v_w%d_%d" % (a, i))
+            nc.vector.tensor_copy(v_w[a, i][:], listed(tab_w[a][:].bitcast(U32), start, width))
+
+        for i in range(4):
+            gather_words(0, i)
+
+        w4_w = held([P, 2 * H // 2], I32, "w4_w")
+        nc.vector.tensor_copy(
+            w4_w[:].rearrange("p (ab t g w) -> p ab t g w", t=4, g=16, w=4),
+            w4_raw[:].rearrange("p (ab g t w) -> p ab t g w", t=4, g=16, w=4),
+        )
+        w4_s = held([P, 2 * H], U8, "w4_s")
+        nc.vector.tensor_copy(
+            w4_s[:].bitcast(I32).rearrange("p (ab t g w) -> p ab t g w", t=4, g=16, w=2),
+            w4_s_raw[:].bitcast(I32).rearrange("p (ab g t w) -> p ab t g w", t=4, g=16, w=2),
+        )
+        w4_bytes = w4_w[:].bitcast(U8)
+
+        for i in range(4):
+            gather_words(1, i)
+
+        def first_product(bank, i, pieces):
+            start = SLICES[i][0]
+            steps = [(a,) + piece for a in range(2) for piece in pieces]
+            for s, (a, b, t, j0, width, c0) in enumerate(steps):
+                col = a * H + b * 512 + t * P
+                nc.tensor.matmul_mx(
+                    out=bank[:, c0 : c0 + width],
+                    lhsT=w4_bytes[:, 2 * col : 2 * (col + P)].bitcast(FP4X4),
+                    lhsT_scale=w4_s[:, col : col + P],
+                    rhs=v_w[a, i][:, j0 : j0 + width].bitcast(FP8X4),
+                    rhs_scale=v_s[a][:, start + j0 : start + j0 + width],
+                    start=(s == 0),
+                    stop=(s == len(steps) - 1),
+                )
+
+        dg = [held([P, S], F32, "dg%d" % m) for m in range(4)]
+
+        def gather_g(m):
+            for half in range(2):
+                nc.vector.tensor_tensor(dg[m][:, HALF * half : HALF * (half + 1)], listed(g_tile[m][:], HALF * half, HALF), decay_wide[m][:], ALU.mult)
+
+        h_il = {}
+        h_w = {}
+        h_s = {}
+
+        def quantize_h(i, b):
+            width = SLICES[i][1]
+            h_w[i, b] = held([P, width], U32, "h_w%d_%d" % (i, b))
+            h_s[i, b] = held([P, width], U8, "h_s%d_%d" % (i, b))
+            nc.vector.quantize_mx(out=h_w[i, b][:].bitcast(FP8X4), scales=h_s[i, b][:], in_=h_il[i, b][:])
+
+        def units_on_vector(i, b):
+            width = SLICES[i][1]
+            h_il[i, b] = held([P, width * 4], BF16, "h_il%d_%d" % (i, b))
+            th = held([P, width * 4], F32, "th%d_%d" % (i, b))
+            for jj in range(width // P):
+                bank = pre_pool.tile([P, BANK], F32, name="pre")
+                first_product(bank, i, [(b, t, jj * P, P, t * P) for t in range(4)])
+                nc.scalar.activation(
+                    th[:, jj * BANK : (jj + 1) * BANK].rearrange("p (j t) -> p j t", t=4),
+                    bank[:].rearrange("p (t j) -> p j t", t=4),
+                    ACT.Tanh,
+                )
+            nc.vector.tensor_tensor(
+                h_il[i, b][:].rearrange("p (j t) -> p j t", t=4),
+                th[:].rearrange("p (j t) -> p j t", t=4),
+                peak_col[b].unsqueeze(1).to_broadcast([P, width, 4]),
+                ALU.mult,
+            )
+
+        def units_on_scalar(i, b):
+            width = SLICES[i][1]
+            h_il[i, b] = held([P, width * 4], BF16, "h_il%d_%d" % (i, b))
+            th = held([P, 4 * width], F32, "th%d_%d" % (i, b))
+            hb = held([P, 4 * width], BF16, "hb%d_%d" % (i, b))
+            per_bank = BANK // width
+            step = width if width == BANK else P
+            for t0 in range(0, 4, per_bank):
+                bank = pre_pool.tile([P, BANK], F32, name="pre")
+                first_product(bank, i, [(b, t0 + u, j0, step, u * width + j0) for u in range(per_bank) for j0 in range(0, width, step)])
+                nc.scalar.activation(th[:, t0 * width : t0 * width + BANK], bank[:], ACT.Tanh)
+                for t in range(t0, t0 + per_bank):
+                    nc.scalar.activation(hb[:, t * width : (t + 1) * width], th[:, t * width : (t + 1) * width], ACT.Copy, scale=peak_col[b][:, t : t + 1])
+            nc.scalar.copy(
+                h_il[i, b][:].rearrange("p (c i t) -> p c t i", i=4, t=4),
+                hb[:].rearrange("p (t c i) -> p c t i", i=4, t=4),
+            )
+
+        w2_w = {}
+        w2_s = {}
+
+        def prepare_w2(b, half):
+            cols = N // 2
+            il = held([P, cols * 4], BF16, "w2_il%d_%d" % (b, half))
+            nc.scalar.copy(
+                il[:].rearrange("p (c i t) -> p c t i", i=4, t=4),
+                w2_raw[b][:, :, cols * half : cols * (half + 1)].rearrange("p t (c i) -> p c t i", i=4),
+            )
+            w2_w[b, half] = held([P, cols], U32, "w2_w%d_%d" % (b, half))
+            w2_s[b, half] = held([P, cols], U8, "w2_s%d_%d" % (b, half))
+            nc.vector.quantize_mx(out=w2_w[b, half][:].bitcast(FP8X4), scales=w2_s[b, half][:], in_=il[:])
+
+        def replace_columns(i, m):
+            start, width = SLICES[i]
+            acc = y_pool.tile([P, BANK], F32, name="acc")
+            c0 = (m % 2) * P
+            for b in range(2):
+                nc.tensor.matmul_mx(
+                    out=acc[:, 0:width],
+                    lhsT=w2_w[b, m // 2][:, c0 : c0 + P].bitcast(FP8X4),
+                    lhsT_scale=w2_s[b, m // 2][:, c0 : c0 + P],
+                    rhs=h_w[i, b][:].bitcast(FP8X4),
+                    rhs_scale=h_s[i, b][:],
+                    start=(b == 0),
+                    stop=(b == 1),
+                )
+            yd = held([P, width], F32, "yd%d_%d" % (i, m))
+            nc.scalar.activation(yd[:], acc[:, 0:width], ACT.Identity, bias=drive_col[:, m : m + 1])
+            nc.vector.tensor_tensor(listed(g_tile[m][:], start, width), dg[m][:, start : start + width], yd[:], ALU.add)
+
+        def units(i, b):
+            units_on_scalar(i, b)
+            quantize_h(i, b)
+
+        gather_g(0)
+        for b in range(2):
+            units_on_vector(0, b)
+            quantize_h(0, b)
+        for b in range(2):
+            prepare_w2(b, 0)
+            prepare_w2(b, 1)
+            gather_g(1 + b)
+        gather_g(3)
+        units(1, 0)
+        units(1, 1)
+        for m in range(4):
+            replace_columns(0, m)
+        units(2, 0)
+        replace_columns(1, 0)
+        replace_columns(1, 1)
+        units(2, 1)
+        replace_columns(1, 2)
+        replace_columns(1, 3)
+        units(3, 0)
+        replace_columns(2, 0)
+        units(3, 1)
+        for m in range(4):
+            if m < 3:
+                replace_columns(2, m + 1)
+            replace_columns(3, m)
+            nc.sync.dma_start(out[P * m : P * (m + 1), :], g_tile[m][:])

@@ -27,8 +27,11 @@ def tile_list_place_cell_replay_kernel(tc, tab_words, tab_scales, offs, w4_words
     nc = tc.nc
     with ExitStack() as ctx:
         keep = ctx.enter_context(tc.tile_pool(name="keep", bufs=1))
-        pre_pool = ctx.enter_context(tc.psum_pool(name="pre", bufs=6))
-        y_pool = ctx.enter_context(tc.psum_pool(name="ypsum", bufs=2))
+        ring = ctx.enter_context(tc.tile_pool(name="ring", bufs=2))
+        psum = ctx.enter_context(tc.psum_pool(name="psum", bufs=1))
+
+        def psum_bank(number):
+            return psum.tile([P, BANK], F32, name="bank%d" % number)
 
         def held(shape, dtype, name):
             return keep.tile(shape, dtype, name=name, align_bytes=64)
@@ -59,22 +62,20 @@ def tile_list_place_cell_replay_kernel(tc, tab_words, tab_scales, offs, w4_words
         nc.sync.dma_start(tab_w[1][:], tab_words[1].rearrange("p t i -> p (t i)").bitcast(I32))
         rows = held([P, P], F32, "rows")
         nc.gpsimd.memset(rows[:], 0.0)
+        identity = held([P, P], F32, "identity")
+        make_identity(nc, identity[:])
         nc.gpsimd.dma_start(rows[8:12, :], decay.rearrange("(m p) -> m p", p=P))
         for b in range(2):
             nc.gpsimd.dma_start(
                 rows[4 * b : 4 * b + 4, :].rearrange("t (g e) -> t g e", e=8),
                 peak[512 * b : 512 * (b + 1)].rearrange("(g t e) -> t g e", t=4, e=8),
             )
-        nc.gpsimd.dma_start(rows[12:16, :], drive.rearrange("(m p) -> m p", p=P))
-        identity = held([P, P], F32, "identity")
-        make_identity(nc, identity[:])
-        turned = y_pool.tile([P, BANK], F32, name="acc")
+        turned = psum_bank(7)
         nc.tensor.transpose(turned[:, 0:P], rows[:], identity[:])
-        columns = held([P, 16], F32, "columns")
-        nc.scalar.copy(columns[:], turned[:, 0:16])
+        columns = held([P, 12], F32, "columns")
+        nc.scalar.copy(columns[:], turned[:, 0:12])
         peak_col = [columns[:, 0:4], columns[:, 4:8]]
         decay_col = columns[:, 8:12]
-        drive_col = columns[:, 12:16]
 
         g_tile = [keep.tile([P, T], F32, name="g_tile%d" % m) for m in range(4)]
         w2_raw = [held([P, 4, N], F32, "w2_raw%d" % b) for b in range(2)]
@@ -88,20 +89,23 @@ def tile_list_place_cell_replay_kernel(tc, tab_words, tab_scales, offs, w4_words
                 nc.sync.dma_start(w2_raw[b][:, t, :], w2_rows[t])
 
         load_g(0)
-        load_w2(0)
         load_g(1)
+        load_w2(0)
         load_w2(1)
         load_g(2)
         load_g(3)
 
         v_s0 = held([P, S], U8, "v_s0")
         nc.vector.tensor_copy(v_s0[:], listed(tab_s[:], 0, S))
-        nc.scalar.dma_start(v_s1[0:112, :].bitcast(I32), v_s0[4:116, :].bitcast(I32))
+        nc.gpsimd.dma_start(v_s1[0:112, :].bitcast(I32), v_s0[4:116, :].bitcast(I32))
         v_s = [v_s0, v_s1]
+        drive_col = held([P, 4], F32, "drive_col")
+        with nc.allow_non_contiguous_dma(reason="one value a partition"):
+            nc.gpsimd.dma_start(drive_col[:], drive.rearrange("(m p) -> p m", p=P))
 
         decay_wide = [held([P, HALF], F32, "decay_wide%d" % m) for m in range(4)]
         for m in range(4):
-            nc.scalar.copy(decay_wide[m][:], decay_col[:, m : m + 1].to_broadcast([P, HALF]))
+            nc.gpsimd.tensor_scalar(decay_wide[m][:], decay_col[:, m : m + 1].to_broadcast([P, HALF]), 1.0, 0.0, ALU.mult, ALU.add)
 
         v_w = {}
 
@@ -164,7 +168,7 @@ def tile_list_place_cell_replay_kernel(tc, tab_words, tab_scales, offs, w4_words
             h_il[i, b] = held([P, width * 4], BF16, "h_il%d_%d" % (i, b))
             th = held([P, width * 4], F32, "th%d_%d" % (i, b))
             for jj in range(width // P):
-                bank = pre_pool.tile([P, BANK], F32, name="pre")
+                bank = psum_bank((4 * i + 2 * b + jj) % 8)
                 first_product(bank, i, [(b, t, jj * P, P, t * P) for t in range(4)])
                 nc.scalar.activation(
                     th[:, jj * BANK : (jj + 1) * BANK].rearrange("p (j t) -> p j t", t=4),
@@ -181,16 +185,15 @@ def tile_list_place_cell_replay_kernel(tc, tab_words, tab_scales, offs, w4_words
         def units_on_scalar(i, b):
             width = SLICES[i][1]
             h_il[i, b] = held([P, width * 4], BF16, "h_il%d_%d" % (i, b))
-            th = held([P, 4 * width], F32, "th%d_%d" % (i, b))
-            hb = held([P, 4 * width], BF16, "hb%d_%d" % (i, b))
-            per_bank = BANK // width
-            step = width if width == BANK else P
-            for t0 in range(0, 4, per_bank):
-                bank = pre_pool.tile([P, BANK], F32, name="pre")
-                first_product(bank, i, [(b, t0 + u, j0, step, u * width + j0) for u in range(per_bank) for j0 in range(0, width, step)])
-                nc.scalar.activation(th[:, t0 * width : t0 * width + BANK], bank[:], ACT.Tanh)
-                for t in range(t0, t0 + per_bank):
-                    nc.scalar.activation(hb[:, t * width : (t + 1) * width], th[:, t * width : (t + 1) * width], ACT.Copy, scale=peak_col[b][:, t : t + 1])
+            hb = keep.tile([P, 4 * width], BF16, name="hb", tag="unit%d_%d" % (i, b))
+            for u in range(2):
+                bank = psum_bank((4 * i + 2 * b + u) % 8)
+                first_product(bank, i, [(b, 2 * u + e, j0, P, e * width + j0) for e in range(2) for j0 in range(0, width, P)])
+                th = ring.tile([P, BANK], F32, name="th")
+                nc.scalar.activation(th[:], bank[:], ACT.Tanh)
+                for e in range(2):
+                    t = 2 * u + e
+                    nc.scalar.activation(hb[:, t * width : (t + 1) * width], th[:, e * width : (e + 1) * width], ACT.Copy, scale=peak_col[b][:, t : t + 1])
             nc.scalar.copy(
                 h_il[i, b][:].rearrange("p (c i t) -> p c t i", i=4, t=4),
                 hb[:].rearrange("p (t c i) -> p c t i", i=4, t=4),
@@ -210,52 +213,63 @@ def tile_list_place_cell_replay_kernel(tc, tab_words, tab_scales, offs, w4_words
             w2_s[b, half] = held([P, cols], U8, "w2_s%d_%d" % (b, half))
             nc.vector.quantize_mx(out=w2_w[b, half][:].bitcast(FP8X4), scales=w2_s[b, half][:], in_=il[:])
 
-        def replace_columns(i, m):
-            start, width = SLICES[i]
-            acc = y_pool.tile([P, BANK], F32, name="acc")
-            c0 = (m % 2) * P
-            for b in range(2):
-                nc.tensor.matmul_mx(
-                    out=acc[:, 0:width],
-                    lhsT=w2_w[b, m // 2][:, c0 : c0 + P].bitcast(FP8X4),
-                    lhsT_scale=w2_s[b, m // 2][:, c0 : c0 + P],
-                    rhs=h_w[i, b][:].bitcast(FP8X4),
-                    rhs_scale=h_s[i, b][:],
-                    start=(b == 0),
-                    stop=(b == 1),
-                )
-            yd = held([P, width], F32, "yd%d_%d" % (i, m))
-            nc.scalar.activation(yd[:], acc[:, 0:width], ACT.Identity, bias=drive_col[:, m : m + 1])
-            nc.vector.tensor_tensor(listed(g_tile[m][:], start, width), dg[m][:, start : start + width], yd[:], ALU.add)
+        def second_product(bank_number, jobs):
+            acc = psum_bank(bank_number)
+            for u, (i, m) in enumerate(jobs):
+                width = SLICES[i][1]
+                c0 = (m % 2) * P
+                for b in range(2):
+                    nc.tensor.matmul_mx(
+                        out=acc[:, u * width : (u + 1) * width],
+                        lhsT=w2_w[b, m // 2][:, c0 : c0 + P].bitcast(FP8X4),
+                        lhsT_scale=w2_s[b, m // 2][:, c0 : c0 + P],
+                        rhs=h_w[i, b][:].bitcast(FP8X4),
+                        rhs_scale=h_s[i, b][:],
+                        start=(b == 0),
+                        stop=(b == 1),
+                    )
+            return acc
+
+        def replace_columns(bank_number, jobs, room):
+            acc = second_product(bank_number, jobs)
+            yd = keep.tile([P, BANK], F32, name="yd", tag=room)
+            for u, (i, m) in enumerate(jobs):
+                start, width = SLICES[i]
+                cols = slice(u * width, (u + 1) * width)
+                nc.scalar.activation(yd[:, cols], acc[:, cols], ACT.Identity, bias=drive_col[:, m : m + 1])
+                nc.vector.tensor_tensor(listed(g_tile[m][:], start, width), dg[m][:, start : start + width], yd[:, cols], ALU.add)
+                if i == 3:
+                    nc.sync.dma_start(out[P * m : P * (m + 1), :], g_tile[m][:])
 
         def units(i, b):
-            units_on_scalar(i, b)
+            if 2 * i + b < 3:
+                units_on_vector(i, b)
+            else:
+                units_on_scalar(i, b)
             quantize_h(i, b)
 
         gather_g(0)
-        for b in range(2):
-            units_on_vector(0, b)
-            quantize_h(0, b)
-        for b in range(2):
-            prepare_w2(b, 0)
-            prepare_w2(b, 1)
-            gather_g(1 + b)
-        gather_g(3)
+        units(0, 0)
+        units(0, 1)
+        prepare_w2(0, 0)
+        prepare_w2(0, 1)
+        gather_g(1)
         units(1, 0)
+        prepare_w2(1, 0)
+        prepare_w2(1, 1)
+        gather_g(2)
+        gather_g(3)
         units(1, 1)
-        for m in range(4):
-            replace_columns(0, m)
         units(2, 0)
-        replace_columns(1, 0)
-        replace_columns(1, 1)
+        replace_columns(0, [(0, 0), (0, 1)], "unit2_0")
+        replace_columns(1, [(0, 2), (0, 3)], "ya")
         units(2, 1)
-        replace_columns(1, 2)
-        replace_columns(1, 3)
+        replace_columns(2, [(1, 0), (1, 1)], "unit2_1")
+        replace_columns(3, [(1, 2), (1, 3)], "yb")
         units(3, 0)
-        replace_columns(2, 0)
+        replace_columns(5, [(2, 0), (2, 1)], "unit3_0")
         units(3, 1)
-        for m in range(4):
-            if m < 3:
-                replace_columns(2, m + 1)
-            replace_columns(3, m)
-            nc.sync.dma_start(out[P * m : P * (m + 1), :], g_tile[m][:])
+        replace_columns(7, [(2, 2)], "unit3_1")
+        replace_columns(0, [(3, 0), (3, 1)], "yc")
+        replace_columns(1, [(3, 2), (2, 3)], "yd")
+        replace_columns(2, [(3, 3)], "ye")

@@ -18,9 +18,11 @@ ACT = mybir.ActivationFunctionType
 ALU = mybir.AluOpType
 
 P = 128
+PASS = 512
 BANK = 512
-HALF = 512
-SLICES = ((0, 256), (256, 256), (512, 256), (768, 256))
+GROUP = 16
+FIRST, SECOND, THIRD = (0, 512), (512, 256), (768, 256)
+LATER = (512, 512)
 
 
 def tile_list_place_cell_replay_kernel(tc, tab_words, tab_scales, offs, w4_words, w4_scales, peak, w2, drive, decay, gT, out):
@@ -30,17 +32,21 @@ def tile_list_place_cell_replay_kernel(tc, tab_words, tab_scales, offs, w4_words
         ring = ctx.enter_context(tc.tile_pool(name="ring", bufs=2))
         psum = ctx.enter_context(tc.psum_pool(name="psum", bufs=1))
 
+        def held(shape, dtype, name, room=None):
+            return keep.tile(shape, dtype, name=name, tag=room or name, align_bytes=64)
+
         def psum_bank(number):
             return psum.tile([P, BANK], F32, name="bank%d" % number)
 
-        def held(shape, dtype, name):
-            return keep.tile(shape, dtype, name=name, align_bytes=64)
-
-        offsets = keep.tile([P, S // 16], U16, name="offsets")
+        offsets = keep.tile([P, S // GROUP], U16, name="offsets")
         nc.sync.dma_start(offsets[:], offs)
 
-        def listed(window, start, width):
-            return window.indirect(offsets[:, start // 16 : (start + width) // 16])
+        def listed(window, part):
+            first, count = part
+            return window.indirect(offsets[:, first // GROUP : (first + count) // GROUP])
+
+        def columns_of(part):
+            return slice(part[0], part[0] + part[1])
 
         tab_s = held([P, T], U8, "tab_s")
         nc.gpsimd.memset(tab_s[:].bitcast(I32), 0)
@@ -48,76 +54,63 @@ def tile_list_place_cell_replay_kernel(tc, tab_words, tab_scales, offs, w4_words
         nc.vector.memset(w4_s_raw[:].bitcast(I32), 0)
         v_s1 = held([P, S], U8, "v_s1")
         nc.vector.memset(v_s1[:].bitcast(I32), 0)
+        tab_w = [held([P, T], I32, "tab_w%d" % a) for a in range(2)]
+        w4_raw = held([P, H], I32, "w4_raw")
+        nc.sync.dma_start(tab_w[0][:], tab_words[0].rearrange("p t i -> p (t i)").bitcast(I32))
         for q in range(4):
             nc.sync.dma_start(tab_s[32 * q : 32 * q + 8, :].bitcast(I32), tab_scales[:, 4 * q : 4 * q + 4, :].bitcast(I32))
-        tab_w = [held([P, T], I32, "tab_w%d" % a) for a in range(2)]
-        w4_raw = held([P, 2 * H // 2], I32, "w4_raw")
-        nc.sync.dma_start(tab_w[0][:], tab_words[0].rearrange("p t i -> p (t i)").bitcast(I32))
         nc.sync.dma_start(w4_raw[:].rearrange("p (a c) -> p a c", a=2), w4_words.bitcast(I32).rearrange("a p c -> p a c"))
+        nc.sync.dma_start(tab_w[1][:], tab_words[1].rearrange("p t i -> p (t i)").bitcast(I32))
         for q in range(4):
             nc.sync.dma_start(
                 w4_s_raw[32 * q : 32 * q + 4, :].bitcast(I32).rearrange("p (a c) -> p a c", a=2),
                 w4_scales[:, 4 * q : 4 * q + 4, :].bitcast(I32).rearrange("a r c -> r a c"),
             )
-        nc.sync.dma_start(tab_w[1][:], tab_words[1].rearrange("p t i -> p (t i)").bitcast(I32))
+
         rows = held([P, P], F32, "rows")
         nc.gpsimd.memset(rows[:], 0.0)
-        identity = held([P, P], F32, "identity")
-        make_identity(nc, identity[:])
         nc.gpsimd.dma_start(rows[8:12, :], decay.rearrange("(m p) -> m p", p=P))
         for b in range(2):
             nc.gpsimd.dma_start(
                 rows[4 * b : 4 * b + 4, :].rearrange("t (g e) -> t g e", e=8),
-                peak[512 * b : 512 * (b + 1)].rearrange("(g t e) -> t g e", t=4, e=8),
+                peak[PASS * b : PASS * (b + 1)].rearrange("(g t e) -> t g e", t=4, e=8),
             )
+        nc.gpsimd.dma_start(rows[12:16, :], drive.rearrange("(m p) -> m p", p=P))
+        identity = held([P, P], F32, "identity")
+        make_identity(nc, identity[:])
         turned = psum_bank(7)
         nc.tensor.transpose(turned[:, 0:P], rows[:], identity[:])
-        columns = held([P, 12], F32, "columns")
-        nc.scalar.copy(columns[:], turned[:, 0:12])
-        peak_col = [columns[:, 0:4], columns[:, 4:8]]
-        decay_col = columns[:, 8:12]
+        per_partition = held([P, 16], F32, "per_partition")
+        nc.scalar.copy(per_partition[:], turned[:, 0:16])
+        peak_col = [per_partition[:, 0:4], per_partition[:, 4:8]]
+        decay_col = per_partition[:, 8:12]
+        drive_col = per_partition[:, 12:16]
 
-        g_tile = [keep.tile([P, T], F32, name="g_tile%d" % m) for m in range(4)]
-        w2_raw = [held([P, 4, N], F32, "w2_raw%d" % b) for b in range(2)]
+        g_tile = {}
 
-        def load_g(m):
+        def load_g(m, room):
+            g_tile[m] = held([P, T], F32, "g_tile%d" % m, room)
             nc.sync.dma_start(g_tile[m][:], gT[P * m : P * (m + 1), :])
 
-        def load_w2(b):
-            w2_rows = w2[512 * b : 512 * (b + 1), :].rearrange("(g t e) n -> t g e n", t=4, e=8)
-            for t in range(4):
-                nc.sync.dma_start(w2_raw[b][:, t, :], w2_rows[t])
-
-        load_g(0)
-        load_g(1)
-        load_w2(0)
-        load_w2(1)
-        load_g(2)
-        load_g(3)
-
-        v_s0 = held([P, S], U8, "v_s0")
-        nc.vector.tensor_copy(v_s0[:], listed(tab_s[:], 0, S))
-        nc.gpsimd.dma_start(v_s1[0:112, :].bitcast(I32), v_s0[4:116, :].bitcast(I32))
+        v_w = [held([P, S], U32, "v_w%d" % a) for a in range(2)]
+        nc.vector.tensor_copy(v_w[0][:], listed(tab_w[0][:].bitcast(U32), (0, S)))
+        v_s0 = held([P, S], U8, "v_s0", room="tab_w0")
+        nc.vector.tensor_copy(v_s0[:], listed(tab_s[:], (0, S)))
+        nc.scalar.dma_start(v_s1[0:112, :].bitcast(I32), v_s0[4:116, :].bitcast(I32))
         v_s = [v_s0, v_s1]
-        drive_col = held([P, 4], F32, "drive_col")
-        with nc.allow_non_contiguous_dma(reason="one value a partition"):
-            nc.gpsimd.dma_start(drive_col[:], drive.rearrange("(m p) -> p m", p=P))
+        load_g(0, None)
 
-        decay_wide = [held([P, HALF], F32, "decay_wide%d" % m) for m in range(4)]
+        decay_wide = [held([P, BANK], F32, "decay_wide%d" % m) for m in range(4)]
         for m in range(4):
-            nc.gpsimd.tensor_scalar(decay_wide[m][:], decay_col[:, m : m + 1].to_broadcast([P, HALF]), 1.0, 0.0, ALU.mult, ALU.add)
+            nc.gpsimd.tensor_scalar(decay_wide[m][:], decay_col[:, m : m + 1].to_broadcast([P, BANK]), 1.0, 0.0, ALU.mult, ALU.add)
 
-        v_w = {}
+        w2_raw = held([P, 2, 4, N], F32, "w2_raw", room="tab_s")
+        w2_rows = w2.rearrange("(b g t e) n -> b t g e n", b=2, t=4, e=8)
+        for b in range(2):
+            for t in range(4):
+                nc.sync.dma_start(w2_raw[:, b, t, :], w2_rows[b, t])
 
-        def gather_words(a, i):
-            start, width = SLICES[i]
-            v_w[a, i] = held([P, width], U32, "v_w%d_%d" % (a, i))
-            nc.vector.tensor_copy(v_w[a, i][:], listed(tab_w[a][:].bitcast(U32), start, width))
-
-        for i in range(4):
-            gather_words(0, i)
-
-        w4_w = held([P, 2 * H // 2], I32, "w4_w")
+        w4_w = held([P, H], I32, "w4_w")
         nc.vector.tensor_copy(
             w4_w[:].rearrange("p (ab t g w) -> p ab t g w", t=4, g=16, w=4),
             w4_raw[:].rearrange("p (ab g t w) -> p ab t g w", t=4, g=16, w=4),
@@ -128,148 +121,129 @@ def tile_list_place_cell_replay_kernel(tc, tab_words, tab_scales, offs, w4_words
             w4_s_raw[:].bitcast(I32).rearrange("p (ab g t w) -> p ab t g w", t=4, g=16, w=2),
         )
         w4_bytes = w4_w[:].bitcast(U8)
+        load_g(1, "w4_raw")
+        load_g(2, "w4_s_raw")
+        load_g(3, "rows")
+        for part in (FIRST, LATER):
+            nc.vector.tensor_copy(v_w[1][:, columns_of(part)], listed(tab_w[1][:].bitcast(U32), part))
 
-        for i in range(4):
-            gather_words(1, i)
+        decayed = [held([P, S], F32, "decayed%d" % m) for m in range(4)]
 
-        def first_product(bank, i, pieces):
-            start = SLICES[i][0]
+        def gather_g(m):
+            for part in (FIRST, LATER):
+                nc.vector.tensor_tensor(decayed[m][:, columns_of(part)], listed(g_tile[m][:], part), decay_wide[m][:], ALU.mult)
+
+        def first_product(bank, b, pieces):
             steps = [(a,) + piece for a in range(2) for piece in pieces]
-            for s, (a, b, t, j0, width, c0) in enumerate(steps):
-                col = a * H + b * 512 + t * P
+            for s, (a, t, part, bank_col) in enumerate(steps):
+                w4_col = a * H + b * PASS + t * P
                 nc.tensor.matmul_mx(
-                    out=bank[:, c0 : c0 + width],
-                    lhsT=w4_bytes[:, 2 * col : 2 * (col + P)].bitcast(FP4X4),
-                    lhsT_scale=w4_s[:, col : col + P],
-                    rhs=v_w[a, i][:, j0 : j0 + width].bitcast(FP8X4),
-                    rhs_scale=v_s[a][:, start + j0 : start + j0 + width],
+                    out=bank[:, bank_col : bank_col + part[1]],
+                    lhsT=w4_bytes[:, 2 * w4_col : 2 * (w4_col + P)].bitcast(FP4X4),
+                    lhsT_scale=w4_s[:, w4_col : w4_col + P],
+                    rhs=v_w[a][:, columns_of(part)].bitcast(FP8X4),
+                    rhs_scale=v_s[a][:, columns_of(part)],
                     start=(s == 0),
                     stop=(s == len(steps) - 1),
                 )
 
-        dg = [held([P, S], F32, "dg%d" % m) for m in range(4)]
+        h_w = [held([P, S], U32, "h_w%d" % b) for b in range(2)]
+        h_s = [held([P, S], U8, "h_s%d" % b) for b in range(2)]
 
-        def gather_g(m):
-            for half in range(2):
-                nc.vector.tensor_tensor(dg[m][:, HALF * half : HALF * (half + 1)], listed(g_tile[m][:], HALF * half, HALF), decay_wide[m][:], ALU.mult)
+        def quantize_h(b, part, grouped):
+            nc.vector.quantize_mx(out=h_w[b][:, columns_of(part)].bitcast(FP8X4), scales=h_s[b][:, columns_of(part)], in_=grouped[:])
 
-        h_il = {}
-        h_w = {}
-        h_s = {}
-
-        def quantize_h(i, b):
-            width = SLICES[i][1]
-            h_w[i, b] = held([P, width], U32, "h_w%d_%d" % (i, b))
-            h_s[i, b] = held([P, width], U8, "h_s%d_%d" % (i, b))
-            nc.vector.quantize_mx(out=h_w[i, b][:].bitcast(FP8X4), scales=h_s[i, b][:], in_=h_il[i, b][:])
-
-        def units_on_vector(i, b):
-            width = SLICES[i][1]
-            h_il[i, b] = held([P, width * 4], BF16, "h_il%d_%d" % (i, b))
-            th = held([P, width * 4], F32, "th%d_%d" % (i, b))
-            for jj in range(width // P):
-                bank = psum_bank((4 * i + 2 * b + jj) % 8)
-                first_product(bank, i, [(b, t, jj * P, P, t * P) for t in range(4)])
+        def make_h_with_vector(b, part, banks):
+            first, count = part
+            rate = held([P, count * 4], F32, "rate")
+            grouped = held([P, count * 4], BF16, "grouped_by_vector")
+            for u, number in enumerate(banks):
+                bank = psum_bank(number)
+                first_product(bank, b, [(t, (first + u * P, P), t * P) for t in range(4)])
                 nc.scalar.activation(
-                    th[:, jj * BANK : (jj + 1) * BANK].rearrange("p (j t) -> p j t", t=4),
+                    rate[:, u * BANK : (u + 1) * BANK].rearrange("p (j t) -> p j t", t=4),
                     bank[:].rearrange("p (t j) -> p j t", t=4),
                     ACT.Tanh,
                 )
             nc.vector.tensor_tensor(
-                h_il[i, b][:].rearrange("p (j t) -> p j t", t=4),
-                th[:].rearrange("p (j t) -> p j t", t=4),
-                peak_col[b].unsqueeze(1).to_broadcast([P, width, 4]),
+                grouped[:].rearrange("p (j t) -> p j t", t=4),
+                rate[:].rearrange("p (j t) -> p j t", t=4),
+                peak_col[b].unsqueeze(1).to_broadcast([P, count, 4]),
                 ALU.mult,
             )
+            quantize_h(b, part, grouped)
 
-        def units_on_scalar(i, b):
-            width = SLICES[i][1]
-            h_il[i, b] = held([P, width * 4], BF16, "h_il%d_%d" % (i, b))
-            hb = keep.tile([P, 4 * width], BF16, name="hb", tag="unit%d_%d" % (i, b))
-            for u in range(2):
-                bank = psum_bank((4 * i + 2 * b + u) % 8)
-                first_product(bank, i, [(b, 2 * u + e, j0, P, e * width + j0) for e in range(2) for j0 in range(0, width, P)])
-                th = ring.tile([P, BANK], F32, name="th")
-                nc.scalar.activation(th[:], bank[:], ACT.Tanh)
-                for e in range(2):
-                    t = 2 * u + e
-                    nc.scalar.activation(hb[:, t * width : (t + 1) * width], th[:, e * width : (e + 1) * width], ACT.Copy, scale=peak_col[b][:, t : t + 1])
-            nc.scalar.copy(
-                h_il[i, b][:].rearrange("p (c i t) -> p c t i", i=4, t=4),
-                hb[:].rearrange("p (t c i) -> p c t i", i=4, t=4),
-            )
-
-        w2_w = {}
-        w2_s = {}
-
-        def prepare_w2(b, half):
-            cols = N // 2
-            il = held([P, cols * 4], BF16, "w2_il%d_%d" % (b, half))
-            nc.scalar.copy(
-                il[:].rearrange("p (c i t) -> p c t i", i=4, t=4),
-                w2_raw[b][:, :, cols * half : cols * (half + 1)].rearrange("p t (c i) -> p c t i", i=4),
-            )
-            w2_w[b, half] = held([P, cols], U32, "w2_w%d_%d" % (b, half))
-            w2_s[b, half] = held([P, cols], U8, "w2_s%d_%d" % (b, half))
-            nc.vector.quantize_mx(out=w2_w[b, half][:].bitcast(FP8X4), scales=w2_s[b, half][:], in_=il[:])
-
-        def second_product(bank_number, jobs):
-            acc = psum_bank(bank_number)
-            for u, (i, m) in enumerate(jobs):
-                width = SLICES[i][1]
-                c0 = (m % 2) * P
-                for b in range(2):
-                    nc.tensor.matmul_mx(
-                        out=acc[:, u * width : (u + 1) * width],
-                        lhsT=w2_w[b, m // 2][:, c0 : c0 + P].bitcast(FP8X4),
-                        lhsT_scale=w2_s[b, m // 2][:, c0 : c0 + P],
-                        rhs=h_w[i, b][:].bitcast(FP8X4),
-                        rhs_scale=h_s[i, b][:],
-                        start=(b == 0),
-                        stop=(b == 1),
+        def make_h_with_scalar(b, part, banks):
+            first, count = part
+            room = "rounded%d_%d" % (b, first)
+            rounded = held([P, 4 * count], BF16, room)
+            grouped = held([P, count * 4], BF16, "grouped%d_%d" % (b, first))
+            t_per_bank = BANK // count
+            width = BANK if count == BANK else P
+            for u, number in enumerate(banks):
+                bank = psum_bank(number)
+                t0 = u * t_per_bank
+                first_product(bank, b, [(t0 + d, (first + j, width), d * count + j) for d in range(t_per_bank) for j in range(0, count, width)])
+                saturated = ring.tile([P, BANK], F32, name="saturated")
+                nc.scalar.activation(saturated[:], bank[:], ACT.Tanh)
+                for d in range(t_per_bank):
+                    t = t0 + d
+                    nc.scalar.activation(
+                        rounded[:, t * count : (t + 1) * count], saturated[:, d * count : (d + 1) * count], ACT.Copy, scale=peak_col[b][:, t : t + 1]
                     )
-            return acc
+            nc.scalar.copy(
+                grouped[:].rearrange("p (c i t) -> p c t i", i=4, t=4),
+                rounded[:].rearrange("p (t c i) -> p c t i", i=4, t=4),
+            )
+            quantize_h(b, part, grouped)
+            return room
 
-        def replace_columns(bank_number, jobs, room):
-            acc = second_product(bank_number, jobs)
-            yd = keep.tile([P, BANK], F32, name="yd", tag=room)
-            for u, (i, m) in enumerate(jobs):
-                start, width = SLICES[i]
-                cols = slice(u * width, (u + 1) * width)
-                nc.scalar.activation(yd[:, cols], acc[:, cols], ACT.Identity, bias=drive_col[:, m : m + 1])
-                nc.vector.tensor_tensor(listed(g_tile[m][:], start, width), dg[m][:, start : start + width], yd[:, cols], ALU.add)
-                if i == 3:
-                    nc.sync.dma_start(out[P * m : P * (m + 1), :], g_tile[m][:])
+        w2_w = [held([P, N], U32, "w2_w%d" % b) for b in range(2)]
+        w2_s = [held([P, N], U8, "w2_s%d" % b) for b in range(2)]
 
-        def units(i, b):
-            if 2 * i + b < 3:
-                units_on_vector(i, b)
-            else:
-                units_on_scalar(i, b)
-            quantize_h(i, b)
+        def quantize_w2(b):
+            grouped = held([P, N * 4], BF16, "w2_grouped%d" % b)
+            nc.scalar.copy(
+                grouped[:].rearrange("p (c i t) -> p c t i", i=4, t=4),
+                w2_raw[:, b, :, :].rearrange("p t (c i) -> p c t i", i=4),
+            )
+            nc.vector.quantize_mx(out=w2_w[b][:].bitcast(FP8X4), scales=w2_s[b][:], in_=grouped[:])
+
+        def replace_columns(room, *groups):
+            driven = held([P, BANK * len(groups)], F32, "driven", room)
+            for place, (number, jobs) in enumerate(groups):
+                bank = psum_bank(number)
+                for u, (part, m) in enumerate(jobs):
+                    for b in range(2):
+                        nc.tensor.matmul_mx(
+                            out=bank[:, u * part[1] : (u + 1) * part[1]],
+                            lhsT=w2_w[b][:, m * P : (m + 1) * P].bitcast(FP8X4),
+                            lhsT_scale=w2_s[b][:, m * P : (m + 1) * P],
+                            rhs=h_w[b][:, columns_of(part)].bitcast(FP8X4),
+                            rhs_scale=h_s[b][:, columns_of(part)],
+                            start=(b == 0),
+                            stop=(b == 1),
+                        )
+                for u, (part, m) in enumerate(jobs):
+                    values = driven[:, place * BANK + u * part[1] : place * BANK + (u + 1) * part[1]]
+                    nc.scalar.activation(values, bank[:, u * part[1] : (u + 1) * part[1]], ACT.Identity, bias=drive_col[:, m : m + 1])
+                    nc.vector.tensor_tensor(listed(g_tile[m][:], part), decayed[m][:, columns_of(part)], values, ALU.add)
+                    if part[0] + part[1] == S:
+                        nc.sync.dma_start(out[P * m : P * (m + 1), :], g_tile[m][:])
 
         gather_g(0)
-        units(0, 0)
-        units(0, 1)
-        prepare_w2(0, 0)
-        prepare_w2(0, 1)
-        gather_g(1)
-        units(1, 0)
-        prepare_w2(1, 0)
-        prepare_w2(1, 1)
-        gather_g(2)
-        gather_g(3)
-        units(1, 1)
-        units(2, 0)
-        replace_columns(0, [(0, 0), (0, 1)], "unit2_0")
-        replace_columns(1, [(0, 2), (0, 3)], "ya")
-        units(2, 1)
-        replace_columns(2, [(1, 0), (1, 1)], "unit2_1")
-        replace_columns(3, [(1, 2), (1, 3)], "yb")
-        units(3, 0)
-        replace_columns(5, [(2, 0), (2, 1)], "unit3_0")
-        units(3, 1)
-        replace_columns(7, [(2, 2)], "unit3_1")
-        replace_columns(0, [(3, 0), (3, 1)], "yc")
-        replace_columns(1, [(3, 2), (2, 3)], "yd")
-        replace_columns(2, [(3, 3)], "ye")
+        make_h_with_vector(0, FIRST, banks=(0, 1, 2, 3))
+        quantize_w2(0)
+        quantize_w2(1)
+        for m in range(1, 4):
+            gather_g(m)
+        room = make_h_with_scalar(1, FIRST, banks=(4, 5, 6, 7))
+        replace_columns(room, (6, [(FIRST, 0)]), (7, [(FIRST, 1)]))
+        room = make_h_with_scalar(0, SECOND, banks=(0, 1))
+        replace_columns(room, (0, [(FIRST, 2)]))
+        room = make_h_with_scalar(1, SECOND, banks=(2, 3))
+        replace_columns(room, (2, [(FIRST, 3)]))
+        room = make_h_with_scalar(0, THIRD, banks=(4, 5))
+        replace_columns(room, (4, [(SECOND, 0), (SECOND, 1)]))
+        room = make_h_with_scalar(1, THIRD, banks=(6, 7))
+        replace_columns(room, (6, [(SECOND, 2)]), (0, [(THIRD, 0), (THIRD, 1)]), (1, [(THIRD, 2)]), (2, [(LATER, 3)]))

@@ -21,8 +21,11 @@ P = 128
 PASS = 512
 BANK = 512
 GROUP = 16
-FIRST, SECOND, THIRD = (0, 512), (512, 256), (768, 256)
-LATER = (512, 512)
+QUARTER = S // 4
+
+
+def quarters(first, count=1):
+    return (first * QUARTER, count * QUARTER)
 
 
 def tile_list_place_cell_replay_kernel(tc, tab_words, tab_scales, offs, w4_words, w4_scales, peak, w2, drive, decay, gT, out):
@@ -124,13 +127,13 @@ def tile_list_place_cell_replay_kernel(tc, tab_words, tab_scales, offs, w4_words
         load_g(1, "w4_raw")
         load_g(2, "w4_s_raw")
         load_g(3, "rows")
-        for part in (FIRST, LATER):
+        for part in (quarters(0), quarters(1, 3)):
             nc.vector.tensor_copy(v_w[1][:, columns_of(part)], listed(tab_w[1][:].bitcast(U32), part))
 
         decayed = [held([P, S], F32, "decayed%d" % m) for m in range(4)]
 
         def gather_g(m):
-            for part in (FIRST, LATER):
+            for part in (quarters(0, 2), quarters(2, 2)):
                 nc.vector.tensor_tensor(decayed[m][:, columns_of(part)], listed(g_tile[m][:], part), decay_wide[m][:], ALU.mult)
 
         def first_product(bank, b, pieces):
@@ -155,8 +158,8 @@ def tile_list_place_cell_replay_kernel(tc, tab_words, tab_scales, offs, w4_words
 
         def make_h_with_vector(b, part, banks):
             first, count = part
-            rate = held([P, count * 4], F32, "rate")
-            grouped = held([P, count * 4], BF16, "grouped_by_vector")
+            rate = held([P, count * 4], F32, "rate%d_%d" % (b, first))
+            grouped = held([P, count * 4], BF16, "grouped%d_%d" % (b, first))
             for u, number in enumerate(banks):
                 bank = psum_bank(number)
                 first_product(bank, b, [(t, (first + u * P, P), t * P) for t in range(4)])
@@ -178,16 +181,13 @@ def tile_list_place_cell_replay_kernel(tc, tab_words, tab_scales, offs, w4_words
             room = "rounded%d_%d" % (b, first)
             rounded = held([P, 4 * count], BF16, room)
             grouped = held([P, count * 4], BF16, "grouped%d_%d" % (b, first))
-            t_per_bank = BANK // count
-            width = BANK if count == BANK else P
             for u, number in enumerate(banks):
                 bank = psum_bank(number)
-                t0 = u * t_per_bank
-                first_product(bank, b, [(t0 + d, (first + j, width), d * count + j) for d in range(t_per_bank) for j in range(0, count, width)])
+                first_product(bank, b, [(2 * u + d, (first + j, P), d * count + j) for d in range(2) for j in range(0, count, P)])
                 saturated = ring.tile([P, BANK], F32, name="saturated")
                 nc.scalar.activation(saturated[:], bank[:], ACT.Tanh)
-                for d in range(t_per_bank):
-                    t = t0 + d
+                for d in range(2):
+                    t = 2 * u + d
                     nc.scalar.activation(
                         rounded[:, t * count : (t + 1) * count], saturated[:, d * count : (d + 1) * count], ACT.Copy, scale=peak_col[b][:, t : t + 1]
                     )
@@ -232,18 +232,26 @@ def tile_list_place_cell_replay_kernel(tc, tab_words, tab_scales, offs, w4_words
                         nc.sync.dma_start(out[P * m : P * (m + 1), :], g_tile[m][:])
 
         gather_g(0)
-        make_h_with_vector(0, FIRST, banks=(0, 1, 2, 3))
+        make_h_with_vector(0, quarters(0), banks=(0, 1))
+        make_h_with_vector(1, quarters(0), banks=(2, 3))
+        make_h_with_vector(0, quarters(1), banks=(4, 5))
         quantize_w2(0)
         quantize_w2(1)
         for m in range(1, 4):
             gather_g(m)
-        room = make_h_with_scalar(1, FIRST, banks=(4, 5, 6, 7))
-        replace_columns(room, (6, [(FIRST, 0)]), (7, [(FIRST, 1)]))
-        room = make_h_with_scalar(0, SECOND, banks=(0, 1))
-        replace_columns(room, (0, [(FIRST, 2)]))
-        room = make_h_with_scalar(1, SECOND, banks=(2, 3))
-        replace_columns(room, (2, [(FIRST, 3)]))
-        room = make_h_with_scalar(0, THIRD, banks=(4, 5))
-        replace_columns(room, (4, [(SECOND, 0), (SECOND, 1)]))
-        room = make_h_with_scalar(1, THIRD, banks=(6, 7))
-        replace_columns(room, (6, [(SECOND, 2)]), (0, [(THIRD, 0), (THIRD, 1)]), (1, [(THIRD, 2)]), (2, [(LATER, 3)]))
+        room = make_h_with_scalar(1, quarters(1), banks=(6, 7))
+        replace_columns(room, (6, [(quarters(0), 0), (quarters(0), 1)]))
+        room = make_h_with_scalar(0, quarters(2), banks=(0, 1))
+        replace_columns(room, (0, [(quarters(0, 2), 2)]))
+        room = make_h_with_scalar(1, quarters(2), banks=(2, 3))
+        replace_columns(room, (2, [(quarters(0, 2), 3)]))
+        room = make_h_with_scalar(0, quarters(3), banks=(4, 5))
+        replace_columns(room, (4, [(quarters(1, 2), 0)]), (5, [(quarters(1, 2), 1)]))
+        room = make_h_with_scalar(1, quarters(3), banks=(6, 7))
+        replace_columns(
+            room,
+            (6, [(quarters(2), 2)]),
+            (0, [(quarters(3), 0), (quarters(3), 1)]),
+            (1, [(quarters(3), 2)]),
+            (2, [(quarters(2, 2), 3)]),
+        )

@@ -51,43 +51,43 @@ def tile_list_place_cell_replay_kernel(tc, tab_words, tab_scales, offs, w4_words
         def columns_of(part):
             return slice(part[0], part[0] + part[1])
 
+        warm = held([P, 2], F32, "warm")
+        nc.gpsimd.memset(warm[:, 0:1], 0.0)
+        nc.scalar.activation(warm[:, 1:2], warm[:, 0:1], ACT.Tanh)
+
         tab_s = held([P, T], U8, "tab_s")
         nc.gpsimd.memset(tab_s[:].bitcast(I32), 0)
         w4_s_raw = held([P, 2 * H], U8, "w4_s_raw")
         nc.vector.memset(w4_s_raw[:].bitcast(I32), 0)
         v_s1 = held([P, S], U8, "v_s1")
         nc.vector.memset(v_s1[:].bitcast(I32), 0)
-        tab_w = [held([P, T], I32, "tab_w%d" % a) for a in range(2)]
+        tab_w = [held([P, T], I32, "tab_w0"), held([P, T], I32, "tab_w1", room="warm")]
         w4_raw = held([P, H], I32, "w4_raw")
         nc.sync.dma_start(tab_w[0][:], tab_words[0].rearrange("p t i -> p (t i)").bitcast(I32))
+        nc.sync.dma_start(w4_raw[:].rearrange("p (a c) -> p a c", a=2), w4_words.bitcast(I32).rearrange("a p c -> p a c"))
         for q in range(4):
             nc.sync.dma_start(tab_s[32 * q : 32 * q + 8, :].bitcast(I32), tab_scales[:, 4 * q : 4 * q + 4, :].bitcast(I32))
-        nc.sync.dma_start(w4_raw[:].rearrange("p (a c) -> p a c", a=2), w4_words.bitcast(I32).rearrange("a p c -> p a c"))
-        nc.sync.dma_start(tab_w[1][:], tab_words[1].rearrange("p t i -> p (t i)").bitcast(I32))
         for q in range(4):
             nc.sync.dma_start(
                 w4_s_raw[32 * q : 32 * q + 4, :].bitcast(I32).rearrange("p (a c) -> p a c", a=2),
                 w4_scales[:, 4 * q : 4 * q + 4, :].bitcast(I32).rearrange("a r c -> r a c"),
             )
+        nc.sync.dma_start(tab_w[1][:], tab_words[1].rearrange("p t i -> p (t i)").bitcast(I32))
 
-        rows = held([P, P], F32, "rows")
+        rows = held([P, 3 * P], F32, "rows")
         nc.gpsimd.memset(rows[:], 0.0)
-        nc.gpsimd.dma_start(rows[8:12, :], decay.rearrange("(m p) -> m p", p=P))
-        for b in range(2):
-            nc.gpsimd.dma_start(
-                rows[4 * b : 4 * b + 4, :].rearrange("t (g e) -> t g e", e=8),
-                peak[PASS * b : PASS * (b + 1)].rearrange("(g t e) -> t g e", t=4, e=8),
-            )
-        nc.gpsimd.dma_start(rows[12:16, :], drive.rearrange("(m p) -> m p", p=P))
+        nc.gpsimd.dma_start(rows[4:8, 0:P], decay.rearrange("(m p) -> m p", p=P))
+        nc.gpsimd.dma_start(rows[0:4, 0 : 2 * P].rearrange("t (bg e) -> t bg e", e=8), peak.rearrange("(bg t e) -> t bg e", t=4, e=8))
+        nc.gpsimd.dma_start(rows[0:4, 2 * P : 3 * P], drive.rearrange("(m p) -> m p", p=P))
         identity = held([P, P], F32, "identity")
         make_identity(nc, identity[:])
         turned = psum_bank(7)
-        nc.tensor.transpose(turned[:, 0:P], rows[:], identity[:])
-        per_partition = held([P, 16], F32, "per_partition")
-        nc.scalar.copy(per_partition[:], turned[:, 0:16])
-        peak_col = [per_partition[:, 0:4], per_partition[:, 4:8]]
-        decay_col = per_partition[:, 8:12]
-        drive_col = per_partition[:, 12:16]
+        for block in range(2):
+            nc.tensor.transpose(turned[:, block * P : (block + 1) * P], rows[:, block * P : (block + 1) * P], identity[:])
+        per_partition = held([P, 2, 8], F32, "per_partition")
+        nc.scalar.copy(per_partition[:], turned[:, 0 : 2 * P].rearrange("p (block c) -> p block c", block=2)[:, :, 0:8])
+        peak_col = [per_partition[:, 0, 0:4], per_partition[:, 1, 0:4]]
+        decay_col = per_partition[:, 0, 4:8]
 
         g_tile = {}
 
@@ -97,15 +97,18 @@ def tile_list_place_cell_replay_kernel(tc, tab_words, tab_scales, offs, w4_words
 
         v_w = [held([P, S], U32, "v_w%d" % a) for a in range(2)]
         nc.vector.tensor_copy(v_w[0][:], listed(tab_w[0][:].bitcast(U32), (0, S)))
-        v_s0 = held([P, S], U8, "v_s0", room="tab_w0")
-        nc.vector.tensor_copy(v_s0[:], listed(tab_s[:], (0, S)))
-        nc.scalar.dma_start(v_s1[0:112, :].bitcast(I32), v_s0[4:116, :].bitcast(I32))
+        v_s0 = held([P, S], U8, "v_s0")
+        for part, queue in ((quarters(0), nc.scalar), (quarters(1, 3), nc.sync)):
+            nc.vector.tensor_copy(v_s0[:, columns_of(part)], listed(tab_s[:], part))
+            queue.dma_start(v_s1[0:112, columns_of(part)].bitcast(I32), v_s0[4:116, columns_of(part)].bitcast(I32))
         v_s = [v_s0, v_s1]
-        load_g(0, None)
+        load_g(0, "tab_w0")
 
-        decay_wide = [held([P, BANK], F32, "decay_wide%d" % m) for m in range(4)]
-        for m in range(4):
-            nc.gpsimd.tensor_scalar(decay_wide[m][:], decay_col[:, m : m + 1].to_broadcast([P, BANK]), 1.0, 0.0, ALU.mult, ALU.add)
+        decay_wide = [held([P, S], F32, "decay_wide%d" % m) for m in range(4)]
+        for m in range(2):
+            nc.scalar.copy(decay_wide[m][:], decay_col[:, m : m + 1].to_broadcast([P, S]))
+        for m in range(2, 4):
+            nc.gpsimd.tensor_scalar(decay_wide[m][:], decay_col[:, m : m + 1].to_broadcast([P, S]), 1.0, 0.0, ALU.mult, ALU.add)
 
         w2_raw = held([P, 2, 4, N], F32, "w2_raw", room="tab_s")
         w2_rows = w2.rearrange("(b g t e) n -> b t g e n", b=2, t=4, e=8)
@@ -124,17 +127,15 @@ def tile_list_place_cell_replay_kernel(tc, tab_words, tab_scales, offs, w4_words
             w4_s_raw[:].bitcast(I32).rearrange("p (ab g t w) -> p ab t g w", t=4, g=16, w=2),
         )
         w4_bytes = w4_w[:].bitcast(U8)
-        load_g(1, "w4_raw")
-        load_g(2, "w4_s_raw")
-        load_g(3, "rows")
         for part in (quarters(0), quarters(1, 3)):
             nc.vector.tensor_copy(v_w[1][:, columns_of(part)], listed(tab_w[1][:].bitcast(U32), part))
+        load_g(1, "warm")
 
-        decayed = [held([P, S], F32, "decayed%d" % m) for m in range(4)]
+        decayed = {}
 
-        def gather_g(m):
-            for part in (quarters(0, 2), quarters(2, 2)):
-                nc.vector.tensor_tensor(decayed[m][:, columns_of(part)], listed(g_tile[m][:], part), decay_wide[m][:], ALU.mult)
+        def gather_g(m, room=None):
+            decayed[m] = held([P, S], F32, "decayed%d" % m, room)
+            nc.vector.tensor_tensor(decayed[m][:], listed(g_tile[m][:], (0, S)), decay_wide[m][:], ALU.mult)
 
         def first_product(bank, b, pieces):
             steps = [(a,) + piece for a in range(2) for piece in pieces]
@@ -150,37 +151,36 @@ def tile_list_place_cell_replay_kernel(tc, tab_words, tab_scales, offs, w4_words
                     stop=(s == len(steps) - 1),
                 )
 
-        h_w = [held([P, S], U32, "h_w%d" % b) for b in range(2)]
-        h_s = [held([P, S], U8, "h_s%d" % b) for b in range(2)]
+        h_w = [held([P, 2 * QUARTER], U32, "h_w%d" % q) for q in range(4)]
+        h_s = [held([P, 2 * QUARTER], U8, "h_s%d" % q) for q in range(4)]
+        grouped = [held([P, 2, QUARTER * 4], BF16, "grouped%d" % q) for q in range(4)]
 
-        def quantize_h(b, part, grouped):
-            nc.vector.quantize_mx(out=h_w[b][:, columns_of(part)].bitcast(FP8X4), scales=h_s[b][:, columns_of(part)], in_=grouped[:])
+        def quantize_h(q):
+            nc.vector.quantize_mx(out=h_w[q][:].bitcast(FP8X4), scales=h_s[q][:], in_=grouped[q][:].rearrange("p b c -> p (b c)"))
 
-        def make_h_with_vector(b, part, banks):
-            first, count = part
-            rate = held([P, count * 4], F32, "rate%d_%d" % (b, first))
-            grouped = held([P, count * 4], BF16, "grouped%d_%d" % (b, first))
-            for u, number in enumerate(banks):
-                bank = psum_bank(number)
-                first_product(bank, b, [(t, (first + u * P, P), t * P) for t in range(4)])
-                nc.scalar.activation(
-                    rate[:, u * BANK : (u + 1) * BANK].rearrange("p (j t) -> p j t", t=4),
-                    bank[:].rearrange("p (t j) -> p j t", t=4),
-                    ACT.Tanh,
-                )
+        def make_h_with_vector(q, banks):
+            rate = held([P, 2, QUARTER * 4], F32, "rate%d" % q)
+            for b in range(2):
+                for u in range(2):
+                    bank = psum_bank(banks[2 * b + u])
+                    first_product(bank, b, [(t, (q * QUARTER + u * P, P), t * P) for t in range(4)])
+                    nc.scalar.activation(
+                        rate[:, b, u * BANK : (u + 1) * BANK].rearrange("p (j t) -> p j t", t=4),
+                        bank[:].rearrange("p (t j) -> p j t", t=4),
+                        ACT.Tanh,
+                    )
             nc.vector.tensor_tensor(
-                grouped[:].rearrange("p (j t) -> p j t", t=4),
-                rate[:].rearrange("p (j t) -> p j t", t=4),
-                peak_col[b].unsqueeze(1).to_broadcast([P, count, 4]),
+                grouped[q][:].rearrange("p b (j t) -> p b j t", t=4),
+                rate[:].rearrange("p b (j t) -> p b j t", t=4),
+                per_partition[:, :, 0:4].unsqueeze(2).to_broadcast([P, 2, QUARTER, 4]),
                 ALU.mult,
             )
-            quantize_h(b, part, grouped)
+            quantize_h(q)
 
-        def make_h_with_scalar(b, part, banks):
-            first, count = part
-            room = "rounded%d_%d" % (b, first)
-            rounded = held([P, 4 * count], BF16, room)
-            grouped = held([P, count * 4], BF16, "grouped%d_%d" % (b, first))
+        def make_h_with_scalar(q, b, banks, room=None):
+            first, count = quarters(q)
+            room = room or "rounded%d_%d" % (q, b)
+            rounded = held([P, 4 * count], BF16, "rounded%d_%d" % (q, b), room)
             for u, number in enumerate(banks):
                 bank = psum_bank(number)
                 first_product(bank, b, [(2 * u + d, (first + j, P), d * count + j) for d in range(2) for j in range(0, count, P)])
@@ -192,66 +192,73 @@ def tile_list_place_cell_replay_kernel(tc, tab_words, tab_scales, offs, w4_words
                         rounded[:, t * count : (t + 1) * count], saturated[:, d * count : (d + 1) * count], ACT.Copy, scale=peak_col[b][:, t : t + 1]
                     )
             nc.scalar.copy(
-                grouped[:].rearrange("p (c i t) -> p c t i", i=4, t=4),
+                grouped[q][:, b, :].rearrange("p (c i t) -> p c t i", i=4, t=4),
                 rounded[:].rearrange("p (t c i) -> p c t i", i=4, t=4),
             )
-            quantize_h(b, part, grouped)
+            if b == 1:
+                quantize_h(q)
             return room
 
-        w2_w = [held([P, N], U32, "w2_w%d" % b) for b in range(2)]
-        w2_s = [held([P, N], U8, "w2_s%d" % b) for b in range(2)]
+        w2_w = held([P, 2 * N], U32, "w2_w")
+        w2_s = held([P, 2 * N], U8, "w2_s")
 
-        def quantize_w2(b):
-            grouped = held([P, N * 4], BF16, "w2_grouped%d" % b)
-            nc.scalar.copy(
-                grouped[:].rearrange("p (c i t) -> p c t i", i=4, t=4),
-                w2_raw[:, b, :, :].rearrange("p t (c i) -> p c t i", i=4),
-            )
-            nc.vector.quantize_mx(out=w2_w[b][:].bitcast(FP8X4), scales=w2_s[b][:], in_=grouped[:])
+        def quantize_w2():
+            w2_grouped = held([P, 2, N * 4], BF16, "w2_grouped")
+            for b in range(2):
+                nc.scalar.copy(
+                    w2_grouped[:, b, :].rearrange("p (c i t) -> p c t i", i=4, t=4),
+                    w2_raw[:, b, :, :].rearrange("p t (c i) -> p c t i", i=4),
+                )
+            nc.vector.quantize_mx(out=w2_w[:].bitcast(FP8X4), scales=w2_s[:], in_=w2_grouped[:].rearrange("p b c -> p (b c)"))
 
         def replace_columns(room, *groups):
             driven = held([P, BANK * len(groups)], F32, "driven", room)
             for place, (number, jobs) in enumerate(groups):
                 bank = psum_bank(number)
-                for u, (part, m) in enumerate(jobs):
-                    for b in range(2):
-                        nc.tensor.matmul_mx(
-                            out=bank[:, u * part[1] : (u + 1) * part[1]],
-                            lhsT=w2_w[b][:, m * P : (m + 1) * P].bitcast(FP8X4),
-                            lhsT_scale=w2_s[b][:, m * P : (m + 1) * P],
-                            rhs=h_w[b][:, columns_of(part)].bitcast(FP8X4),
-                            rhs_scale=h_s[b][:, columns_of(part)],
-                            start=(b == 0),
-                            stop=(b == 1),
-                        )
-                for u, (part, m) in enumerate(jobs):
-                    values = driven[:, place * BANK + u * part[1] : place * BANK + (u + 1) * part[1]]
-                    nc.scalar.activation(values, bank[:, u * part[1] : (u + 1) * part[1]], ACT.Identity, bias=drive_col[:, m : m + 1])
+                spans = []
+                column = 0
+                for first_q, count_q, m in jobs:
+                    spans.append(slice(column, column + count_q * QUARTER))
+                    for q in range(first_q, first_q + count_q):
+                        for b in range(2):
+                            nc.tensor.matmul_mx(
+                                out=bank[:, column : column + QUARTER],
+                                lhsT=w2_w[:, b * N + m * P : b * N + (m + 1) * P].bitcast(FP8X4),
+                                lhsT_scale=w2_s[:, b * N + m * P : b * N + (m + 1) * P],
+                                rhs=h_w[q][:, b * QUARTER : (b + 1) * QUARTER].bitcast(FP8X4),
+                                rhs_scale=h_s[q][:, b * QUARTER : (b + 1) * QUARTER],
+                                start=(b == 0),
+                                stop=(b == 1),
+                            )
+                        column += QUARTER
+                for span, (first_q, count_q, m) in zip(spans, jobs):
+                    part = quarters(first_q, count_q)
+                    values = driven[:, place * BANK + span.start : place * BANK + span.stop]
+                    nc.scalar.activation(values, bank[:, span], ACT.Identity, bias=drive_col[:, m : m + 1])
                     nc.vector.tensor_tensor(listed(g_tile[m][:], part), decayed[m][:, columns_of(part)], values, ALU.add)
-                    if part[0] + part[1] == S:
+                    if first_q + count_q == 4:
                         nc.sync.dma_start(out[P * m : P * (m + 1), :], g_tile[m][:])
 
         gather_g(0)
-        make_h_with_vector(0, quarters(0), banks=(0, 1))
-        make_h_with_vector(1, quarters(0), banks=(2, 3))
-        make_h_with_vector(0, quarters(1), banks=(4, 5))
-        quantize_w2(0)
-        quantize_w2(1)
-        for m in range(1, 4):
-            gather_g(m)
-        room = make_h_with_scalar(1, quarters(1), banks=(6, 7))
-        replace_columns(room, (6, [(quarters(0), 0), (quarters(0), 1)]))
-        room = make_h_with_scalar(0, quarters(2), banks=(0, 1))
-        replace_columns(room, (0, [(quarters(0, 2), 2)]))
-        room = make_h_with_scalar(1, quarters(2), banks=(2, 3))
-        replace_columns(room, (2, [(quarters(0, 2), 3)]))
-        room = make_h_with_scalar(0, quarters(3), banks=(4, 5))
-        replace_columns(room, (4, [(quarters(1, 2), 0)]), (5, [(quarters(1, 2), 1)]))
-        room = make_h_with_scalar(1, quarters(3), banks=(6, 7))
-        replace_columns(
-            room,
-            (6, [(quarters(2), 2)]),
-            (0, [(quarters(3), 0), (quarters(3), 1)]),
-            (1, [(quarters(3), 2)]),
-            (2, [(quarters(2, 2), 3)]),
-        )
+        load_g(2, "decay_wide0")
+        make_h_with_vector(0, banks=(0, 1, 2, 3))
+        load_g(3, "rate0")
+        turned = psum_bank(3)
+        nc.tensor.transpose(turned[:, 0:P], rows[:, 2 * P : 3 * P], identity[:])
+        drive_col = held([P, 4], F32, "drive_col")
+        nc.scalar.copy(drive_col[:], turned[:, 0:4])
+        quantize_w2()
+        gather_g(1)
+        gather_g(2)
+        room = make_h_with_scalar(1, 0, banks=(4, 5), room="tab_s")
+        replace_columns(room, (4, [(0, 1, 0)]))
+        make_h_with_scalar(1, 1, banks=(6, 7))
+        gather_g(3, room="grouped1")
+        room = make_h_with_scalar(2, 0, banks=(0, 1))
+        replace_columns(room, (0, [(0, 2, 1)]), (1, [(0, 2, 3)]))
+        room = make_h_with_scalar(2, 1, banks=(2, 3))
+        replace_columns(room, (2, [(0, 2, 2)]))
+        room = make_h_with_scalar(3, 0, banks=(4, 5))
+        replace_columns(room, (4, [(1, 2, 0)]))
+        room = make_h_with_scalar(3, 1, banks=(6, 7))
+        replace_columns(room, (3, [(2, 1, 2)]), (0, [(3, 1, 0), (3, 1, 2)]), (1, [(2, 2, 1)]), (5, [(2, 2, 3)]))

@@ -56,9 +56,9 @@ def tile_list_place_cell_replay_kernel(tc, tab_words, tab_scales, offs, w4_words
         nc.scalar.activation(warm[:, 1:2], warm[:, 0:1], ACT.Tanh)
 
         tab_s = held([P, T], U8, "tab_s")
-        nc.gpsimd.memset(tab_s[:].bitcast(I32), 0)
+        nc.vector.memset(tab_s[:].bitcast(I32), 0)
         w4_s_raw = held([P, 2 * H], U8, "w4_s_raw")
-        nc.vector.memset(w4_s_raw[:].bitcast(I32), 0)
+        nc.gpsimd.memset(w4_s_raw[:].bitcast(I32), 0)
         v_s1 = held([P, S], U8, "v_s1")
         nc.vector.memset(v_s1[:].bitcast(I32), 0)
         tab_w = [held([P, T], I32, "tab_w0"), held([P, T], I32, "tab_w1", room="warm")]
@@ -66,12 +66,12 @@ def tile_list_place_cell_replay_kernel(tc, tab_words, tab_scales, offs, w4_words
         nc.sync.dma_start(tab_w[0][:], tab_words[0].rearrange("p t i -> p (t i)").bitcast(I32))
         nc.sync.dma_start(w4_raw[:].rearrange("p (a c) -> p a c", a=2), w4_words.bitcast(I32).rearrange("a p c -> p a c"))
         for q in range(4):
-            nc.sync.dma_start(tab_s[32 * q : 32 * q + 8, :].bitcast(I32), tab_scales[:, 4 * q : 4 * q + 4, :].bitcast(I32))
-        for q in range(4):
             nc.sync.dma_start(
                 w4_s_raw[32 * q : 32 * q + 4, :].bitcast(I32).rearrange("p (a c) -> p a c", a=2),
                 w4_scales[:, 4 * q : 4 * q + 4, :].bitcast(I32).rearrange("a r c -> r a c"),
             )
+        for q in range(4):
+            nc.sync.dma_start(tab_s[32 * q : 32 * q + 8, :].bitcast(I32), tab_scales[:, 4 * q : 4 * q + 4, :].bitcast(I32))
         nc.sync.dma_start(tab_w[1][:], tab_words[1].rearrange("p t i -> p (t i)").bitcast(I32))
 
         rows = held([P, 3 * P], F32, "rows")
@@ -137,8 +137,8 @@ def tile_list_place_cell_replay_kernel(tc, tab_words, tab_scales, offs, w4_words
             decayed[m] = held([P, S], F32, "decayed%d" % m, room)
             nc.vector.tensor_tensor(decayed[m][:], listed(g_tile[m][:], (0, S)), decay_wide[m][:], ALU.mult)
 
-        def first_product(bank, b, pieces):
-            steps = [(a,) + piece for a in range(2) for piece in pieces]
+        def first_product(bank, b, pieces, order=(1, 0)):
+            steps = [(a,) + piece for a in order for piece in pieces]
             for s, (a, t, part, bank_col) in enumerate(steps):
                 w4_col = a * H + b * PASS + t * P
                 nc.tensor.matmul_mx(
@@ -158,24 +158,25 @@ def tile_list_place_cell_replay_kernel(tc, tab_words, tab_scales, offs, w4_words
         def quantize_h(q):
             nc.vector.quantize_mx(out=h_w[q][:].bitcast(FP8X4), scales=h_s[q][:], in_=grouped[q][:].rearrange("p b c -> p (b c)"))
 
-        def make_h_with_vector(q, banks):
-            rate = held([P, 2, QUARTER * 4], F32, "rate%d" % q)
-            for b in range(2):
+        def make_h_with_vector(q, passes, banks):
+            rate = held([P, passes, QUARTER * 4], F32, "rate%d" % q)
+            for b in range(passes):
                 for u in range(2):
                     bank = psum_bank(banks[2 * b + u])
-                    first_product(bank, b, [(t, (q * QUARTER + u * P, P), t * P) for t in range(4)])
+                    first_product(bank, b, [(t, (q * QUARTER + u * P, P), t * P) for t in range(4)], (0, 1) if q == 0 else (1, 0))
                     nc.scalar.activation(
                         rate[:, b, u * BANK : (u + 1) * BANK].rearrange("p (j t) -> p j t", t=4),
                         bank[:].rearrange("p (t j) -> p j t", t=4),
                         ACT.Tanh,
                     )
             nc.vector.tensor_tensor(
-                grouped[q][:].rearrange("p b (j t) -> p b j t", t=4),
+                grouped[q][:, 0:passes, :].rearrange("p b (j t) -> p b j t", t=4),
                 rate[:].rearrange("p b (j t) -> p b j t", t=4),
-                per_partition[:, :, 0:4].unsqueeze(2).to_broadcast([P, 2, QUARTER, 4]),
+                per_partition[:, 0:passes, 0:4].unsqueeze(2).to_broadcast([P, passes, QUARTER, 4]),
                 ALU.mult,
             )
-            quantize_h(q)
+            if passes == 2:
+                quantize_h(q)
 
         def make_h_with_scalar(q, b, banks, room=None):
             first, count = quarters(q)
@@ -191,10 +192,7 @@ def tile_list_place_cell_replay_kernel(tc, tab_words, tab_scales, offs, w4_words
                     nc.scalar.activation(
                         rounded[:, t * count : (t + 1) * count], saturated[:, d * count : (d + 1) * count], ACT.Copy, scale=peak_col[b][:, t : t + 1]
                     )
-            nc.scalar.copy(
-                grouped[q][:, b, :].rearrange("p (c i t) -> p c t i", i=4, t=4),
-                rounded[:].rearrange("p (t c i) -> p c t i", i=4, t=4),
-            )
+            nc.scalar.copy(grouped[q][:, b, :].rearrange("p (j t) -> p j t", t=4), rounded[:].rearrange("p (t j) -> p j t", t=4))
             if b == 1:
                 quantize_h(q)
             return room
@@ -205,60 +203,56 @@ def tile_list_place_cell_replay_kernel(tc, tab_words, tab_scales, offs, w4_words
         def quantize_w2():
             w2_grouped = held([P, 2, N * 4], BF16, "w2_grouped")
             for b in range(2):
-                nc.scalar.copy(
-                    w2_grouped[:, b, :].rearrange("p (c i t) -> p c t i", i=4, t=4),
-                    w2_raw[:, b, :, :].rearrange("p t (c i) -> p c t i", i=4),
-                )
+                nc.scalar.copy(w2_grouped[:, b, :].rearrange("p (n t) -> p n t", t=4), w2_raw[:, b, :, :].rearrange("p t n -> p n t"))
             nc.vector.quantize_mx(out=w2_w[:].bitcast(FP8X4), scales=w2_s[:], in_=w2_grouped[:].rearrange("p b c -> p (b c)"))
 
-        def replace_columns(room, *groups):
-            driven = held([P, BANK * len(groups)], F32, "driven", room)
-            for place, (number, jobs) in enumerate(groups):
-                bank = psum_bank(number)
-                spans = []
-                column = 0
-                for first_q, count_q, m in jobs:
-                    spans.append(slice(column, column + count_q * QUARTER))
-                    for q in range(first_q, first_q + count_q):
+        def replace_columns(room, *jobs):
+            driven = held([P, QUARTER * sum(count for job in jobs for number, count in job[2])], F32, "driven", room)
+            filled = 0
+            for m, first_q, stretches in jobs:
+                q = first_q
+                start = filled
+                for number, count in stretches:
+                    bank = psum_bank(number)
+                    for u in range(count):
                         for b in range(2):
                             nc.tensor.matmul_mx(
-                                out=bank[:, column : column + QUARTER],
+                                out=bank[:, u * QUARTER : (u + 1) * QUARTER],
                                 lhsT=w2_w[:, b * N + m * P : b * N + (m + 1) * P].bitcast(FP8X4),
                                 lhsT_scale=w2_s[:, b * N + m * P : b * N + (m + 1) * P],
-                                rhs=h_w[q][:, b * QUARTER : (b + 1) * QUARTER].bitcast(FP8X4),
-                                rhs_scale=h_s[q][:, b * QUARTER : (b + 1) * QUARTER],
+                                rhs=h_w[q + u][:, b * QUARTER : (b + 1) * QUARTER].bitcast(FP8X4),
+                                rhs_scale=h_s[q + u][:, b * QUARTER : (b + 1) * QUARTER],
                                 start=(b == 0),
                                 stop=(b == 1),
                             )
-                        column += QUARTER
-                for span, (first_q, count_q, m) in zip(spans, jobs):
-                    part = quarters(first_q, count_q)
-                    values = driven[:, place * BANK + span.start : place * BANK + span.stop]
-                    nc.scalar.activation(values, bank[:, span], ACT.Identity, bias=drive_col[:, m : m + 1])
-                    nc.vector.tensor_tensor(listed(g_tile[m][:], part), decayed[m][:, columns_of(part)], values, ALU.add)
-                    if first_q + count_q == 4:
-                        nc.sync.dma_start(out[P * m : P * (m + 1), :], g_tile[m][:])
+                    nc.scalar.activation(
+                        driven[:, filled : filled + count * QUARTER], bank[:, 0 : count * QUARTER], ACT.Identity, bias=drive_col[:, m : m + 1]
+                    )
+                    q = q + count
+                    filled = filled + count * QUARTER
+                part = quarters(first_q, q - first_q)
+                nc.vector.tensor_tensor(listed(g_tile[m][:], part), decayed[m][:, columns_of(part)], driven[:, start:filled], ALU.add)
+                if q == 4:
+                    nc.sync.dma_start(out[P * m : P * (m + 1), :], g_tile[m][:])
 
         gather_g(0)
         load_g(2, "decay_wide0")
-        make_h_with_vector(0, banks=(0, 1, 2, 3))
+        make_h_with_vector(0, 2, banks=(0, 1, 2, 3))
         load_g(3, "rate0")
         turned = psum_bank(3)
         nc.tensor.transpose(turned[:, 0:P], rows[:, 2 * P : 3 * P], identity[:])
         drive_col = held([P, 4], F32, "drive_col")
         nc.scalar.copy(drive_col[:], turned[:, 0:4])
+        make_h_with_vector(1, 2, banks=(4, 5, 6, 7))
         quantize_w2()
         gather_g(1)
-        gather_g(2)
-        room = make_h_with_scalar(1, 0, banks=(4, 5), room="tab_s")
-        replace_columns(room, (4, [(0, 1, 0)]))
-        make_h_with_scalar(1, 1, banks=(6, 7))
-        gather_g(3, room="grouped1")
-        room = make_h_with_scalar(2, 0, banks=(0, 1))
-        replace_columns(room, (0, [(0, 2, 1)]), (1, [(0, 2, 3)]))
+        gather_g(2, room="w2_grouped")
+        gather_g(3, room="decay_wide2")
+        room = make_h_with_scalar(2, 0, banks=(0, 1), room="tab_s")
+        replace_columns(room, (0, 0, [(0, 2)]), (1, 0, [(1, 2)]))
         room = make_h_with_scalar(2, 1, banks=(2, 3))
-        replace_columns(room, (2, [(0, 2, 2)]))
+        replace_columns(room, (3, 0, [(2, 2)]))
         room = make_h_with_scalar(3, 0, banks=(4, 5))
-        replace_columns(room, (4, [(1, 2, 0)]))
+        replace_columns(room, (2, 0, [(3, 2), (4, 1)]))
         room = make_h_with_scalar(3, 1, banks=(6, 7))
-        replace_columns(room, (3, [(2, 1, 2)]), (0, [(3, 1, 0), (3, 1, 2)]), (1, [(2, 2, 1)]), (5, [(2, 2, 3)]))
+        replace_columns(room, (0, 2, [(5, 1)]), (0, 3, [(0, 1)]), (2, 3, [(1, 1)]), (1, 2, [(2, 2)]), (3, 2, [(3, 2)]))

@@ -243,16 +243,18 @@ def tile_list_place_cell_replay_kernel(tc, tab_words, tab_scales, offs, w4_words
         nc.tensor.transpose(turned[:, 0:P], rows[:, 2 * P : 3 * P], identity[:])
         drive_col = held([P, 4], F32, "drive_col")
         nc.scalar.copy(drive_col[:], turned[:, 0:4])
-        make_h_with_vector(1, 2, banks=(4, 5, 6, 7))
+        make_h_with_vector(1, 1, banks=(4, 5))
         quantize_w2()
         gather_g(1)
         gather_g(2, room="w2_grouped")
-        gather_g(3, room="decay_wide2")
-        room = make_h_with_scalar(2, 0, banks=(0, 1), room="tab_s")
-        replace_columns(room, (0, 0, [(0, 2)]), (1, 0, [(1, 2)]))
+        room = make_h_with_scalar(1, 1, banks=(6, 7), room="tab_s")
+        gather_g(3, room="grouped1")
+        replace_columns(room, (0, 0, [(4, 1)]))
+        room = make_h_with_scalar(2, 0, banks=(0, 1))
+        replace_columns(room, (1, 0, [(0, 2)]), (3, 0, [(1, 2)]))
         room = make_h_with_scalar(2, 1, banks=(2, 3))
-        replace_columns(room, (3, 0, [(2, 2)]))
+        replace_columns(room, (2, 0, [(2, 2)]))
         room = make_h_with_scalar(3, 0, banks=(4, 5))
-        replace_columns(room, (2, 0, [(3, 2), (4, 1)]))
+        replace_columns(room, (0, 1, [(3, 2)]), (1, 2, [(4, 1)]))
         room = make_h_with_scalar(3, 1, banks=(6, 7))
-        replace_columns(room, (0, 2, [(5, 1)]), (0, 3, [(0, 1)]), (2, 3, [(1, 1)]), (1, 2, [(2, 2)]), (3, 2, [(3, 2)]))
+        replace_columns(room, (2, 2, [(5, 1)]), (0, 3, [(0, 1)]), (1, 3, [(1, 1)]), (2, 3, [(2, 1)]), (3, 2, [(3, 2)]))

@@ -33,6 +33,7 @@ def tile_list_place_cell_replay_kernel(tc, tab_words, tab_scales, offs, w4_words
     with ExitStack() as ctx:
         keep = ctx.enter_context(tc.tile_pool(name="keep", bufs=1))
         ring = ctx.enter_context(tc.tile_pool(name="ring", bufs=2))
+        placed = ctx.enter_context(tc.tile_pool(name="placed", bufs=1))
         psum = ctx.enter_context(tc.psum_pool(name="psum", bufs=1))
 
         def held(shape, dtype, name, room=None):
@@ -51,17 +52,20 @@ def tile_list_place_cell_replay_kernel(tc, tab_words, tab_scales, offs, w4_words
         def columns_of(part):
             return slice(part[0], part[0] + part[1])
 
-        warm = held([P, 2], F32, "warm")
-        nc.gpsimd.memset(warm[:, 0:1], 0.0)
-        nc.scalar.activation(warm[:, 1:2], warm[:, 0:1], ACT.Tanh)
-
         tab_s = held([P, T], U8, "tab_s")
         nc.vector.memset(tab_s[:].bitcast(I32), 0)
-        w4_s_raw = held([P, 2 * H], U8, "w4_s_raw")
-        nc.gpsimd.memset(w4_s_raw[:].bitcast(I32), 0)
-        v_s1 = held([P, S], U8, "v_s1")
-        nc.vector.memset(v_s1[:].bitcast(I32), 0)
-        tab_w = [held([P, T], I32, "tab_w0"), held([P, T], I32, "tab_w1", room="warm")]
+        warm_in = held([P, 1], F32, "warm_in")
+        nc.vector.memset(warm_in[:], 0.0)
+        warm_out = held([P, 1], F32, "warm_out")
+        nc.scalar.activation(warm_out[:], warm_in[:], ACT.Tanh)
+
+        w4_s_raw = held([P, 2 * H], U8, "w4_s_raw", room="warm_in")
+        nc.vector.memset(w4_s_raw[:].bitcast(I32), 0)
+        early, late = quarters(0), quarters(1, 3)
+        moved_s = {part: held([P, part[1]], U8, "moved_s%d" % part[0]) for part in (early, late)}
+        for part in (early, late):
+            nc.gpsimd.memset(moved_s[part][:].bitcast(I32), 0)
+        tab_w = [placed.tile([P, T], I32, name="tab_w0", align_bytes=64, offset=0), held([P, T], I32, "tab_w1", room="warm_out")]
         w4_raw = held([P, H], I32, "w4_raw")
         nc.sync.dma_start(tab_w[0][:], tab_words[0].rearrange("p t i -> p (t i)").bitcast(I32))
         nc.sync.dma_start(w4_raw[:].rearrange("p (a c) -> p a c", a=2), w4_words.bitcast(I32).rearrange("a p c -> p a c"))
@@ -91,24 +95,28 @@ def tile_list_place_cell_replay_kernel(tc, tab_words, tab_scales, offs, w4_words
 
         g_tile = {}
 
-        def load_g(m, room):
-            g_tile[m] = held([P, T], F32, "g_tile%d" % m, room)
+        def load_g(m, tile):
+            g_tile[m] = tile
             nc.sync.dma_start(g_tile[m][:], gT[P * m : P * (m + 1), :])
 
-        v_w = [held([P, S], U32, "v_w%d" % a) for a in range(2)]
-        nc.vector.tensor_copy(v_w[0][:], listed(tab_w[0][:].bitcast(U32), (0, S)))
-        v_s0 = held([P, S], U8, "v_s0")
-        for part, queue in ((quarters(0), nc.scalar), (quarters(1, 3), nc.sync)):
-            nc.vector.tensor_copy(v_s0[:, columns_of(part)], listed(tab_s[:], part))
-            queue.dma_start(v_s1[0:112, columns_of(part)].bitcast(I32), v_s0[4:116, columns_of(part)].bitcast(I32))
-        v_s = [v_s0, v_s1]
-        load_g(0, "tab_w0")
+        v_w0 = held([P, S], U32, "v_w0")
+        nc.vector.tensor_copy(v_w0[:], listed(tab_w[0][:].bitcast(U32), (0, S)))
+        gathered_s = {
+            part: placed.tile([P, part[1]], U8, name="gathered_s%d" % part[0], align_bytes=64, offset=part[0]) for part in (early, late)
+        }
+        for part, queue in ((early, nc.scalar), (late, nc.sync)):
+            nc.vector.tensor_copy(gathered_s[part][:], listed(tab_s[:], part))
+            queue.dma_start(moved_s[part][0:112, :].bitcast(I32), gathered_s[part][4:116, :].bitcast(I32))
 
-        decay_wide = [held([P, S], F32, "decay_wide%d" % m) for m in range(4)]
+        def entries_of(tiles, part):
+            whole = early if part[0] < late[0] else late
+            return tiles[whole][:, part[0] - whole[0] : part[0] - whole[0] + part[1]]
+
+        load_g(0, placed.tile([P, T], F32, name="g_tile0", align_bytes=64, offset=S))
+
+        decay_wide = {m: held([P, S], F32, "decay_wide%d" % m) for m in range(2)}
         for m in range(2):
             nc.scalar.copy(decay_wide[m][:], decay_col[:, m : m + 1].to_broadcast([P, S]))
-        for m in range(2, 4):
-            nc.gpsimd.tensor_scalar(decay_wide[m][:], decay_col[:, m : m + 1].to_broadcast([P, S]), 1.0, 0.0, ALU.mult, ALU.add)
 
         w2_raw = held([P, 2, 4, N], F32, "w2_raw", room="tab_s")
         w2_rows = w2.rearrange("(b g t e) n -> b t g e n", b=2, t=4, e=8)
@@ -117,19 +125,23 @@ def tile_list_place_cell_replay_kernel(tc, tab_words, tab_scales, offs, w4_words
                 nc.sync.dma_start(w2_raw[:, b, t, :], w2_rows[b, t])
 
         w4_w = held([P, H], I32, "w4_w")
-        nc.vector.tensor_copy(
+        nc.gpsimd.tensor_copy(
             w4_w[:].rearrange("p (ab t g w) -> p ab t g w", t=4, g=16, w=4),
             w4_raw[:].rearrange("p (ab g t w) -> p ab t g w", t=4, g=16, w=4),
         )
         w4_s = held([P, 2 * H], U8, "w4_s")
-        nc.vector.tensor_copy(
+        nc.gpsimd.tensor_copy(
             w4_s[:].bitcast(I32).rearrange("p (ab t g w) -> p ab t g w", t=4, g=16, w=2),
             w4_s_raw[:].bitcast(I32).rearrange("p (ab g t w) -> p ab t g w", t=4, g=16, w=2),
         )
         w4_bytes = w4_w[:].bitcast(U8)
-        for part in (quarters(0), quarters(1, 3)):
-            nc.vector.tensor_copy(v_w[1][:, columns_of(part)], listed(tab_w[1][:].bitcast(U32), part))
-        load_g(1, "warm")
+        for m, room in ((2, "w4_raw"), (3, "warm_in")):
+            decay_wide[m] = held([P, S], F32, "decay_wide%d" % m, room)
+            nc.gpsimd.tensor_scalar(decay_wide[m][:], decay_col[:, m : m + 1].to_broadcast([P, S]), 1.0, 0.0, ALU.mult, ALU.add)
+        v_w1 = {part: held([P, part[1]], U32, "v_w1_%d" % part[0]) for part in (early, late)}
+        for part in (early, late):
+            nc.vector.tensor_copy(v_w1[part][:], listed(tab_w[1][:].bitcast(U32), part))
+        load_g(1, held([P, T], F32, "g_tile1", "warm_out"))
 
         decayed = {}
 
@@ -145,15 +157,15 @@ def tile_list_place_cell_replay_kernel(tc, tab_words, tab_scales, offs, w4_words
                     out=bank[:, bank_col : bank_col + part[1]],
                     lhsT=w4_bytes[:, 2 * w4_col : 2 * (w4_col + P)].bitcast(FP4X4),
                     lhsT_scale=w4_s[:, w4_col : w4_col + P],
-                    rhs=v_w[a][:, columns_of(part)].bitcast(FP8X4),
-                    rhs_scale=v_s[a][:, columns_of(part)],
+                    rhs=(v_w0[:, columns_of(part)] if a == 0 else entries_of(v_w1, part)).bitcast(FP8X4),
+                    rhs_scale=entries_of(gathered_s if a == 0 else moved_s, part),
                     start=(s == 0),
                     stop=(s == len(steps) - 1),
                 )
 
         h_w = [held([P, 2 * QUARTER], U32, "h_w%d" % q) for q in range(4)]
         h_s = [held([P, 2 * QUARTER], U8, "h_s%d" % q) for q in range(4)]
-        grouped = [held([P, 2, QUARTER * 4], BF16, "grouped%d" % q) for q in range(4)]
+        grouped = {q: held([P, 2, QUARTER * 4], BF16, "grouped%d" % q) for q in range(1, 4)}
 
         def quantize_h(q):
             nc.vector.quantize_mx(out=h_w[q][:].bitcast(FP8X4), scales=h_s[q][:], in_=grouped[q][:].rearrange("p b c -> p (b c)"))
@@ -163,7 +175,7 @@ def tile_list_place_cell_replay_kernel(tc, tab_words, tab_scales, offs, w4_words
             for b in range(passes):
                 for u in range(2):
                     bank = psum_bank(banks[2 * b + u])
-                    first_product(bank, b, [(t, (q * QUARTER + u * P, P), t * P) for t in range(4)], (0, 1) if q == 0 else (1, 0))
+                    first_product(bank, b, [(t, (q * QUARTER + u * P, P), t * P) for t in range(4)], (0, 1) if (q, b) == (0, 0) else (1, 0))
                     nc.scalar.activation(
                         rate[:, b, u * BANK : (u + 1) * BANK].rearrange("p (j t) -> p j t", t=4),
                         bank[:].rearrange("p (t j) -> p j t", t=4),
@@ -192,7 +204,10 @@ def tile_list_place_cell_replay_kernel(tc, tab_words, tab_scales, offs, w4_words
                     nc.scalar.activation(
                         rounded[:, t * count : (t + 1) * count], saturated[:, d * count : (d + 1) * count], ACT.Copy, scale=peak_col[b][:, t : t + 1]
                     )
-            nc.scalar.copy(grouped[q][:, b, :].rearrange("p (j t) -> p j t", t=4), rounded[:].rearrange("p (t j) -> p j t", t=4))
+            nc.scalar.copy(
+                grouped[q][:, b, :].rearrange("p (c i t) -> p c t i", i=4, t=4),
+                rounded[:].rearrange("p (t c i) -> p c t i", i=4, t=4),
+            )
             if b == 1:
                 quantize_h(q)
             return room
@@ -203,7 +218,10 @@ def tile_list_place_cell_replay_kernel(tc, tab_words, tab_scales, offs, w4_words
         def quantize_w2():
             w2_grouped = held([P, 2, N * 4], BF16, "w2_grouped")
             for b in range(2):
-                nc.scalar.copy(w2_grouped[:, b, :].rearrange("p (n t) -> p n t", t=4), w2_raw[:, b, :, :].rearrange("p t n -> p n t"))
+                nc.scalar.copy(
+                    w2_grouped[:, b, :].rearrange("p (c i t) -> p c t i", i=4, t=4),
+                    w2_raw[:, b, :, :].rearrange("p t (c i) -> p c t i", i=4),
+                )
             nc.vector.quantize_mx(out=w2_w[:].bitcast(FP8X4), scales=w2_s[:], in_=w2_grouped[:].rearrange("p b c -> p (b c)"))
 
         def replace_columns(room, *jobs):
@@ -232,18 +250,23 @@ def tile_list_place_cell_replay_kernel(tc, tab_words, tab_scales, offs, w4_words
                     filled = filled + count * QUARTER
                 part = quarters(first_q, q - first_q)
                 nc.vector.tensor_tensor(listed(g_tile[m][:], part), decayed[m][:, columns_of(part)], driven[:, start:filled], ALU.add)
-                if q == 4:
+                if q == 4 and m < 3:
                     nc.sync.dma_start(out[P * m : P * (m + 1), :], g_tile[m][:])
+                elif q == 4:
+                    for half, queue in enumerate((nc.sync, nc.scalar)):
+                        columns = slice(half * T // 2, (half + 1) * T // 2)
+                        queue.dma_start(out[P * m : P * (m + 1), columns], g_tile[m][:, columns])
 
         gather_g(0)
-        load_g(2, "decay_wide0")
+        grouped[0] = held([P, 2, QUARTER * 4], BF16, "grouped0", room="decay_wide0")
         make_h_with_vector(0, 2, banks=(0, 1, 2, 3))
-        load_g(3, "rate0")
+        load_g(2, held([P, T], F32, "g_tile2", "rate0"))
         turned = psum_bank(3)
         nc.tensor.transpose(turned[:, 0:P], rows[:, 2 * P : 3 * P], identity[:])
         drive_col = held([P, 4], F32, "drive_col")
         nc.scalar.copy(drive_col[:], turned[:, 0:4])
         make_h_with_vector(1, 1, banks=(4, 5))
+        load_g(3, held([P, T], F32, "g_tile3", "rate1"))
         quantize_w2()
         gather_g(1)
         gather_g(2, room="w2_grouped")

@@ -114,9 +114,10 @@ def tile_list_place_cell_replay_kernel(tc, tab_words, tab_scales, offs, w4_words
 
         load_g(0, placed.tile([P, T], F32, name="g_tile0", align_bytes=64, offset=S))
 
-        decay_wide = {m: held([P, S], F32, "decay_wide%d" % m) for m in range(2)}
-        for m in range(2):
-            nc.scalar.copy(decay_wide[m][:], decay_col[:, m : m + 1].to_broadcast([P, S]))
+        widths = (S, S, S // 2, S // 2)
+        decay_wide = [held([P, widths[m]], F32, "decay_wide%d" % m) for m in range(4)]
+        for m in range(4):
+            nc.scalar.copy(decay_wide[m][:], decay_col[:, m : m + 1].to_broadcast([P, widths[m]]))
 
         w2_raw = held([P, 2, 4, N], F32, "w2_raw", room="tab_s")
         w2_rows = w2.rearrange("(b g t e) n -> b t g e n", b=2, t=4, e=8)
@@ -125,19 +126,16 @@ def tile_list_place_cell_replay_kernel(tc, tab_words, tab_scales, offs, w4_words
                 nc.sync.dma_start(w2_raw[:, b, t, :], w2_rows[b, t])
 
         w4_w = held([P, H], I32, "w4_w")
-        nc.gpsimd.tensor_copy(
+        nc.vector.tensor_copy(
             w4_w[:].rearrange("p (ab t g w) -> p ab t g w", t=4, g=16, w=4),
             w4_raw[:].rearrange("p (ab g t w) -> p ab t g w", t=4, g=16, w=4),
         )
         w4_s = held([P, 2 * H], U8, "w4_s")
-        nc.gpsimd.tensor_copy(
+        nc.vector.tensor_copy(
             w4_s[:].bitcast(I32).rearrange("p (ab t g w) -> p ab t g w", t=4, g=16, w=2),
             w4_s_raw[:].bitcast(I32).rearrange("p (ab g t w) -> p ab t g w", t=4, g=16, w=2),
         )
         w4_bytes = w4_w[:].bitcast(U8)
-        for m, room in ((2, "w4_raw"), (3, "warm_in")):
-            decay_wide[m] = held([P, S], F32, "decay_wide%d" % m, room)
-            nc.gpsimd.tensor_scalar(decay_wide[m][:], decay_col[:, m : m + 1].to_broadcast([P, S]), 1.0, 0.0, ALU.mult, ALU.add)
         v_w1 = {part: held([P, part[1]], U32, "v_w1_%d" % part[0]) for part in (early, late)}
         for part in (early, late):
             nc.vector.tensor_copy(v_w1[part][:], listed(tab_w[1][:].bitcast(U32), part))
@@ -147,7 +145,9 @@ def tile_list_place_cell_replay_kernel(tc, tab_words, tab_scales, offs, w4_words
 
         def gather_g(m, room=None):
             decayed[m] = held([P, S], F32, "decayed%d" % m, room)
-            nc.vector.tensor_tensor(decayed[m][:], listed(g_tile[m][:], (0, S)), decay_wide[m][:], ALU.mult)
+            for first in range(0, S, widths[m]):
+                part = (first, widths[m])
+                nc.vector.tensor_tensor(decayed[m][:, columns_of(part)], listed(g_tile[m][:], part), decay_wide[m][:], ALU.mult)
 
         def first_product(bank, b, pieces, order=(1, 0)):
             steps = [(a,) + piece for a in order for piece in pieces]
@@ -217,8 +217,8 @@ def tile_list_place_cell_replay_kernel(tc, tab_words, tab_scales, offs, w4_words
 
         def quantize_w2():
             w2_grouped = held([P, 2, N * 4], BF16, "w2_grouped")
-            for b in range(2):
-                nc.scalar.copy(
+            for b, copy in enumerate((nc.scalar.copy, nc.vector.tensor_copy)):
+                copy(
                     w2_grouped[:, b, :].rearrange("p (c i t) -> p c t i", i=4, t=4),
                     w2_raw[:, b, :, :].rearrange("p t (c i) -> p c t i", i=4),
                 )
@@ -270,14 +270,14 @@ def tile_list_place_cell_replay_kernel(tc, tab_words, tab_scales, offs, w4_words
         quantize_w2()
         gather_g(1)
         gather_g(2, room="w2_grouped")
-        room = make_h_with_scalar(1, 1, banks=(6, 7), room="tab_s")
+        room = make_h_with_scalar(1, 1, banks=(6, 7))
         gather_g(3, room="grouped1")
         replace_columns(room, (0, 0, [(4, 1)]))
         room = make_h_with_scalar(2, 0, banks=(0, 1))
-        replace_columns(room, (1, 0, [(0, 2)]), (3, 0, [(1, 2)]))
+        replace_columns(room, (1, 0, [(0, 2)]), (2, 0, [(1, 2)]))
         room = make_h_with_scalar(2, 1, banks=(2, 3))
-        replace_columns(room, (2, 0, [(2, 2)]))
+        replace_columns(room, (3, 0, [(2, 2)]))
         room = make_h_with_scalar(3, 0, banks=(4, 5))
-        replace_columns(room, (0, 1, [(3, 2)]), (1, 2, [(4, 1)]))
+        replace_columns(room, (0, 1, [(3, 1)]))
         room = make_h_with_scalar(3, 1, banks=(6, 7))
-        replace_columns(room, (2, 2, [(5, 1)]), (0, 3, [(0, 1)]), (1, 3, [(1, 1)]), (2, 3, [(2, 1)]), (3, 2, [(3, 2)]))
+        replace_columns(room, (0, 2, [(4, 1)]), (0, 3, [(0, 1)]), (1, 2, [(1, 2)]), (2, 2, [(2, 2)]), (3, 2, [(3, 2)]))

@@ -22,6 +22,7 @@ PASS = 512
 BANK = 512
 GROUP = 16
 QUARTER = S // 4
+SHARED_AT = S + 4 * T + 2 * S
 
 
 def quarters(first, count=1):
@@ -58,7 +59,6 @@ def tile_list_place_cell_replay_kernel(tc, tab_words, tab_scales, offs, w4_words
         nc.vector.memset(warm_in[:], 0.0)
         warm_out = held([P, 1], F32, "warm_out")
         nc.scalar.activation(warm_out[:], warm_in[:], ACT.Tanh)
-
         w4_s_raw = held([P, 2 * H], U8, "w4_s_raw", room="warm_in")
         nc.vector.memset(w4_s_raw[:].bitcast(I32), 0)
         early, late = quarters(0), quarters(1, 3)
@@ -115,7 +115,8 @@ def tile_list_place_cell_replay_kernel(tc, tab_words, tab_scales, offs, w4_words
         load_g(0, placed.tile([P, T], F32, name="g_tile0", align_bytes=64, offset=S))
 
         widths = (S, S, S // 2, S // 2)
-        decay_wide = [held([P, widths[m]], F32, "decay_wide%d" % m) for m in range(4)]
+        decay_wide = [placed.tile([P, S], F32, name="decay_wide0", align_bytes=64, offset=SHARED_AT)]
+        decay_wide = decay_wide + [held([P, widths[m]], F32, "decay_wide%d" % m) for m in range(1, 4)]
         for m in range(4):
             nc.scalar.copy(decay_wide[m][:], decay_col[:, m : m + 1].to_broadcast([P, widths[m]]))
 
@@ -149,8 +150,8 @@ def tile_list_place_cell_replay_kernel(tc, tab_words, tab_scales, offs, w4_words
                 part = (first, widths[m])
                 nc.vector.tensor_tensor(decayed[m][:, columns_of(part)], listed(g_tile[m][:], part), decay_wide[m][:], ALU.mult)
 
-        def first_product(bank, b, pieces, order=(1, 0)):
-            steps = [(a,) + piece for a in order for piece in pieces]
+        def first_product(bank, b, spans, order=(1, 0)):
+            steps = [(a,) + span for a in order for span in spans]
             for s, (a, t, part, bank_col) in enumerate(steps):
                 w4_col = a * H + b * PASS + t * P
                 nc.tensor.matmul_mx(
@@ -190,10 +191,10 @@ def tile_list_place_cell_replay_kernel(tc, tab_words, tab_scales, offs, w4_words
             if passes == 2:
                 quantize_h(q)
 
-        def make_h_with_scalar(q, b, banks, room=None):
+        def make_h_with_scalar(q, b, banks):
             first, count = quarters(q)
-            room = room or "rounded%d_%d" % (q, b)
-            rounded = held([P, 4 * count], BF16, "rounded%d_%d" % (q, b), room)
+            room = "rounded%d_%d" % (q, b)
+            rounded = held([P, 4 * count], BF16, room)
             for u, number in enumerate(banks):
                 bank = psum_bank(number)
                 first_product(bank, b, [(2 * u + d, (first + j, P), d * count + j) for d in range(2) for j in range(0, count, P)])
@@ -225,59 +226,55 @@ def tile_list_place_cell_replay_kernel(tc, tab_words, tab_scales, offs, w4_words
             nc.vector.quantize_mx(out=w2_w[:].bitcast(FP8X4), scales=w2_s[:], in_=w2_grouped[:].rearrange("p b c -> p (b c)"))
 
         def replace_columns(room, *jobs):
-            driven = held([P, QUARTER * sum(count for job in jobs for number, count in job[2])], F32, "driven", room)
+            driven = held([P, QUARTER * sum(job[2] for job in jobs)], F32, "driven", room)
             filled = 0
-            for m, first_q, stretches in jobs:
-                q = first_q
-                start = filled
-                for number, count in stretches:
-                    bank = psum_bank(number)
-                    for u in range(count):
-                        for b in range(2):
-                            nc.tensor.matmul_mx(
-                                out=bank[:, u * QUARTER : (u + 1) * QUARTER],
-                                lhsT=w2_w[:, b * N + m * P : b * N + (m + 1) * P].bitcast(FP8X4),
-                                lhsT_scale=w2_s[:, b * N + m * P : b * N + (m + 1) * P],
-                                rhs=h_w[q + u][:, b * QUARTER : (b + 1) * QUARTER].bitcast(FP8X4),
-                                rhs_scale=h_s[q + u][:, b * QUARTER : (b + 1) * QUARTER],
-                                start=(b == 0),
-                                stop=(b == 1),
-                            )
-                    nc.scalar.activation(
-                        driven[:, filled : filled + count * QUARTER], bank[:, 0 : count * QUARTER], ACT.Identity, bias=drive_col[:, m : m + 1]
-                    )
-                    q = q + count
-                    filled = filled + count * QUARTER
-                part = quarters(first_q, q - first_q)
-                nc.vector.tensor_tensor(listed(g_tile[m][:], part), decayed[m][:, columns_of(part)], driven[:, start:filled], ALU.add)
-                if q == 4 and m < 3:
+            for m, first_q, count, number in jobs:
+                bank = psum_bank(number)
+                for u in range(count):
+                    for b in range(2):
+                        nc.tensor.matmul_mx(
+                            out=bank[:, u * QUARTER : (u + 1) * QUARTER],
+                            lhsT=w2_w[:, b * N + m * P : b * N + (m + 1) * P].bitcast(FP8X4),
+                            lhsT_scale=w2_s[:, b * N + m * P : b * N + (m + 1) * P],
+                            rhs=h_w[first_q + u][:, b * QUARTER : (b + 1) * QUARTER].bitcast(FP8X4),
+                            rhs_scale=h_s[first_q + u][:, b * QUARTER : (b + 1) * QUARTER],
+                            start=(b == 0),
+                            stop=(b == 1),
+                        )
+                part = quarters(first_q, count)
+                values = driven[:, filled : filled + part[1]]
+                filled = filled + part[1]
+                nc.scalar.activation(values, bank[:, 0 : part[1]], ACT.Identity, bias=drive_col[:, m : m + 1])
+                nc.vector.tensor_tensor(listed(g_tile[m][:], part), decayed[m][:, columns_of(part)], values, ALU.add)
+                finished = first_q + count == 4
+                if finished and m < 3:
                     nc.sync.dma_start(out[P * m : P * (m + 1), :], g_tile[m][:])
-                elif q == 4:
+                elif finished:
                     for half, queue in enumerate((nc.sync, nc.scalar)):
                         columns = slice(half * T // 2, (half + 1) * T // 2)
                         queue.dma_start(out[P * m : P * (m + 1), columns], g_tile[m][:, columns])
 
         gather_g(0)
-        grouped[0] = held([P, 2, QUARTER * 4], BF16, "grouped0", room="decay_wide0")
+        grouped[0] = placed.tile([P, 2, QUARTER * 4], BF16, name="grouped0", align_bytes=64, offset=SHARED_AT - 2 * S)
+        load_g(2, placed.tile([P, T], F32, name="g_tile2", align_bytes=64, offset=SHARED_AT + 2 * S))
         make_h_with_vector(0, 2, banks=(0, 1, 2, 3))
-        load_g(2, held([P, T], F32, "g_tile2", "rate0"))
+        load_g(3, held([P, T], F32, "g_tile3", "rate0"))
         turned = psum_bank(3)
         nc.tensor.transpose(turned[:, 0:P], rows[:, 2 * P : 3 * P], identity[:])
         drive_col = held([P, 4], F32, "drive_col")
         nc.scalar.copy(drive_col[:], turned[:, 0:4])
         make_h_with_vector(1, 1, banks=(4, 5))
-        load_g(3, held([P, T], F32, "g_tile3", "rate1"))
         quantize_w2()
         gather_g(1)
         gather_g(2, room="w2_grouped")
         room = make_h_with_scalar(1, 1, banks=(6, 7))
         gather_g(3, room="grouped1")
-        replace_columns(room, (0, 0, [(4, 1)]))
+        replace_columns(room, (0, 0, 1, 4))
         room = make_h_with_scalar(2, 0, banks=(0, 1))
-        replace_columns(room, (1, 0, [(0, 2)]), (2, 0, [(1, 2)]))
+        replace_columns(room, (1, 0, 2, 0), (2, 0, 2, 1))
         room = make_h_with_scalar(2, 1, banks=(2, 3))
-        replace_columns(room, (3, 0, [(2, 2)]))
+        replace_columns(room, (3, 0, 2, 2))
         room = make_h_with_scalar(3, 0, banks=(4, 5))
-        replace_columns(room, (0, 1, [(3, 1)]))
+        replace_columns(room, (0, 1, 2, 3))
         room = make_h_with_scalar(3, 1, banks=(6, 7))
-        replace_columns(room, (0, 2, [(4, 1)]), (0, 3, [(0, 1)]), (1, 2, [(1, 2)]), (2, 2, [(2, 2)]), (3, 2, [(3, 2)]))
+        replace_columns(room, (1, 2, 1, 4), (0, 3, 1, 0), (1, 3, 1, 1), (2, 2, 2, 2), (3, 2, 2, 3))

@@ -22,7 +22,16 @@ PASS = 512
 BANK = 512
 GROUP = 16
 QUARTER = S // 4
-SHARED_AT = S + 4 * T + 2 * S
+HALF = N // 2
+TABS_AT = 0
+G0_AT = TABS_AT + T
+LATER_AT = G0_AT + 4 * T
+G_AT = [G0_AT] + [LATER_AT + 4 * T * m for m in range(3)]
+W2_AT = [G_AT[3] + 4 * T + 16 * HALF * i for i in range(4)]
+W4_AT = W2_AT[3] + 32 * HALF
+W4S_AT = W4_AT + 4 * H
+TAB0_AT = W4S_AT + 2 * H
+TAB1_AT = TAB0_AT + 4 * T
 
 
 def quarters(first, count=1):
@@ -33,11 +42,12 @@ def tile_list_place_cell_replay_kernel(tc, tab_words, tab_scales, offs, w4_words
     nc = tc.nc
     with ExitStack() as ctx:
         keep = ctx.enter_context(tc.tile_pool(name="keep", bufs=1))
-        ring = ctx.enter_context(tc.tile_pool(name="ring", bufs=2))
         placed = ctx.enter_context(tc.tile_pool(name="placed", bufs=1))
         psum = ctx.enter_context(tc.psum_pool(name="psum", bufs=1))
 
         def held(shape, dtype, name, room=None):
+            if isinstance(room, int):
+                return placed.tile(shape, dtype, name=name, align_bytes=64, offset=room)
             return keep.tile(shape, dtype, name=name, tag=room or name, align_bytes=64)
 
         def psum_bank(number):
@@ -53,83 +63,76 @@ def tile_list_place_cell_replay_kernel(tc, tab_words, tab_scales, offs, w4_words
         def columns_of(part):
             return slice(part[0], part[0] + part[1])
 
-        tab_s = held([P, T], U8, "tab_s")
-        nc.vector.memset(tab_s[:].bitcast(I32), 0)
-        warm_in = held([P, 1], F32, "warm_in")
-        nc.vector.memset(warm_in[:], 0.0)
-        warm_out = held([P, 1], F32, "warm_out")
-        nc.scalar.activation(warm_out[:], warm_in[:], ACT.Tanh)
-        w4_s_raw = held([P, 2 * H], U8, "w4_s_raw", room="warm_in")
+        tab_s_room = held([P, LATER_AT - TABS_AT], U8, "tab_s", TABS_AT)
+        tab_s = tab_s_room[:, 0:T]
+        zeros = held([P, (TAB1_AT - W4S_AT + 192) // 4], F32, "zeros", W4S_AT - 64)
+        nc.vector.memset(zeros[:, 0:32], 0.0)
+        nc.vector.memset(tab_s.bitcast(I32), 0)
+        rows = held([P, 4 * P], F32, "rows")
+
+        def clear_rows(first, end, source):
+            nc.vector.tensor_copy(
+                rows[:, first:end].rearrange("p (r c) -> p r c", c=32), source.unsqueeze(1).to_broadcast([P, (end - first) // 32, 32])
+            )
+
+        clear_rows(0, 2 * P, zeros[:, 0:32])
+        w4_s_raw = held([P, 2 * H], U8, "w4_s_raw", W4S_AT)
         nc.vector.memset(w4_s_raw[:].bitcast(I32), 0)
+        zeros_again = held([P, 32], F32, "zeros_again", TAB1_AT)
+        nc.vector.memset(zeros_again[:], 0.0)
+        clear_rows(2 * P, 3 * P, zeros_again[:])
+        zero_col = held([P, 1], F32, "zero_col")
+        nc.gpsimd.memset(zero_col[:], 0.0)
+        nc.scalar.activation(rows[:, 3 * P : 4 * P], zero_col[:].to_broadcast([P, P]), ACT.Tanh)
         early, late = quarters(0), quarters(1, 3)
-        moved_s = {part: held([P, part[1]], U8, "moved_s%d" % part[0]) for part in (early, late)}
-        for part in (early, late):
-            nc.gpsimd.memset(moved_s[part][:].bitcast(I32), 0)
-        tab_w = [placed.tile([P, T], I32, name="tab_w0", align_bytes=64, offset=0), held([P, T], I32, "tab_w1", room="warm_out")]
-        w4_raw = held([P, H], I32, "w4_raw")
-        nc.sync.dma_start(tab_w[0][:], tab_words[0].rearrange("p t i -> p (t i)").bitcast(I32))
-        nc.sync.dma_start(w4_raw[:].rearrange("p (a c) -> p a c", a=2), w4_words.bitcast(I32).rearrange("a p c -> p a c"))
+        moved_s = held([P, S], U8, "moved_s")
+        nc.gpsimd.memset(moved_s[:].bitcast(I32), 0)
+        tab_w = [held([P, T], I32, "tab_w0", TAB0_AT)[:], held([P, T], I32, "tab_w1", TAB1_AT)[:]]
+        w4_raw = held([P, (W4S_AT - LATER_AT) // 4], I32, "w4_raw", LATER_AT)[:, (W4_AT - LATER_AT) // 4 :]
+        for q in range(4):
+            nc.sync.dma_start(tab_s[32 * q : 32 * q + 8, :].bitcast(I32), tab_scales[:, 4 * q : 4 * q + 4, :].bitcast(I32))
+        nc.sync.dma_start(tab_w[0], tab_words[0].rearrange("p t i -> p (t i)").bitcast(I32))
+        nc.sync.dma_start(w4_raw.rearrange("p (a c) -> p a c", a=2), w4_words.bitcast(I32).rearrange("a p c -> p a c"))
         for q in range(4):
             nc.sync.dma_start(
                 w4_s_raw[32 * q : 32 * q + 4, :].bitcast(I32).rearrange("p (a c) -> p a c", a=2),
                 w4_scales[:, 4 * q : 4 * q + 4, :].bitcast(I32).rearrange("a r c -> r a c"),
             )
-        for q in range(4):
-            nc.sync.dma_start(tab_s[32 * q : 32 * q + 8, :].bitcast(I32), tab_scales[:, 4 * q : 4 * q + 4, :].bitcast(I32))
-        nc.sync.dma_start(tab_w[1][:], tab_words[1].rearrange("p t i -> p (t i)").bitcast(I32))
+        nc.sync.dma_start(tab_w[1], tab_words[1].rearrange("p t i -> p (t i)").bitcast(I32))
 
-        rows = held([P, 3 * P], F32, "rows")
-        nc.gpsimd.memset(rows[:], 0.0)
-        nc.gpsimd.dma_start(rows[4:8, 0:P], decay.rearrange("(m p) -> m p", p=P))
-        nc.gpsimd.dma_start(rows[0:4, 0 : 2 * P].rearrange("t (bg e) -> t bg e", e=8), peak.rearrange("(bg t e) -> t bg e", t=4, e=8))
-        nc.gpsimd.dma_start(rows[0:4, 2 * P : 3 * P], drive.rearrange("(m p) -> m p", p=P))
         identity = held([P, P], F32, "identity")
         make_identity(nc, identity[:])
+        nc.gpsimd.dma_start(rows[0:4, 0 : 2 * P].rearrange("t (bg e) -> t bg e", e=8), peak.rearrange("(bg t e) -> t bg e", t=4, e=8))
+        nc.gpsimd.dma_start(rows[0:4, 2 * P : 3 * P], decay.rearrange("(m p) -> m p", p=P))
+        nc.gpsimd.dma_start(rows[0:4, 3 * P : 4 * P], drive.rearrange("(m p) -> m p", p=P))
         turned = psum_bank(7)
         for block in range(2):
             nc.tensor.transpose(turned[:, block * P : (block + 1) * P], rows[:, block * P : (block + 1) * P], identity[:])
-        per_partition = held([P, 2, 8], F32, "per_partition")
-        nc.scalar.copy(per_partition[:], turned[:, 0 : 2 * P].rearrange("p (block c) -> p block c", block=2)[:, :, 0:8])
-        peak_col = [per_partition[:, 0, 0:4], per_partition[:, 1, 0:4]]
-        decay_col = per_partition[:, 0, 4:8]
+        peak_col = held([P, 2, 4], F32, "peak_col")
+        nc.scalar.copy(peak_col[:], turned[:, 0 : 2 * P].rearrange("p (block c) -> p block c", block=2)[:, :, 0:4])
 
         g_tile = {}
 
-        def load_g(m, tile):
-            g_tile[m] = tile
+        def load_g(m, room):
+            g_tile[m] = held([P, T], F32, "g_tile%d" % m, room)
             nc.sync.dma_start(g_tile[m][:], gT[P * m : P * (m + 1), :])
 
-        v_w0 = held([P, S], U32, "v_w0")
-        nc.vector.tensor_copy(v_w0[:], listed(tab_w[0][:].bitcast(U32), (0, S)))
-        gathered_s = {
-            part: placed.tile([P, part[1]], U8, name="gathered_s%d" % part[0], align_bytes=64, offset=part[0]) for part in (early, late)
-        }
-        for part, queue in ((early, nc.scalar), (late, nc.sync)):
-            nc.vector.tensor_copy(gathered_s[part][:], listed(tab_s[:], part))
-            queue.dma_start(moved_s[part][0:112, :].bitcast(I32), gathered_s[part][4:116, :].bitcast(I32))
+        gathered_s = held([P, S], U8, "gathered_s")
+        nc.vector.tensor_copy(gathered_s[:], listed(tab_s, (0, S)))
+        nc.sync.dma_start(moved_s[0:112, :].bitcast(I32), gathered_s[4:116, :].bitcast(I32))
+        v_w0 = [held([P, S // 2], U32, "v_w0_0")]
+        nc.vector.tensor_copy(v_w0[0][:], listed(tab_w[0].bitcast(U32), quarters(0, 2)))
 
         def entries_of(tiles, part):
             whole = early if part[0] < late[0] else late
             return tiles[whole][:, part[0] - whole[0] : part[0] - whole[0] + part[1]]
 
-        load_g(0, placed.tile([P, T], F32, name="g_tile0", align_bytes=64, offset=S))
-
-        widths = (S, S, S // 2, S // 2)
-        decay_wide = [placed.tile([P, S], F32, name="decay_wide0", align_bytes=64, offset=SHARED_AT)]
-        decay_wide = decay_wide + [held([P, widths[m]], F32, "decay_wide%d" % m) for m in range(1, 4)]
-        for m in range(4):
-            nc.scalar.copy(decay_wide[m][:], decay_col[:, m : m + 1].to_broadcast([P, widths[m]]))
-
-        w2_raw = held([P, 2, 4, N], F32, "w2_raw", room="tab_s")
-        w2_rows = w2.rearrange("(b g t e) n -> b t g e n", b=2, t=4, e=8)
-        for b in range(2):
-            for t in range(4):
-                nc.sync.dma_start(w2_raw[:, b, t, :], w2_rows[b, t])
+        load_g(0, G_AT[0])
 
         w4_w = held([P, H], I32, "w4_w")
         nc.vector.tensor_copy(
             w4_w[:].rearrange("p (ab t g w) -> p ab t g w", t=4, g=16, w=4),
-            w4_raw[:].rearrange("p (ab g t w) -> p ab t g w", t=4, g=16, w=4),
+            w4_raw.rearrange("p (ab g t w) -> p ab t g w", t=4, g=16, w=4),
         )
         w4_s = held([P, 2 * H], U8, "w4_s")
         nc.vector.tensor_copy(
@@ -137,18 +140,32 @@ def tile_list_place_cell_replay_kernel(tc, tab_words, tab_scales, offs, w4_words
             w4_s_raw[:].bitcast(I32).rearrange("p (ab g t w) -> p ab t g w", t=4, g=16, w=2),
         )
         w4_bytes = w4_w[:].bitcast(U8)
+        v_w0.append(held([P, S // 2], U32, "v_w0_1", W4S_AT))
+        nc.vector.tensor_copy(v_w0[1][:], listed(tab_w[0].bitcast(U32), quarters(2, 2)))
         v_w1 = {part: held([P, part[1]], U32, "v_w1_%d" % part[0]) for part in (early, late)}
         for part in (early, late):
-            nc.vector.tensor_copy(v_w1[part][:], listed(tab_w[1][:].bitcast(U32), part))
-        load_g(1, held([P, T], F32, "g_tile1", "warm_out"))
+            nc.vector.tensor_copy(v_w1[part][:], listed(tab_w[1].bitcast(U32), part))
 
-        decayed = {}
+        w2_rows = w2.rearrange("(b g t e) n -> b t g e n", b=2, t=4, e=8)
+        w2_raw = {}
+
+        def load_w2(half, rooms):
+            for b in range(2):
+                w2_raw[half, b] = held([P, 4, HALF], F32, "w2_raw%d_%d" % (half, b), rooms[b])
+                for t in range(4):
+                    nc.sync.dma_start(w2_raw[half, b][:, t, :], w2_rows[b, t][:, :, half * HALF : (half + 1) * HALF])
+
+        load_w2(0, (W2_AT[0], W2_AT[1]))
+        load_g(1, G_AT[1])
+        load_g(2, G_AT[2])
+        load_w2(1, (W2_AT[2], W2_AT[3]))
+        load_g(3, G_AT[3])
+
+        picked = {}
 
         def gather_g(m, room=None):
-            decayed[m] = held([P, S], F32, "decayed%d" % m, room)
-            for first in range(0, S, widths[m]):
-                part = (first, widths[m])
-                nc.vector.tensor_tensor(decayed[m][:, columns_of(part)], listed(g_tile[m][:], part), decay_wide[m][:], ALU.mult)
+            picked[m] = held([P, S], F32, "picked%d" % m, room)
+            nc.vector.tensor_copy(picked[m][:], listed(g_tile[m][:], (0, S)))
 
         def first_product(bank, b, spans, order=(1, 0)):
             steps = [(a,) + span for a in order for span in spans]
@@ -158,123 +175,190 @@ def tile_list_place_cell_replay_kernel(tc, tab_words, tab_scales, offs, w4_words
                     out=bank[:, bank_col : bank_col + part[1]],
                     lhsT=w4_bytes[:, 2 * w4_col : 2 * (w4_col + P)].bitcast(FP4X4),
                     lhsT_scale=w4_s[:, w4_col : w4_col + P],
-                    rhs=(v_w0[:, columns_of(part)] if a == 0 else entries_of(v_w1, part)).bitcast(FP8X4),
-                    rhs_scale=entries_of(gathered_s if a == 0 else moved_s, part),
+                    rhs=(v_w0[part[0] // (S // 2)][:, part[0] % (S // 2) : part[0] % (S // 2) + part[1]] if a == 0 else entries_of(v_w1, part)).bitcast(FP8X4),
+                    rhs_scale=(gathered_s if a == 0 else moved_s)[:, columns_of(part)],
                     start=(s == 0),
                     stop=(s == len(steps) - 1),
                 )
 
-        h_w = [held([P, 2 * QUARTER], U32, "h_w%d" % q) for q in range(4)]
-        h_s = [held([P, 2 * QUARTER], U8, "h_s%d" % q) for q in range(4)]
-        grouped = {q: held([P, 2, QUARTER * 4], BF16, "grouped%d" % q) for q in range(1, 4)}
+        PIECE = 4 * QUARTER
+        grouped, words, scales, saturated = {}, {}, {}, {}
 
-        def quantize_h(q):
-            nc.vector.quantize_mx(out=h_w[q][:].bitcast(FP8X4), scales=h_s[q][:], in_=grouped[q][:].rearrange("p b c -> p (b c)"))
+        def open_round(q, room=None):
+            pieces = 4 if q < 2 else 2
+            grouped[q] = held([P, pieces * PIECE], BF16, "grouped%d" % q, room)
+            words[q] = held([P, pieces * QUARTER], U32, "words%d" % q)
+            scales[q] = held([P, pieces * QUARTER], U8, "scales%d" % q)
 
-        def make_h_with_vector(q, passes, banks):
-            rate = held([P, passes, QUARTER * 4], F32, "rate%d" % q)
-            for b in range(passes):
-                for u in range(2):
-                    bank = psum_bank(banks[2 * b + u])
-                    first_product(bank, b, [(t, (q * QUARTER + u * P, P), t * P) for t in range(4)], (0, 1) if (q, b) == (0, 0) else (1, 0))
-                    nc.scalar.activation(
-                        rate[:, b, u * BANK : (u + 1) * BANK].rearrange("p (j t) -> p j t", t=4),
-                        bank[:].rearrange("p (t j) -> p j t", t=4),
-                        ACT.Tanh,
-                    )
-            nc.vector.tensor_tensor(
-                grouped[q][:, 0:passes, :].rearrange("p b (j t) -> p b j t", t=4),
-                rate[:].rearrange("p b (j t) -> p b j t", t=4),
-                per_partition[:, 0:passes, 0:4].unsqueeze(2).to_broadcast([P, passes, QUARTER, 4]),
-                ALU.mult,
-            )
-            if passes == 2:
-                quantize_h(q)
+        def quantize(q):
+            nc.vector.quantize_mx(out=words[q][:].bitcast(FP8X4), scales=scales[q][:], in_=grouped[q][:])
 
-        def make_h_with_scalar(q, b, banks):
+        def tanh_side_by_side(q):
+            for u in range(2):
+                bank = psum_bank(u)
+                first_product(bank, 0, [(t, (q * QUARTER + u * P, P), t * P) for t in range(4)], (0, 1) if q == 0 else (1, 0))
+                nc.scalar.activation(
+                    saturated[q][:, u * BANK : (u + 1) * BANK].rearrange("p (j t) -> p j t", t=4),
+                    bank[:].rearrange("p (t j) -> p j t", t=4),
+                    ACT.Tanh,
+                )
+
+        def piece_on_gpsimd(q):
+            for u in range(2):
+                columns = slice(u * BANK, (u + 1) * BANK)
+                nc.gpsimd.tensor_tensor(
+                    grouped[q][:, columns].rearrange("p (j t) -> p j t", t=4),
+                    saturated[q][:, columns].rearrange("p (j t) -> p j t", t=4),
+                    peak_col[:, 0, :].unsqueeze(1).to_broadcast([P, P, 4]),
+                    ALU.mult,
+                )
+
+        def piece_on_scalar(q):
             first, count = quarters(q)
-            room = "rounded%d_%d" % (q, b)
-            rounded = held([P, 4 * count], BF16, room)
-            for u, number in enumerate(banks):
-                bank = psum_bank(number)
-                first_product(bank, b, [(2 * u + d, (first + j, P), d * count + j) for d in range(2) for j in range(0, count, P)])
-                saturated = ring.tile([P, BANK], F32, name="saturated")
-                nc.scalar.activation(saturated[:], bank[:], ACT.Tanh)
+            rounded = held([P, PIECE], BF16, "rounded%d" % q)
+            for u in range(2):
+                bank = psum_bank(2 + u)
+                first_product(bank, 1, [(2 * u + d, (first + j, P), d * count + j) for d in range(2) for j in range(0, count, P)], (0, 1) if q == 0 else (1, 0))
+                values = saturated[q][:, PIECE + u * BANK : PIECE + (u + 1) * BANK]
+                nc.scalar.activation(values, bank[:], ACT.Tanh)
                 for d in range(2):
                     t = 2 * u + d
                     nc.scalar.activation(
-                        rounded[:, t * count : (t + 1) * count], saturated[:, d * count : (d + 1) * count], ACT.Copy, scale=peak_col[b][:, t : t + 1]
+                        rounded[:, t * count : (t + 1) * count], values[:, d * count : (d + 1) * count], ACT.Copy, scale=peak_col[:, 1, t : t + 1]
                     )
             nc.scalar.copy(
-                grouped[q][:, b, :].rearrange("p (c i t) -> p c t i", i=4, t=4),
+                grouped[q][:, PIECE : 2 * PIECE].rearrange("p (c i t) -> p c t i", i=4, t=4),
                 rounded[:].rearrange("p (t c i) -> p c t i", i=4, t=4),
             )
-            if b == 1:
-                quantize_h(q)
-            return room
 
-        w2_w = held([P, 2 * N], U32, "w2_w")
-        w2_s = held([P, 2 * N], U8, "w2_s")
+        def round_w2(half):
+            nc.gpsimd.tensor_scalar(
+                grouped[half][:, 2 * PIECE : 3 * PIECE].rearrange("p (n t) -> p n t", t=4),
+                w2_raw[half, 0][:].rearrange("p t n -> p n t"),
+                1.0,
+                0.0,
+                ALU.mult,
+                ALU.add,
+            )
+            nc.scalar.copy(
+                grouped[half][:, 3 * PIECE : 4 * PIECE].rearrange("p (c i t) -> p c t i", i=4, t=4),
+                w2_raw[half, 1][:].rearrange("p t (c i) -> p c t i", i=4),
+            )
 
-        def quantize_w2():
-            w2_grouped = held([P, 2, N * 4], BF16, "w2_grouped")
-            for b, copy in enumerate((nc.scalar.copy, nc.vector.tensor_copy)):
-                copy(
-                    w2_grouped[:, b, :].rearrange("p (c i t) -> p c t i", i=4, t=4),
-                    w2_raw[:, b, :, :].rearrange("p t (c i) -> p c t i", i=4),
+        def round_w2_on_vector(half):
+            for b in range(2):
+                nc.vector.tensor_copy(
+                    grouped[half][:, (2 + b) * PIECE : (3 + b) * PIECE].rearrange("p (c i t) -> p c t i", i=4, t=4),
+                    w2_raw[half, b][:].rearrange("p t (c i) -> p c t i", i=4),
                 )
-            nc.vector.quantize_mx(out=w2_w[:].bitcast(FP8X4), scales=w2_s[:], in_=w2_grouped[:].rearrange("p b c -> p (b c)"))
 
-        def replace_columns(room, *jobs):
-            driven = held([P, QUARTER * sum(job[2] for job in jobs)], F32, "driven", room)
-            filled = 0
-            for m, first_q, count, number in jobs:
-                bank = psum_bank(number)
-                for u in range(count):
-                    for b in range(2):
-                        nc.tensor.matmul_mx(
-                            out=bank[:, u * QUARTER : (u + 1) * QUARTER],
-                            lhsT=w2_w[:, b * N + m * P : b * N + (m + 1) * P].bitcast(FP8X4),
-                            lhsT_scale=w2_s[:, b * N + m * P : b * N + (m + 1) * P],
-                            rhs=h_w[first_q + u][:, b * QUARTER : (b + 1) * QUARTER].bitcast(FP8X4),
-                            rhs_scale=h_s[first_q + u][:, b * QUARTER : (b + 1) * QUARTER],
-                            start=(b == 0),
-                            stop=(b == 1),
-                        )
-                part = quarters(first_q, count)
-                values = driven[:, filled : filled + part[1]]
-                filled = filled + part[1]
-                nc.scalar.activation(values, bank[:, 0 : part[1]], ACT.Identity, bias=drive_col[:, m : m + 1])
-                nc.vector.tensor_tensor(listed(g_tile[m][:], part), decayed[m][:, columns_of(part)], values, ALU.add)
-                finished = first_q + count == 4
-                if finished and m < 3:
-                    nc.sync.dma_start(out[P * m : P * (m + 1), :], g_tile[m][:])
-                elif finished:
-                    for half, queue in enumerate((nc.sync, nc.scalar)):
-                        columns = slice(half * T // 2, (half + 1) * T // 2)
-                        queue.dma_start(out[P * m : P * (m + 1), columns], g_tile[m][:, columns])
+        def decay_on_gpsimd(m, part, room=None):
+            new = held([P, part[1]], F32, "new%d_%d" % (m, part[0]), room)
+            nc.gpsimd.tensor_scalar(new[:], picked[m][:, columns_of(part)], leak[:, m : m + 1], leak[:, 4 + m : 5 + m], ALU.mult, ALU.add)
+            return new
 
+        def second_product(m, part, number, room=None):
+            bank = psum_bank(number)
+            for u in range(part[1] // QUARTER):
+                q = part[0] // QUARTER + u
+                for b in range(2):
+                    w2_col = (2 + b) * QUARTER + (m % 2) * P
+                    nc.tensor.matmul_mx(
+                        out=bank[:, u * QUARTER : (u + 1) * QUARTER],
+                        lhsT=words[m // 2][:, w2_col : w2_col + P].bitcast(FP8X4),
+                        lhsT_scale=scales[m // 2][:, w2_col : w2_col + P],
+                        rhs=words[q][:, b * QUARTER : (b + 1) * QUARTER].bitcast(FP8X4),
+                        rhs_scale=scales[q][:, b * QUARTER : (b + 1) * QUARTER],
+                        start=(b == 0),
+                        stop=(b == 1),
+                    )
+            y = held([P, part[1]], F32, "y%d_%d" % (m, part[0]), room)
+            nc.scalar.copy(y[:], bank[:, 0 : part[1]])
+            return y
+
+        def replace_with_gpsimd(m, part, new, y):
+            nc.gpsimd.tensor_tensor(new[:], new[:], y[:], ALU.add)
+            nc.vector.tensor_copy(listed(g_tile[m][:], part), new[:])
+
+        def replace_fused(m, part, y):
+            start = rest_at[m] + part[0] - rest_from[m]
+            nc.vector.tensor_tensor(listed(g_tile[m][:], part), rest[:, start : start + part[1]], y[:], ALU.add)
+            finished = part[0] + part[1] == S
+            if finished and m < 3:
+                nc.sync.dma_start(out[P * m : P * (m + 1), :], g_tile[m][:])
+            elif finished:
+                for half, queue in enumerate((nc.sync, nc.scalar)):
+                    columns = slice(half * T // 2, (half + 1) * T // 2)
+                    queue.dma_start(out[P * m : P * (m + 1), columns], g_tile[m][:, columns])
+
+        open_round(0)
+        saturated[0] = held([P, 2 * PIECE], F32, "saturated0")
+        tanh_side_by_side(0)
+        turned = psum_bank(0)
+        for block in range(2):
+            nc.tensor.transpose(turned[:, block * P : (block + 1) * P], rows[:, (2 + block) * P : (3 + block) * P], identity[:])
         gather_g(0)
-        grouped[0] = placed.tile([P, 2, QUARTER * 4], BF16, name="grouped0", align_bytes=64, offset=SHARED_AT - 2 * S)
-        load_g(2, placed.tile([P, T], F32, name="g_tile2", align_bytes=64, offset=SHARED_AT + 2 * S))
-        make_h_with_vector(0, 2, banks=(0, 1, 2, 3))
-        load_g(3, held([P, T], F32, "g_tile3", "rate0"))
-        turned = psum_bank(3)
-        nc.tensor.transpose(turned[:, 0:P], rows[:, 2 * P : 3 * P], identity[:])
-        drive_col = held([P, 4], F32, "drive_col")
-        nc.scalar.copy(drive_col[:], turned[:, 0:4])
-        make_h_with_vector(1, 1, banks=(4, 5))
-        quantize_w2()
-        gather_g(1)
-        gather_g(2, room="w2_grouped")
-        room = make_h_with_scalar(1, 1, banks=(6, 7))
-        gather_g(3, room="grouped1")
-        replace_columns(room, (0, 0, 1, 4))
-        room = make_h_with_scalar(2, 0, banks=(0, 1))
-        replace_columns(room, (1, 0, 2, 0), (2, 0, 2, 1))
-        room = make_h_with_scalar(2, 1, banks=(2, 3))
-        replace_columns(room, (3, 0, 2, 2))
-        room = make_h_with_scalar(3, 0, banks=(4, 5))
-        replace_columns(room, (0, 1, 2, 3))
-        room = make_h_with_scalar(3, 1, banks=(6, 7))
-        replace_columns(room, (1, 2, 1, 4), (0, 3, 1, 0), (1, 3, 1, 1), (2, 2, 2, 2), (3, 2, 2, 3))
+        piece_on_gpsimd(0)
+        piece_on_scalar(0)
+        leak = held([P, 8], F32, "leak")
+        nc.scalar.copy(leak[:].rearrange("p (block c) -> p block c", block=2), turned[:, 0 : 2 * P].rearrange("p (block c) -> p block c", block=2)[:, :, 0:4])
+        new00 = decay_on_gpsimd(0, quarters(0))
+        round_w2_on_vector(0)
+        quantize(0)
+        gather_g(1, "grouped0")
+        saturated[1] = held([P, 2 * PIECE], F32, "saturated1", W2_AT[0])
+        tanh_side_by_side(1)
+        y00 = second_product(0, quarters(0), 4)
+        y10 = second_product(1, quarters(0), 5)
+        replace_with_gpsimd(0, quarters(0), new00, y00)
+        gather_g(2)
+        new10 = decay_on_gpsimd(1, quarters(0))
+        replace_with_gpsimd(1, quarters(0), new10, y10)
+        open_round(1, "y1_0")
+        piece_on_gpsimd(1)
+        piece_on_scalar(1)
+        round_w2(1)
+        quantize(1)
+        gather_g(3, "y1_0")
+        new20 = decay_on_gpsimd(2, quarters(0, 2), W2_AT[2])
+        new11 = decay_on_gpsimd(1, quarters(1), W2_AT[0])
+        saturated[2] = held([P, 2 * PIECE], F32, "saturated2", W2_AT[3])
+        tanh_side_by_side(2)
+        y11 = second_product(1, quarters(1), 6)
+        y20 = second_product(2, quarters(0, 2), 7)
+        replace_with_gpsimd(1, quarters(1), new11, y11)
+        replace_with_gpsimd(2, quarters(0, 2), new20, y20)
+        open_round(2, "y2_0")
+        piece_on_gpsimd(2)
+        piece_on_scalar(2)
+        quantize(2)
+        new30 = decay_on_gpsimd(3, quarters(0, 2), W2_AT[3])
+        y30 = second_product(3, quarters(0, 2), 4, "rounded2")
+        replace_with_gpsimd(3, quarters(0, 2), new30, y30)
+        rest_from = (QUARTER, 2 * QUARTER, 2 * QUARTER, 2 * QUARTER)
+        rest_at = (0, 3 * QUARTER, 5 * QUARTER, 7 * QUARTER)
+        rest = held([P, 9 * QUARTER], F32, "rest", "y1_256")
+
+        def decay_on_scalar(m):
+            nc.scalar.activation(
+                rest[:, rest_at[m] : rest_at[m] + S - rest_from[m]],
+                picked[m][:, rest_from[m] : S],
+                ACT.Identity,
+                bias=leak[:, 4 + m : 5 + m],
+                scale=leak[:, m : m + 1],
+            )
+
+        decay_on_scalar(0)
+        decay_on_scalar(1)
+        saturated[3] = held([P, 2 * PIECE], F32, "saturated3", "rounded2")
+        tanh_side_by_side(3)
+        open_round(3, "y2_0")
+        piece_on_gpsimd(3)
+        replace_fused(0, quarters(1, 2), second_product(0, quarters(1, 2), 5))
+        piece_on_scalar(3)
+        quantize(3)
+        replace_fused(1, quarters(2), second_product(1, quarters(2), 6, "rounded3"))
+        decay_on_scalar(2)
+        decay_on_scalar(3)
+        for m, part, number in ((0, quarters(3), 7), (1, quarters(3), 4), (2, quarters(2, 2), 5), (3, quarters(2, 2), 6)):
+            replace_fused(m, part, second_product(m, part, number))

@@ -28,8 +28,7 @@ G0_AT = TABS_AT + T
 LATER_AT = G0_AT + 4 * T
 G_AT = [G0_AT] + [LATER_AT + 4 * T * m for m in range(3)]
 W2_AT = [G_AT[3] + 4 * T + 16 * HALF * i for i in range(4)]
-W4_AT = W2_AT[3] + 32 * HALF
-W4S_AT = W4_AT + 4 * H
+W4S_AT = W2_AT[3] + 36 * HALF
 TAB0_AT = W4S_AT + 2 * H
 TAB1_AT = TAB0_AT + 4 * T
 
@@ -63,12 +62,17 @@ def tile_list_place_cell_replay_kernel(tc, tab_words, tab_scales, offs, w4_words
         def columns_of(part):
             return slice(part[0], part[0] + part[1])
 
-        tab_s_room = held([P, LATER_AT - TABS_AT], U8, "tab_s", TABS_AT)
-        tab_s = tab_s_room[:, 0:T]
-        zeros = held([P, (TAB1_AT - W4S_AT + 192) // 4], F32, "zeros", W4S_AT - 64)
+        decay_col = held([P, 4], F32, "decay_col")
+        with nc.allow_non_contiguous_dma(reason="512 values, one to a partition and tile"):
+            nc.sync.dma_start(decay_col[:], decay.rearrange("(m p) -> p m", p=P))
+        w4_raw = held([P, H], I32, "w4_raw")
+        nc.sync.dma_start(w4_raw[:].rearrange("p (a c) -> p a c", a=2), w4_words.bitcast(I32).rearrange("a p c -> p a c"))
+
+        tab_s = held([P, LATER_AT - TABS_AT], U8, "tab_s", TABS_AT)[:, 0:T]
+        zeros = held([P, (TAB1_AT - W4S_AT + 128) // 4], F32, "zeros", W4S_AT)
         nc.vector.memset(zeros[:, 0:32], 0.0)
         nc.vector.memset(tab_s.bitcast(I32), 0)
-        rows = held([P, 4 * P], F32, "rows")
+        rows = held([P, 3 * P], F32, "rows")
 
         def clear_rows(first, end, source):
             nc.vector.tensor_copy(
@@ -76,23 +80,21 @@ def tile_list_place_cell_replay_kernel(tc, tab_words, tab_scales, offs, w4_words
             )
 
         clear_rows(0, 2 * P, zeros[:, 0:32])
-        w4_s_raw = held([P, 2 * H], U8, "w4_s_raw", W4S_AT)
-        nc.vector.memset(w4_s_raw[:].bitcast(I32), 0)
+        w4_s_raw = held([P, TAB0_AT - LATER_AT], U8, "w4_s_raw", LATER_AT)[:, W4S_AT - LATER_AT :]
+        nc.vector.memset(w4_s_raw.bitcast(I32), 0)
         zeros_again = held([P, 32], F32, "zeros_again", TAB1_AT)
         nc.vector.memset(zeros_again[:], 0.0)
-        clear_rows(2 * P, 3 * P, zeros_again[:])
+        clear_rows(2 * P + P // 2, 3 * P, zeros_again[:])
         zero_col = held([P, 1], F32, "zero_col")
         nc.gpsimd.memset(zero_col[:], 0.0)
-        nc.scalar.activation(rows[:, 3 * P : 4 * P], zero_col[:].to_broadcast([P, P]), ACT.Tanh)
+        nc.scalar.activation(rows[:, 2 * P : 2 * P + P // 2], zero_col[:].to_broadcast([P, P // 2]), ACT.Tanh)
         early, late = quarters(0), quarters(1, 3)
         moved_s = held([P, S], U8, "moved_s")
         nc.gpsimd.memset(moved_s[:].bitcast(I32), 0)
         tab_w = [held([P, T], I32, "tab_w0", TAB0_AT)[:], held([P, T], I32, "tab_w1", TAB1_AT)[:]]
-        w4_raw = held([P, (W4S_AT - LATER_AT) // 4], I32, "w4_raw", LATER_AT)[:, (W4_AT - LATER_AT) // 4 :]
         for q in range(4):
             nc.sync.dma_start(tab_s[32 * q : 32 * q + 8, :].bitcast(I32), tab_scales[:, 4 * q : 4 * q + 4, :].bitcast(I32))
         nc.sync.dma_start(tab_w[0], tab_words[0].rearrange("p t i -> p (t i)").bitcast(I32))
-        nc.sync.dma_start(w4_raw.rearrange("p (a c) -> p a c", a=2), w4_words.bitcast(I32).rearrange("a p c -> p a c"))
         for q in range(4):
             nc.sync.dma_start(
                 w4_s_raw[32 * q : 32 * q + 4, :].bitcast(I32).rearrange("p (a c) -> p a c", a=2),
@@ -103,8 +105,10 @@ def tile_list_place_cell_replay_kernel(tc, tab_words, tab_scales, offs, w4_words
         identity = held([P, P], F32, "identity")
         make_identity(nc, identity[:])
         nc.gpsimd.dma_start(rows[0:4, 0 : 2 * P].rearrange("t (bg e) -> t bg e", e=8), peak.rearrange("(bg t e) -> t bg e", t=4, e=8))
-        nc.gpsimd.dma_start(rows[0:4, 2 * P : 3 * P], decay.rearrange("(m p) -> m p", p=P))
-        nc.gpsimd.dma_start(rows[0:4, 3 * P : 4 * P], drive.rearrange("(m p) -> m p", p=P))
+        nc.gpsimd.dma_start(rows[0:4, 2 * P : 3 * P], drive.rearrange("(m p) -> m p", p=P))
+        decay_wide = [held([P, S], F32, "decay_wide%d" % m) for m in range(4)]
+        for m in range(4):
+            nc.scalar.copy(decay_wide[m][:], decay_col[:, m : m + 1].to_broadcast([P, S]))
         turned = psum_bank(7)
         for block in range(2):
             nc.tensor.transpose(turned[:, block * P : (block + 1) * P], rows[:, block * P : (block + 1) * P], identity[:])
@@ -132,12 +136,12 @@ def tile_list_place_cell_replay_kernel(tc, tab_words, tab_scales, offs, w4_words
         w4_w = held([P, H], I32, "w4_w")
         nc.vector.tensor_copy(
             w4_w[:].rearrange("p (ab t g w) -> p ab t g w", t=4, g=16, w=4),
-            w4_raw.rearrange("p (ab g t w) -> p ab t g w", t=4, g=16, w=4),
+            w4_raw[:].rearrange("p (ab g t w) -> p ab t g w", t=4, g=16, w=4),
         )
         w4_s = held([P, 2 * H], U8, "w4_s")
         nc.vector.tensor_copy(
             w4_s[:].bitcast(I32).rearrange("p (ab t g w) -> p ab t g w", t=4, g=16, w=2),
-            w4_s_raw[:].bitcast(I32).rearrange("p (ab g t w) -> p ab t g w", t=4, g=16, w=2),
+            w4_s_raw.bitcast(I32).rearrange("p (ab g t w) -> p ab t g w", t=4, g=16, w=2),
         )
         w4_bytes = w4_w[:].bitcast(U8)
         v_w0.append(held([P, S // 2], U32, "v_w0_1", W4S_AT))
@@ -155,17 +159,17 @@ def tile_list_place_cell_replay_kernel(tc, tab_words, tab_scales, offs, w4_words
                 for t in range(4):
                     nc.sync.dma_start(w2_raw[half, b][:, t, :], w2_rows[b, t][:, :, half * HALF : (half + 1) * HALF])
 
-        load_w2(0, (W2_AT[0], W2_AT[1]))
         load_g(1, G_AT[1])
+        load_w2(0, (W2_AT[0], W2_AT[1]))
         load_g(2, G_AT[2])
-        load_w2(1, (W2_AT[2], W2_AT[3]))
         load_g(3, G_AT[3])
+        load_w2(1, (W2_AT[2], W2_AT[3]))
 
         picked = {}
 
         def gather_g(m, room=None):
             picked[m] = held([P, S], F32, "picked%d" % m, room)
-            nc.vector.tensor_copy(picked[m][:], listed(g_tile[m][:], (0, S)))
+            nc.vector.tensor_tensor(picked[m][:], listed(g_tile[m][:], (0, S)), decay_wide[m][:], ALU.mult)
 
         def first_product(bank, b, spans, order=(1, 0)):
             steps = [(a,) + span for a in order for span in spans]
@@ -182,107 +186,87 @@ def tile_list_place_cell_replay_kernel(tc, tab_words, tab_scales, offs, w4_words
                 )
 
         PIECE = 4 * QUARTER
-        grouped, words, scales, saturated = {}, {}, {}, {}
+        grouped, words, scales = {}, {}, {}
 
-        def open_round(q, room=None):
+        def open_round(q, room=None, words_room=None):
             pieces = 4 if q < 2 else 2
             grouped[q] = held([P, pieces * PIECE], BF16, "grouped%d" % q, room)
-            words[q] = held([P, pieces * QUARTER], U32, "words%d" % q)
+            words[q] = held([P, pieces * QUARTER], U32, "words%d" % q, words_room)
             scales[q] = held([P, pieces * QUARTER], U8, "scales%d" % q)
 
         def quantize(q):
             nc.vector.quantize_mx(out=words[q][:].bitcast(FP8X4), scales=scales[q][:], in_=grouped[q][:])
 
-        def tanh_side_by_side(q):
-            for u in range(2):
-                bank = psum_bank(u)
-                first_product(bank, 0, [(t, (q * QUARTER + u * P, P), t * P) for t in range(4)], (0, 1) if q == 0 else (1, 0))
-                nc.scalar.activation(
-                    saturated[q][:, u * BANK : (u + 1) * BANK].rearrange("p (j t) -> p j t", t=4),
-                    bank[:].rearrange("p (t j) -> p j t", t=4),
-                    ACT.Tanh,
-                )
+        def piece_with_vector(q, passes, banks):
+            rate = held([P, passes, PIECE], F32, "rate%d" % q)
+            for b in range(passes):
+                for u in range(2):
+                    bank = psum_bank(banks[2 * b + u])
+                    first_product(bank, b, [(t, (q * QUARTER + u * P, P), t * P) for t in range(4)], (0, 1) if q == 0 else (1, 0))
+                    nc.scalar.activation(
+                        rate[:, b, u * BANK : (u + 1) * BANK].rearrange("p (j t) -> p j t", t=4),
+                        bank[:].rearrange("p (t j) -> p j t", t=4),
+                        ACT.Tanh,
+                    )
+            nc.vector.tensor_tensor(
+                grouped[q][:, 0 : passes * PIECE].rearrange("p (b j t) -> p b j t", b=passes, t=4),
+                rate[:].rearrange("p b (j t) -> p b j t", t=4),
+                peak_col[:, 0:passes, :].unsqueeze(2).to_broadcast([P, passes, QUARTER, 4]),
+                ALU.mult,
+            )
 
-        def piece_on_gpsimd(q):
-            for u in range(2):
-                columns = slice(u * BANK, (u + 1) * BANK)
-                nc.gpsimd.tensor_tensor(
-                    grouped[q][:, columns].rearrange("p (j t) -> p j t", t=4),
-                    saturated[q][:, columns].rearrange("p (j t) -> p j t", t=4),
-                    peak_col[:, 0, :].unsqueeze(1).to_broadcast([P, P, 4]),
-                    ALU.mult,
-                )
-
-        def piece_on_scalar(q):
+        def piece_on_scalar(q, b, banks, room=None, between=None):
             first, count = quarters(q)
-            rounded = held([P, PIECE], BF16, "rounded%d" % q)
+            rounded = held([P, PIECE], BF16, "rounded%d_%d" % (q, b))
             for u in range(2):
-                bank = psum_bank(2 + u)
-                first_product(bank, 1, [(2 * u + d, (first + j, P), d * count + j) for d in range(2) for j in range(0, count, P)], (0, 1) if q == 0 else (1, 0))
-                values = saturated[q][:, PIECE + u * BANK : PIECE + (u + 1) * BANK]
-                nc.scalar.activation(values, bank[:], ACT.Tanh)
+                bank = psum_bank(banks[u])
+                first_product(bank, b, [(2 * u + d, (first + j, P), d * count + j) for d in range(2) for j in range(0, count, P)])
+                values = held([P, BANK], F32, "saturated%d_%d_%d" % (q, b, u), room and room[u])
+                nc.scalar.activation(values[:], bank[:], ACT.Tanh)
                 for d in range(2):
                     t = 2 * u + d
                     nc.scalar.activation(
-                        rounded[:, t * count : (t + 1) * count], values[:, d * count : (d + 1) * count], ACT.Copy, scale=peak_col[:, 1, t : t + 1]
+                        rounded[:, t * count : (t + 1) * count], values[:, d * count : (d + 1) * count], ACT.Copy, scale=peak_col[:, b, t : t + 1]
                     )
+                if between and between[0] == u:
+                    between[1]("saturated%d_%d_%d" % (q, b, u))
             nc.scalar.copy(
-                grouped[q][:, PIECE : 2 * PIECE].rearrange("p (c i t) -> p c t i", i=4, t=4),
+                grouped[q][:, b * PIECE : (b + 1) * PIECE].rearrange("p (c i t) -> p c t i", i=4, t=4),
                 rounded[:].rearrange("p (t c i) -> p c t i", i=4, t=4),
             )
 
         def round_w2(half):
-            nc.gpsimd.tensor_scalar(
-                grouped[half][:, 2 * PIECE : 3 * PIECE].rearrange("p (n t) -> p n t", t=4),
-                w2_raw[half, 0][:].rearrange("p t n -> p n t"),
-                1.0,
-                0.0,
-                ALU.mult,
-                ALU.add,
-            )
-            nc.scalar.copy(
-                grouped[half][:, 3 * PIECE : 4 * PIECE].rearrange("p (c i t) -> p c t i", i=4, t=4),
-                w2_raw[half, 1][:].rearrange("p t (c i) -> p c t i", i=4),
-            )
-
-        def round_w2_on_vector(half):
+            q, first = half, 2
             for b in range(2):
-                nc.vector.tensor_copy(
-                    grouped[half][:, (2 + b) * PIECE : (3 + b) * PIECE].rearrange("p (c i t) -> p c t i", i=4, t=4),
+                (nc.vector.tensor_copy if (half, b) == (0, 0) else nc.scalar.copy)(
+                    grouped[q][:, (first + b) * PIECE : (first + b + 1) * PIECE].rearrange("p (c i t) -> p c t i", i=4, t=4),
                     w2_raw[half, b][:].rearrange("p t (c i) -> p c t i", i=4),
                 )
 
-        def decay_on_gpsimd(m, part, room=None):
-            new = held([P, part[1]], F32, "new%d_%d" % (m, part[0]), room)
-            nc.gpsimd.tensor_scalar(new[:], picked[m][:, columns_of(part)], leak[:, m : m + 1], leak[:, 4 + m : 5 + m], ALU.mult, ALU.add)
-            return new
+        driven = {}
 
         def second_product(m, part, number, room=None):
             bank = psum_bank(number)
+            w2_round, w2_first = m // 2, 2
             for u in range(part[1] // QUARTER):
                 q = part[0] // QUARTER + u
                 for b in range(2):
-                    w2_col = (2 + b) * QUARTER + (m % 2) * P
+                    w2_col = (w2_first + b) * QUARTER + (m % 2) * P
                     nc.tensor.matmul_mx(
                         out=bank[:, u * QUARTER : (u + 1) * QUARTER],
-                        lhsT=words[m // 2][:, w2_col : w2_col + P].bitcast(FP8X4),
-                        lhsT_scale=scales[m // 2][:, w2_col : w2_col + P],
+                        lhsT=words[w2_round][:, w2_col : w2_col + P].bitcast(FP8X4),
+                        lhsT_scale=scales[w2_round][:, w2_col : w2_col + P],
                         rhs=words[q][:, b * QUARTER : (b + 1) * QUARTER].bitcast(FP8X4),
                         rhs_scale=scales[q][:, b * QUARTER : (b + 1) * QUARTER],
                         start=(b == 0),
                         stop=(b == 1),
                     )
-            y = held([P, part[1]], F32, "y%d_%d" % (m, part[0]), room)
-            nc.scalar.copy(y[:], bank[:, 0 : part[1]])
-            return y
+            driven[m, part] = held([P, part[1]], F32, "y%d_%d" % (m, part[0]), room)
+            nc.scalar.activation(driven[m, part][:], bank[:, 0 : part[1]], ACT.Identity, bias=drive_col[:, m : m + 1])
 
-        def replace_with_gpsimd(m, part, new, y):
-            nc.gpsimd.tensor_tensor(new[:], new[:], y[:], ALU.add)
-            nc.vector.tensor_copy(listed(g_tile[m][:], part), new[:])
-
-        def replace_fused(m, part, y):
-            start = rest_at[m] + part[0] - rest_from[m]
-            nc.vector.tensor_tensor(listed(g_tile[m][:], part), rest[:, start : start + part[1]], y[:], ALU.add)
+        def replace(m, part, number, room=None):
+            second_product(m, part, number, room)
+            nc.vector.tensor_tensor(listed(g_tile[m][:], part), picked[m][:, columns_of(part)], driven[m, part][:], ALU.add)
             finished = part[0] + part[1] == S
             if finished and m < 3:
                 nc.sync.dma_start(out[P * m : P * (m + 1), :], g_tile[m][:])
@@ -291,74 +275,34 @@ def tile_list_place_cell_replay_kernel(tc, tab_words, tab_scales, offs, w4_words
                     columns = slice(half * T // 2, (half + 1) * T // 2)
                     queue.dma_start(out[P * m : P * (m + 1), columns], g_tile[m][:, columns])
 
-        open_round(0)
-        saturated[0] = held([P, 2 * PIECE], F32, "saturated0")
-        tanh_side_by_side(0)
-        turned = psum_bank(0)
-        for block in range(2):
-            nc.tensor.transpose(turned[:, block * P : (block + 1) * P], rows[:, (2 + block) * P : (3 + block) * P], identity[:])
+        open_round(0, None, "decay_wide2")
         gather_g(0)
-        piece_on_gpsimd(0)
-        piece_on_scalar(0)
-        leak = held([P, 8], F32, "leak")
-        nc.scalar.copy(leak[:].rearrange("p (block c) -> p block c", block=2), turned[:, 0 : 2 * P].rearrange("p (block c) -> p block c", block=2)[:, :, 0:4])
-        new00 = decay_on_gpsimd(0, quarters(0))
-        round_w2_on_vector(0)
-        quantize(0)
-        gather_g(1, "grouped0")
-        saturated[1] = held([P, 2 * PIECE], F32, "saturated1", W2_AT[0])
-        tanh_side_by_side(1)
-        y00 = second_product(0, quarters(0), 4)
-        y10 = second_product(1, quarters(0), 5)
-        replace_with_gpsimd(0, quarters(0), new00, y00)
+        piece_with_vector(0, 2, (0, 1, 2, 3))
+        gather_g(1)
+        open_round(1, None, "decay_wide3")
+        piece_with_vector(1, 1, (4, 5))
+        round_w2(0)
         gather_g(2)
-        new10 = decay_on_gpsimd(1, quarters(0))
-        replace_with_gpsimd(1, quarters(0), new10, y10)
-        open_round(1, "y1_0")
-        piece_on_gpsimd(1)
-        piece_on_scalar(1)
+        quantize(0)
+        gather_g(3, "grouped0")
+        piece_on_scalar(1, 1, (6, 7))
+        turned = psum_bank(7)
+        nc.tensor.transpose(turned[:, 0:P], rows[:, 2 * P : 3 * P], identity[:])
+        drive_col = held([P, 4], F32, "drive_col")
+        nc.scalar.copy(drive_col[:], turned[:, 0:4])
         round_w2(1)
         quantize(1)
-        gather_g(3, "y1_0")
-        new20 = decay_on_gpsimd(2, quarters(0, 2), W2_AT[2])
-        new11 = decay_on_gpsimd(1, quarters(1), W2_AT[0])
-        saturated[2] = held([P, 2 * PIECE], F32, "saturated2", W2_AT[3])
-        tanh_side_by_side(2)
-        y11 = second_product(1, quarters(1), 6)
-        y20 = second_product(2, quarters(0, 2), 7)
-        replace_with_gpsimd(1, quarters(1), new11, y11)
-        replace_with_gpsimd(2, quarters(0, 2), new20, y20)
-        open_round(2, "y2_0")
-        piece_on_gpsimd(2)
-        piece_on_scalar(2)
+        open_round(2)
+        piece_on_scalar(2, 0, (0, 1))
+        replace(0, quarters(0), 4, W2_AT[3])
+        replace(1, quarters(0), 5, W2_AT[3] + 4 * QUARTER)
+        piece_on_scalar(2, 1, (2, 3), (W2_AT[3] + 8 * QUARTER, W2_AT[2]), (1, lambda room: replace(2, quarters(0, 2), 6, W2_AT[2])))
         quantize(2)
-        new30 = decay_on_gpsimd(3, quarters(0, 2), W2_AT[3])
-        y30 = second_product(3, quarters(0, 2), 4, "rounded2")
-        replace_with_gpsimd(3, quarters(0, 2), new30, y30)
-        rest_from = (QUARTER, 2 * QUARTER, 2 * QUARTER, 2 * QUARTER)
-        rest_at = (0, 3 * QUARTER, 5 * QUARTER, 7 * QUARTER)
-        rest = held([P, 9 * QUARTER], F32, "rest", "y1_256")
-
-        def decay_on_scalar(m):
-            nc.scalar.activation(
-                rest[:, rest_at[m] : rest_at[m] + S - rest_from[m]],
-                picked[m][:, rest_from[m] : S],
-                ACT.Identity,
-                bias=leak[:, 4 + m : 5 + m],
-                scale=leak[:, m : m + 1],
-            )
-
-        decay_on_scalar(0)
-        decay_on_scalar(1)
-        saturated[3] = held([P, 2 * PIECE], F32, "saturated3", "rounded2")
-        tanh_side_by_side(3)
-        open_round(3, "y2_0")
-        piece_on_gpsimd(3)
-        replace_fused(0, quarters(1, 2), second_product(0, quarters(1, 2), 5))
-        piece_on_scalar(3)
+        replace(3, quarters(0, 2), 7, "rounded2_1")
+        open_round(3)
+        piece_on_scalar(3, 0, (2, 3))
+        piece_on_scalar(3, 1, (2, 3), None, (0, lambda room: replace(0, quarters(1, 2), 4, room)))
         quantize(3)
-        replace_fused(1, quarters(2), second_product(1, quarters(2), 6, "rounded3"))
-        decay_on_scalar(2)
-        decay_on_scalar(3)
-        for m, part, number in ((0, quarters(3), 7), (1, quarters(3), 4), (2, quarters(2, 2), 5), (3, quarters(2, 2), 6)):
-            replace_fused(m, part, second_product(m, part, number))
+        replace(1, quarters(1, 2), 5, "rounded3_1")
+        for m, part, number in ((0, quarters(3), 6), (1, quarters(3), 7), (2, quarters(2, 2), 0), (3, quarters(2, 2), 1)):
+            replace(m, part, number)

@@ -238,7 +238,7 @@ def tile_list_place_cell_replay_kernel(tc, tab_words, tab_scales, offs, w4_words
         def round_w2(half):
             q, first = half, 2
             for b in range(2):
-                (nc.vector.tensor_copy if (half, b) == (0, 0) else nc.scalar.copy)(
+                (nc.vector.tensor_copy if half == 0 else nc.scalar.copy)(
                     grouped[q][:, (first + b) * PIECE : (first + b + 1) * PIECE].rearrange("p (c i t) -> p c t i", i=4, t=4),
                     w2_raw[half, b][:].rearrange("p t (c i) -> p c t i", i=4),
                 )
@@ -280,12 +280,11 @@ def tile_list_place_cell_replay_kernel(tc, tab_words, tab_scales, offs, w4_words
         piece_with_vector(0, 2, (0, 1, 2, 3))
         gather_g(1)
         open_round(1, None, "decay_wide3")
-        piece_with_vector(1, 1, (4, 5))
+        piece_with_vector(1, 2, (4, 5, 6, 7))
         round_w2(0)
         gather_g(2)
         quantize(0)
         gather_g(3, "grouped0")
-        piece_on_scalar(1, 1, (6, 7))
         turned = psum_bank(7)
         nc.tensor.transpose(turned[:, 0:P], rows[:, 2 * P : 3 * P], identity[:])
         drive_col = held([P, 4], F32, "drive_col")
@@ -299,10 +298,11 @@ def tile_list_place_cell_replay_kernel(tc, tab_words, tab_scales, offs, w4_words
         piece_on_scalar(2, 1, (2, 3), (W2_AT[3] + 8 * QUARTER, W2_AT[2]), (1, lambda room: replace(2, quarters(0, 2), 6, W2_AT[2])))
         quantize(2)
         replace(3, quarters(0, 2), 7, "rounded2_1")
+        replace(1, quarters(1), 7)
         open_round(3)
         piece_on_scalar(3, 0, (2, 3))
         piece_on_scalar(3, 1, (2, 3), None, (0, lambda room: replace(0, quarters(1, 2), 4, room)))
         quantize(3)
-        replace(1, quarters(1, 2), 5, "rounded3_1")
+        replace(1, quarters(2), 5, "rounded3_1")
         for m, part, number in ((0, quarters(3), 6), (1, quarters(3), 7), (2, quarters(2, 2), 0), (3, quarters(2, 2), 1)):
             replace(m, part, number)

@@ -23,14 +23,18 @@ BANK = 512
 GROUP = 16
 QUARTER = S // 4
 HALF = N // 2
-TABS_AT = 0
-G0_AT = TABS_AT + T
-LATER_AT = G0_AT + 4 * T
-G_AT = [G0_AT] + [LATER_AT + 4 * T * m for m in range(3)]
-W2_AT = [G_AT[3] + 4 * T + 16 * HALF * i for i in range(4)]
-W4S_AT = W2_AT[3] + 36 * HALF
-TAB0_AT = W4S_AT + 2 * H
-TAB1_AT = TAB0_AT + 4 * T
+TAB0_AT = 0
+G0_AT = TAB0_AT + QUARTER
+TABS_AT = G0_AT + 4 * T
+G1_AT = TABS_AT + T
+W2_AT = [G1_AT + 4 * T + 16 * HALF * i for i in range(4)]
+G2_AT = W2_AT[3] + 16 * HALF
+G3_AT = G2_AT + 4 * T
+W4_AT = G3_AT + 4 * T
+W4S_AT = W4_AT + 4 * H
+TAB1_AT = W4S_AT + 2 * H
+ROUNDED_AT = TAB1_AT + 4 * T
+G_AT = [G0_AT, G1_AT, G2_AT, G3_AT]
 
 
 def quarters(first, count=1):
@@ -62,39 +66,33 @@ def tile_list_place_cell_replay_kernel(tc, tab_words, tab_scales, offs, w4_words
         def columns_of(part):
             return slice(part[0], part[0] + part[1])
 
-        decay_col = held([P, 4], F32, "decay_col")
-        with nc.allow_non_contiguous_dma(reason="512 values, one to a partition and tile"):
-            nc.sync.dma_start(decay_col[:], decay.rearrange("(m p) -> p m", p=P))
-        w4_raw = held([P, H], I32, "w4_raw")
-        nc.sync.dma_start(w4_raw[:].rearrange("p (a c) -> p a c", a=2), w4_words.bitcast(I32).rearrange("a p c -> p a c"))
+        tab_w = [held([P, T], I32, "tab_w0", TAB0_AT)[:]]
+        nc.sync.dma_start(tab_w[0], tab_words[0].rearrange("p t i -> p (t i)").bitcast(I32))
 
-        tab_s = held([P, LATER_AT - TABS_AT], U8, "tab_s", TABS_AT)[:, 0:T]
-        zeros = held([P, (TAB1_AT - W4S_AT + 128) // 4], F32, "zeros", W4S_AT)
-        nc.vector.memset(zeros[:, 0:32], 0.0)
-        nc.vector.memset(tab_s.bitcast(I32), 0)
         rows = held([P, 3 * P], F32, "rows")
-
-        def clear_rows(first, end, source):
-            nc.vector.tensor_copy(
-                rows[:, first:end].rearrange("p (r c) -> p r c", c=32), source.unsqueeze(1).to_broadcast([P, (end - first) // 32, 32])
-            )
-
-        clear_rows(0, 2 * P, zeros[:, 0:32])
-        w4_s_raw = held([P, TAB0_AT - LATER_AT], U8, "w4_s_raw", LATER_AT)[:, W4S_AT - LATER_AT :]
+        nc.gpsimd.memset(rows[:, 0 : 2 * P], 0.0)
+        zeros = held([P, (TAB1_AT - W4S_AT + 192) // 4], F32, "zeros", W4S_AT - 64)
+        nc.vector.memset(zeros[:, 0:32], 0.0)
+        tab_s = held([P, W4_AT - TABS_AT], U8, "tab_s", TABS_AT)[:, 0:T]
+        nc.vector.memset(tab_s.bitcast(I32), 0)
+        nc.vector.tensor_copy(rows[:, 3 * P - 64 : 3 * P - 32], zeros[:, 0:32])
+        w4_s_raw = held([P, 2 * H], U8, "w4_s_raw", W4S_AT)[:]
         nc.vector.memset(w4_s_raw.bitcast(I32), 0)
         zeros_again = held([P, 32], F32, "zeros_again", TAB1_AT)
         nc.vector.memset(zeros_again[:], 0.0)
-        clear_rows(2 * P + P // 2, 3 * P, zeros_again[:])
+        nc.vector.tensor_copy(rows[:, 3 * P - 32 : 3 * P], zeros_again[:])
         zero_col = held([P, 1], F32, "zero_col")
         nc.gpsimd.memset(zero_col[:], 0.0)
         nc.scalar.activation(rows[:, 2 * P : 2 * P + P // 2], zero_col[:].to_broadcast([P, P // 2]), ACT.Tanh)
         early, late = quarters(0), quarters(1, 3)
-        moved_s = held([P, S], U8, "moved_s")
-        nc.gpsimd.memset(moved_s[:].bitcast(I32), 0)
-        tab_w = [held([P, T], I32, "tab_w0", TAB0_AT)[:], held([P, T], I32, "tab_w1", TAB1_AT)[:]]
+        moved_s = {part: held([P, part[1]], U8, "moved_s%d" % part[0]) for part in (early, late)}
+        for part in (early, late):
+            nc.vector.memset(moved_s[part][:].bitcast(I32), 0)
+        tab_w.append(held([P, T], I32, "tab_w1", TAB1_AT)[:])
         for q in range(4):
             nc.sync.dma_start(tab_s[32 * q : 32 * q + 8, :].bitcast(I32), tab_scales[:, 4 * q : 4 * q + 4, :].bitcast(I32))
-        nc.sync.dma_start(tab_w[0], tab_words[0].rearrange("p t i -> p (t i)").bitcast(I32))
+        w4_raw = held([P, H], I32, "w4_raw", W4_AT)
+        nc.sync.dma_start(w4_raw[:].rearrange("p (a c) -> p a c", a=2), w4_words.bitcast(I32).rearrange("a p c -> p a c"))
         for q in range(4):
             nc.sync.dma_start(
                 w4_s_raw[32 * q : 32 * q + 4, :].bitcast(I32).rearrange("p (a c) -> p a c", a=2),
@@ -102,18 +100,22 @@ def tile_list_place_cell_replay_kernel(tc, tab_words, tab_scales, offs, w4_words
             )
         nc.sync.dma_start(tab_w[1], tab_words[1].rearrange("p t i -> p (t i)").bitcast(I32))
 
+        nc.gpsimd.dma_start(rows[4:8, 0:P], decay.rearrange("(m p) -> m p", p=P))
+        nc.gpsimd.dma_start(rows[0:4, 0 : 2 * P].rearrange("t (bg e) -> t bg e", e=8), peak.rearrange("(bg t e) -> t bg e", t=4, e=8))
         identity = held([P, P], F32, "identity")
         make_identity(nc, identity[:])
-        nc.gpsimd.dma_start(rows[0:4, 0 : 2 * P].rearrange("t (bg e) -> t bg e", e=8), peak.rearrange("(bg t e) -> t bg e", t=4, e=8))
         nc.gpsimd.dma_start(rows[0:4, 2 * P : 3 * P], drive.rearrange("(m p) -> m p", p=P))
-        decay_wide = [held([P, S], F32, "decay_wide%d" % m) for m in range(4)]
-        for m in range(4):
-            nc.scalar.copy(decay_wide[m][:], decay_col[:, m : m + 1].to_broadcast([P, S]))
         turned = psum_bank(7)
         for block in range(2):
             nc.tensor.transpose(turned[:, block * P : (block + 1) * P], rows[:, block * P : (block + 1) * P], identity[:])
-        peak_col = held([P, 2, 4], F32, "peak_col")
-        nc.scalar.copy(peak_col[:], turned[:, 0 : 2 * P].rearrange("p (block c) -> p block c", block=2)[:, :, 0:4])
+        per_partition = held([P, 2, 8], F32, "per_partition")
+        nc.scalar.copy(per_partition[:], turned[:, 0 : 2 * P].rearrange("p (block c) -> p block c", block=2)[:, :, 0:8])
+        peak_col = per_partition[:, :, 0:4]
+        decay_col = per_partition[:, 0, 4:8]
+        widths = (S, S, S // 2, S // 2)
+        decay_wide = [held([P, widths[m]], F32, "decay_wide%d" % m) for m in range(4)]
+        for m in range(4):
+            nc.scalar.copy(decay_wide[m][:], decay_col[:, m : m + 1].to_broadcast([P, widths[m]]))
 
         g_tile = {}
 
@@ -121,11 +123,16 @@ def tile_list_place_cell_replay_kernel(tc, tab_words, tab_scales, offs, w4_words
             g_tile[m] = held([P, T], F32, "g_tile%d" % m, room)
             nc.sync.dma_start(g_tile[m][:], gT[P * m : P * (m + 1), :])
 
-        gathered_s = held([P, S], U8, "gathered_s")
-        nc.vector.tensor_copy(gathered_s[:], listed(tab_s, (0, S)))
-        nc.sync.dma_start(moved_s[0:112, :].bitcast(I32), gathered_s[4:116, :].bitcast(I32))
-        v_w0 = [held([P, S // 2], U32, "v_w0_0")]
-        nc.vector.tensor_copy(v_w0[0][:], listed(tab_w[0].bitcast(U32), quarters(0, 2)))
+        v_w0 = held([P, S], U32, "v_w0")
+        nc.vector.tensor_copy(v_w0[:], listed(tab_w[0].bitcast(U32), (0, S)))
+        gathered_s = {}
+
+        def gather_scales(part, room, queue):
+            gathered_s[part] = held([P, part[1]], U8, "gathered_s%d" % part[0], room)
+            nc.vector.tensor_copy(gathered_s[part][:], listed(tab_s, part))
+            queue.dma_start(moved_s[part][0:112, :].bitcast(I32), gathered_s[part][4:116, :].bitcast(I32))
+
+        gather_scales(early, TAB0_AT, nc.scalar)
 
         def entries_of(tiles, part):
             whole = early if part[0] < late[0] else late
@@ -144,8 +151,7 @@ def tile_list_place_cell_replay_kernel(tc, tab_words, tab_scales, offs, w4_words
             w4_s_raw.bitcast(I32).rearrange("p (ab g t w) -> p ab t g w", t=4, g=16, w=2),
         )
         w4_bytes = w4_w[:].bitcast(U8)
-        v_w0.append(held([P, S // 2], U32, "v_w0_1", W4S_AT))
-        nc.vector.tensor_copy(v_w0[1][:], listed(tab_w[0].bitcast(U32), quarters(2, 2)))
+        gather_scales(late, W4S_AT, nc.sync)
         v_w1 = {part: held([P, part[1]], U32, "v_w1_%d" % part[0]) for part in (early, late)}
         for part in (early, late):
             nc.vector.tensor_copy(v_w1[part][:], listed(tab_w[1].bitcast(U32), part))
@@ -159,17 +165,19 @@ def tile_list_place_cell_replay_kernel(tc, tab_words, tab_scales, offs, w4_words
                 for t in range(4):
                     nc.sync.dma_start(w2_raw[half, b][:, t, :], w2_rows[b, t][:, :, half * HALF : (half + 1) * HALF])
 
-        load_g(1, G_AT[1])
         load_w2(0, (W2_AT[0], W2_AT[1]))
+        load_g(1, G_AT[1])
+        load_w2(1, (W2_AT[2], W2_AT[3]))
         load_g(2, G_AT[2])
         load_g(3, G_AT[3])
-        load_w2(1, (W2_AT[2], W2_AT[3]))
 
         picked = {}
 
         def gather_g(m, room=None):
             picked[m] = held([P, S], F32, "picked%d" % m, room)
-            nc.vector.tensor_tensor(picked[m][:], listed(g_tile[m][:], (0, S)), decay_wide[m][:], ALU.mult)
+            for first in range(0, S, widths[m]):
+                part = (first, widths[m])
+                nc.vector.tensor_tensor(picked[m][:, columns_of(part)], listed(g_tile[m][:], part), decay_wide[m][:], ALU.mult)
 
         def first_product(bank, b, spans, order=(1, 0)):
             steps = [(a,) + span for a in order for span in spans]
@@ -179,8 +187,8 @@ def tile_list_place_cell_replay_kernel(tc, tab_words, tab_scales, offs, w4_words
                     out=bank[:, bank_col : bank_col + part[1]],
                     lhsT=w4_bytes[:, 2 * w4_col : 2 * (w4_col + P)].bitcast(FP4X4),
                     lhsT_scale=w4_s[:, w4_col : w4_col + P],
-                    rhs=(v_w0[part[0] // (S // 2)][:, part[0] % (S // 2) : part[0] % (S // 2) + part[1]] if a == 0 else entries_of(v_w1, part)).bitcast(FP8X4),
-                    rhs_scale=(gathered_s if a == 0 else moved_s)[:, columns_of(part)],
+                    rhs=(v_w0[:, columns_of(part)] if a == 0 else entries_of(v_w1, part)).bitcast(FP8X4),
+                    rhs_scale=entries_of(gathered_s if a == 0 else moved_s, part),
                     start=(s == 0),
                     stop=(s == len(steps) - 1),
                 )
@@ -215,9 +223,9 @@ def tile_list_place_cell_replay_kernel(tc, tab_words, tab_scales, offs, w4_words
                 ALU.mult,
             )
 
-        def piece_on_scalar(q, b, banks, room=None, between=None):
+        def piece_on_scalar(q, b, banks, room=None, between=None, rounded_room=None):
             first, count = quarters(q)
-            rounded = held([P, PIECE], BF16, "rounded%d_%d" % (q, b))
+            rounded = held([P, PIECE], BF16, "rounded%d_%d" % (q, b), rounded_room)
             for u in range(2):
                 bank = psum_bank(banks[u])
                 first_product(bank, b, [(2 * u + d, (first + j, P), d * count + j) for d in range(2) for j in range(0, count, P)])
@@ -238,7 +246,7 @@ def tile_list_place_cell_replay_kernel(tc, tab_words, tab_scales, offs, w4_words
         def round_w2(half):
             q, first = half, 2
             for b in range(2):
-                (nc.vector.tensor_copy if half == 0 else nc.scalar.copy)(
+                (nc.vector.tensor_copy if (half, b) == (0, 0) else nc.scalar.copy)(
                     grouped[q][:, (first + b) * PIECE : (first + b + 1) * PIECE].rearrange("p (c i t) -> p c t i", i=4, t=4),
                     w2_raw[half, b][:].rearrange("p t (c i) -> p c t i", i=4),
                 )
@@ -275,34 +283,35 @@ def tile_list_place_cell_replay_kernel(tc, tab_words, tab_scales, offs, w4_words
                     columns = slice(half * T // 2, (half + 1) * T // 2)
                     queue.dma_start(out[P * m : P * (m + 1), columns], g_tile[m][:, columns])
 
-        open_round(0, None, "decay_wide2")
+        open_round(0)
         gather_g(0)
         piece_with_vector(0, 2, (0, 1, 2, 3))
-        gather_g(1)
-        open_round(1, None, "decay_wide3")
-        piece_with_vector(1, 2, (4, 5, 6, 7))
+        open_round(1)
+        piece_with_vector(1, 1, (4, 5))
         round_w2(0)
-        gather_g(2)
         quantize(0)
-        gather_g(3, "grouped0")
-        turned = psum_bank(7)
+        gather_g(1, "grouped0")
+        piece_on_scalar(1, 1, (6, 7), None, None, ROUNDED_AT)
+        turned = psum_bank(6)
         nc.tensor.transpose(turned[:, 0:P], rows[:, 2 * P : 3 * P], identity[:])
         drive_col = held([P, 4], F32, "drive_col")
         nc.scalar.copy(drive_col[:], turned[:, 0:4])
+        replace(0, quarters(0), 4, ROUNDED_AT)
+        replace(1, quarters(0), 5, ROUNDED_AT + 4 * QUARTER)
         round_w2(1)
         quantize(1)
+        gather_g(2, "grouped1")
         open_round(2)
-        piece_on_scalar(2, 0, (0, 1))
-        replace(0, quarters(0), 4, W2_AT[3])
-        replace(1, quarters(0), 5, W2_AT[3] + 4 * QUARTER)
-        piece_on_scalar(2, 1, (2, 3), (W2_AT[3] + 8 * QUARTER, W2_AT[2]), (1, lambda room: replace(2, quarters(0, 2), 6, W2_AT[2])))
+        piece_on_scalar(2, 0, (0, 1), (W2_AT[3], W2_AT[3] + 4 * BANK))
+        replace(2, quarters(0, 2), 6, "rounded2_0")
+        gather_g(3)
+        piece_on_scalar(2, 1, (0, 1), None, (1, lambda room: replace(1, quarters(1), 7, room)))
         quantize(2)
-        replace(3, quarters(0, 2), 7, "rounded2_1")
-        replace(1, quarters(1), 7)
+        replace(3, quarters(0, 2), 4, "rounded2_1")
         open_round(3)
-        piece_on_scalar(3, 0, (2, 3))
-        piece_on_scalar(3, 1, (2, 3), None, (0, lambda room: replace(0, quarters(1, 2), 4, room)))
+        piece_on_scalar(3, 0, (0, 1))
+        piece_on_scalar(3, 1, (0, 1), None, (0, lambda room: replace(0, quarters(1, 2), 5, room)))
         quantize(3)
-        replace(1, quarters(2), 5, "rounded3_1")
-        for m, part, number in ((0, quarters(3), 6), (1, quarters(3), 7), (2, quarters(2, 2), 0), (3, quarters(2, 2), 1)):
+        replace(1, quarters(2), 6, "rounded3_1")
+        for m, part, number in ((0, quarters(3), 7), (1, quarters(3), 4), (2, quarters(2, 2), 2), (3, quarters(2, 2), 3)):
             replace(m, part, number)

@@ -25,15 +25,16 @@ QUARTER = S // 4
 HALF = N // 2
 TAB0_AT = 0
 G0_AT = TAB0_AT + QUARTER
-TABS_AT = G0_AT + 4 * T
+W4_AT = TAB0_AT + 4 * T
+W4S_AT = W4_AT + 4 * H
+TAB1_AT = W4S_AT + 2 * H
+TABS_AT = TAB1_AT + 4 * T
 G1_AT = TABS_AT + T
 W2_AT = [G1_AT + 4 * T + 16 * HALF * i for i in range(4)]
 G2_AT = W2_AT[3] + 16 * HALF
 G3_AT = G2_AT + 4 * T
-W4_AT = G3_AT + 4 * T
-W4S_AT = W4_AT + 4 * H
-TAB1_AT = W4S_AT + 2 * H
-ROUNDED_AT = TAB1_AT + 4 * T
+TABS_END = G3_AT + 4 * T
+ROUNDED_AT = TABS_END + 6 * QUARTER
 G_AT = [G0_AT, G1_AT, G2_AT, G3_AT]
 
 
@@ -73,7 +74,7 @@ def tile_list_place_cell_replay_kernel(tc, tab_words, tab_scales, offs, w4_words
         nc.gpsimd.memset(rows[:, 0 : 2 * P], 0.0)
         zeros = held([P, (TAB1_AT - W4S_AT + 192) // 4], F32, "zeros", W4S_AT - 64)
         nc.vector.memset(zeros[:, 0:32], 0.0)
-        tab_s = held([P, W4_AT - TABS_AT], U8, "tab_s", TABS_AT)[:, 0:T]
+        tab_s = held([P, TABS_END - TABS_AT], U8, "tab_s", TABS_AT)[:, 0:T]
         nc.vector.memset(tab_s.bitcast(I32), 0)
         nc.vector.tensor_copy(rows[:, 3 * P - 64 : 3 * P - 32], zeros[:, 0:32])
         w4_s_raw = held([P, 2 * H], U8, "w4_s_raw", W4S_AT)[:]
@@ -112,7 +113,7 @@ def tile_list_place_cell_replay_kernel(tc, tab_words, tab_scales, offs, w4_words
         nc.scalar.copy(per_partition[:], turned[:, 0 : 2 * P].rearrange("p (block c) -> p block c", block=2)[:, :, 0:8])
         peak_col = per_partition[:, :, 0:4]
         decay_col = per_partition[:, 0, 4:8]
-        widths = (S, S, S // 2, S // 2)
+        widths = (S, S, S, S)
         decay_wide = [held([P, widths[m]], F32, "decay_wide%d" % m) for m in range(4)]
         for m in range(4):
             nc.scalar.copy(decay_wide[m][:], decay_col[:, m : m + 1].to_broadcast([P, widths[m]]))
@@ -132,7 +133,7 @@ def tile_list_place_cell_replay_kernel(tc, tab_words, tab_scales, offs, w4_words
             nc.vector.tensor_copy(gathered_s[part][:], listed(tab_s, part))
             queue.dma_start(moved_s[part][0:112, :].bitcast(I32), gathered_s[part][4:116, :].bitcast(I32))
 
-        gather_scales(early, TAB0_AT, nc.scalar)
+        gather_scales(early, TAB0_AT, nc.sync)
 
         def entries_of(tiles, part):
             whole = early if part[0] < late[0] else late
@@ -197,7 +198,7 @@ def tile_list_place_cell_replay_kernel(tc, tab_words, tab_scales, offs, w4_words
         grouped, words, scales = {}, {}, {}
 
         def open_round(q, room=None, words_room=None):
-            pieces = 4 if q < 2 else 2
+            pieces = 4 if q == 0 else 2
             grouped[q] = held([P, pieces * PIECE], BF16, "grouped%d" % q, room)
             words[q] = held([P, pieces * QUARTER], U32, "words%d" % q, words_room)
             scales[q] = held([P, pieces * QUARTER], U8, "scales%d" % q)
@@ -223,30 +224,32 @@ def tile_list_place_cell_replay_kernel(tc, tab_words, tab_scales, offs, w4_words
                 ALU.mult,
             )
 
-        def piece_on_scalar(q, b, banks, room=None, between=None, rounded_room=None):
+        rounded = {}
+
+        def scale_on_scalar(q, b, u, number, room=None):
             first, count = quarters(q)
-            rounded = held([P, PIECE], BF16, "rounded%d_%d" % (q, b), rounded_room)
-            for u in range(2):
-                bank = psum_bank(banks[u])
-                first_product(bank, b, [(2 * u + d, (first + j, P), d * count + j) for d in range(2) for j in range(0, count, P)])
-                values = held([P, BANK], F32, "saturated%d_%d_%d" % (q, b, u), room and room[u])
-                nc.scalar.activation(values[:], bank[:], ACT.Tanh)
-                for d in range(2):
-                    t = 2 * u + d
-                    nc.scalar.activation(
-                        rounded[:, t * count : (t + 1) * count], values[:, d * count : (d + 1) * count], ACT.Copy, scale=peak_col[:, b, t : t + 1]
-                    )
-                if between and between[0] == u:
-                    between[1]("saturated%d_%d_%d" % (q, b, u))
+            if u == 0:
+                rounded[q, b] = held([P, PIECE], BF16, "rounded%d_%d" % (q, b))
+            bank = psum_bank(number)
+            first_product(bank, b, [(2 * u + d, (first + j, P), d * count + j) for d in range(2) for j in range(0, count, P)])
+            values = held([P, BANK], F32, "saturated%d_%d_%d" % (q, b, u), room)
+            nc.scalar.activation(values[:], bank[:], ACT.Tanh)
+            for d in range(2):
+                t = 2 * u + d
+                nc.scalar.activation(
+                    rounded[q, b][:, t * count : (t + 1) * count], values[:, d * count : (d + 1) * count], ACT.Copy, scale=peak_col[:, b, t : t + 1]
+                )
+
+        def side_by_side(q, b):
             nc.scalar.copy(
                 grouped[q][:, b * PIECE : (b + 1) * PIECE].rearrange("p (c i t) -> p c t i", i=4, t=4),
-                rounded[:].rearrange("p (t c i) -> p c t i", i=4, t=4),
+                rounded[q, b][:].rearrange("p (t c i) -> p c t i", i=4, t=4),
             )
 
         def round_w2(half):
-            q, first = half, 2
+            q, first = ((0, 2), (4, 0))[half]
             for b in range(2):
-                (nc.vector.tensor_copy if (half, b) == (0, 0) else nc.scalar.copy)(
+                (nc.vector.tensor_copy if half == 0 else nc.scalar.copy)(
                     grouped[q][:, (first + b) * PIECE : (first + b + 1) * PIECE].rearrange("p (c i t) -> p c t i", i=4, t=4),
                     w2_raw[half, b][:].rearrange("p t (c i) -> p c t i", i=4),
                 )
@@ -255,7 +258,7 @@ def tile_list_place_cell_replay_kernel(tc, tab_words, tab_scales, offs, w4_words
 
         def second_product(m, part, number, room=None):
             bank = psum_bank(number)
-            w2_round, w2_first = m // 2, 2
+            w2_round, w2_first = ((0, 2), (4, 0))[m // 2]
             for u in range(part[1] // QUARTER):
                 q = part[0] // QUARTER + u
                 for b in range(2):
@@ -286,31 +289,44 @@ def tile_list_place_cell_replay_kernel(tc, tab_words, tab_scales, offs, w4_words
         open_round(0)
         gather_g(0)
         piece_with_vector(0, 2, (0, 1, 2, 3))
-        open_round(1)
-        piece_with_vector(1, 1, (4, 5))
         round_w2(0)
+        open_round(1, W2_AT[0])
+        piece_with_vector(1, 1, (4, 5))
         quantize(0)
-        gather_g(1, "grouped0")
-        piece_on_scalar(1, 1, (6, 7), None, None, ROUNDED_AT)
+        for u in range(2):
+            scale_on_scalar(1, 1, u, 6 + u)
+        side_by_side(1, 1)
+        quantize(1)
+        gather_g(1, W2_AT[0])
         turned = psum_bank(6)
         nc.tensor.transpose(turned[:, 0:P], rows[:, 2 * P : 3 * P], identity[:])
         drive_col = held([P, 4], F32, "drive_col")
         nc.scalar.copy(drive_col[:], turned[:, 0:4])
-        replace(0, quarters(0), 4, ROUNDED_AT)
-        replace(1, quarters(0), 5, ROUNDED_AT + 4 * QUARTER)
+        scale_on_scalar(2, 0, 0, 0)
+        scale_on_scalar(2, 0, 1, 1, ROUNDED_AT)
+        replace(0, quarters(0, 2), 4, ROUNDED_AT - 6 * QUARTER)
+        replace(1, quarters(0, 2), 4)
+        open_round(4, ROUNDED_AT + 2 * QUARTER)
         round_w2(1)
-        quantize(1)
-        gather_g(2, "grouped1")
-        open_round(2)
-        piece_on_scalar(2, 0, (0, 1), (W2_AT[3], W2_AT[3] + 4 * BANK))
-        replace(2, quarters(0, 2), 6, "rounded2_0")
-        gather_g(3)
-        piece_on_scalar(2, 1, (0, 1), None, (1, lambda room: replace(1, quarters(1), 7, room)))
+        quantize(4)
+        gather_g(2, ROUNDED_AT + 2 * QUARTER)
+        open_round(2, W2_AT[3])
+        side_by_side(2, 0)
+        for u in range(2):
+            scale_on_scalar(2, 1, u, u, W2_AT[2] + u * 4 * BANK)
+        side_by_side(2, 1)
         quantize(2)
-        replace(3, quarters(0, 2), 4, "rounded2_1")
+        gather_g(3)
         open_round(3)
-        piece_on_scalar(3, 0, (0, 1))
-        piece_on_scalar(3, 1, (0, 1), None, (0, lambda room: replace(0, quarters(1, 2), 5, room)))
+        for u in range(2):
+            scale_on_scalar(3, 0, u, u)
+        replace(2, quarters(0, 2), 6, "saturated3_0_1")
+        side_by_side(3, 0)
+        replace(3, quarters(0, 2), 7, "rounded3_0")
+        for u in range(2):
+            scale_on_scalar(3, 1, u, u)
+        replace(0, quarters(2), 5, "saturated3_1_1")
+        side_by_side(3, 1)
         quantize(3)
         replace(1, quarters(2), 6, "rounded3_1")
         for m, part, number in ((0, quarters(3), 7), (1, quarters(3), 4), (2, quarters(2, 2), 2), (3, quarters(2, 2), 3)):

@@ -128,12 +128,15 @@ def tile_list_place_cell_replay_kernel(tc, tab_words, tab_scales, offs, w4_words
         nc.vector.tensor_copy(v_w0[:], listed(tab_w[0].bitcast(U32), (0, S)))
         gathered_s = {}
 
-        def gather_scales(part, room, queue):
+        def gather_scales(part, room, queue, pieces):
             gathered_s[part] = held([P, part[1]], U8, "gathered_s%d" % part[0], room)
             nc.vector.tensor_copy(gathered_s[part][:], listed(tab_s, part))
-            queue.dma_start(moved_s[part][0:112, :].bitcast(I32), gathered_s[part][4:116, :].bitcast(I32))
+            for first, count in pieces:
+                queue.dma_start(
+                    moved_s[part][first : first + count, :].bitcast(I32), gathered_s[part][first + 4 : first + 4 + count, :].bitcast(I32)
+                )
 
-        gather_scales(early, TAB0_AT, nc.sync)
+        gather_scales(early, TAB0_AT, nc.sync, ((0, 64), (64, 32), (96, 4)))
 
         def entries_of(tiles, part):
             whole = early if part[0] < late[0] else late
@@ -152,7 +155,7 @@ def tile_list_place_cell_replay_kernel(tc, tab_words, tab_scales, offs, w4_words
             w4_s_raw.bitcast(I32).rearrange("p (ab g t w) -> p ab t g w", t=4, g=16, w=2),
         )
         w4_bytes = w4_w[:].bitcast(U8)
-        gather_scales(late, W4S_AT, nc.sync)
+        gather_scales(late, W4S_AT, nc.sync, ((0, 64), (64, 32), (96, 4)))
         v_w1 = {part: held([P, part[1]], U32, "v_w1_%d" % part[0]) for part in (early, late)}
         for part in (early, late):
             nc.vector.tensor_copy(v_w1[part][:], listed(tab_w[1].bitcast(U32), part))

@@ -292,15 +292,15 @@ def tile_list_place_cell_replay_kernel(tc, tab_words, tab_scales, offs, w4_words
         open_round(0)
         gather_g(0)
         piece_with_vector(0, 2, (0, 1, 2, 3))
-        round_w2(0)
-        open_round(1, W2_AT[0])
+        open_round(1)
         piece_with_vector(1, 1, (4, 5))
+        round_w2(0)
         quantize(0)
         for u in range(2):
             scale_on_scalar(1, 1, u, 6 + u)
         side_by_side(1, 1)
         quantize(1)
-        gather_g(1, W2_AT[0])
+        gather_g(1, "grouped1")
         turned = psum_bank(6)
         nc.tensor.transpose(turned[:, 0:P], rows[:, 2 * P : 3 * P], identity[:])
         drive_col = held([P, 4], F32, "drive_col")

@@ -1,7 +1,6 @@
 from contextlib import ExitStack
 
 import concourse.mybir as mybir
-from concourse.masks import make_identity
 
 K, H, N, T, S = 1024, 1024, 512, 2048, 1024
 FLOPS = 2 * K * H * S + 2 * H * N * S
@@ -23,19 +22,15 @@ BANK = 512
 GROUP = 16
 QUARTER = S // 4
 HALF = N // 2
-TAB0_AT = 0
-G0_AT = TAB0_AT + QUARTER
-W4_AT = TAB0_AT + 4 * T
-W4S_AT = W4_AT + 4 * H
-TAB1_AT = W4S_AT + 2 * H
-TABS_AT = TAB1_AT + 4 * T
-G1_AT = TABS_AT + T
-W2_AT = [G1_AT + 4 * T + 16 * HALF * i for i in range(4)]
-G2_AT = W2_AT[3] + 16 * HALF
-G3_AT = G2_AT + 4 * T
-TABS_END = G3_AT + 4 * T
-ROUNDED_AT = TABS_END + 6 * QUARTER
-G_AT = [G0_AT, G1_AT, G2_AT, G3_AT]
+PIECE = 4 * QUARTER
+ROWS_AT = 96
+TILE = 4 * T
+G_AT = [0, 2 * TILE, 4 * TILE, 5 * TILE]
+W2_AT = [TILE, 3 * TILE]
+TABS_AT = TILE - T // 2
+TAB0_AT = 5 * TILE // 2
+TAB1_AT = 9 * TILE // 2
+W4_AT = TAB1_AT + TILE
 
 
 def quarters(first, count=1):
@@ -67,141 +62,119 @@ def tile_list_place_cell_replay_kernel(tc, tab_words, tab_scales, offs, w4_words
         def columns_of(part):
             return slice(part[0], part[0] + part[1])
 
-        tab_w = [held([P, T], I32, "tab_w0", TAB0_AT)[:]]
-        nc.sync.dma_start(tab_w[0], tab_words[0].rearrange("p t i -> p (t i)").bitcast(I32))
-
-        rows = held([P, 3 * P], F32, "rows")
-        nc.gpsimd.memset(rows[:, 0 : 2 * P], 0.0)
-        zeros = held([P, (TAB1_AT - W4S_AT + 192) // 4], F32, "zeros", W4S_AT - 64)
-        nc.vector.memset(zeros[:, 0:32], 0.0)
-        tab_s = held([P, TABS_END - TABS_AT], U8, "tab_s", TABS_AT)[:, 0:T]
-        nc.vector.memset(tab_s.bitcast(I32), 0)
-        nc.vector.tensor_copy(rows[:, 3 * P - 64 : 3 * P - 32], zeros[:, 0:32])
-        w4_s_raw = held([P, 2 * H], U8, "w4_s_raw", W4S_AT)[:]
-        nc.vector.memset(w4_s_raw.bitcast(I32), 0)
-        zeros_again = held([P, 32], F32, "zeros_again", TAB1_AT)
-        nc.vector.memset(zeros_again[:], 0.0)
-        nc.vector.tensor_copy(rows[:, 3 * P - 32 : 3 * P], zeros_again[:])
-        zero_col = held([P, 1], F32, "zero_col")
-        nc.gpsimd.memset(zero_col[:], 0.0)
-        nc.scalar.activation(rows[:, 2 * P : 2 * P + P // 2], zero_col[:].to_broadcast([P, P // 2]), ACT.Tanh)
+        whole = (0, S)
         early, late = quarters(0), quarters(1, 3)
-        moved_s = {part: held([P, part[1]], U8, "moved_s%d" % part[0]) for part in (early, late)}
-        for part in (early, late):
-            nc.vector.memset(moved_s[part][:].bitcast(I32), 0)
-        tab_w.append(held([P, T], I32, "tab_w1", TAB1_AT)[:])
-        for q in range(4):
-            nc.sync.dma_start(tab_s[32 * q : 32 * q + 8, :].bitcast(I32), tab_scales[:, 4 * q : 4 * q + 4, :].bitcast(I32))
-        w4_raw = held([P, H], I32, "w4_raw", W4_AT)
-        nc.sync.dma_start(w4_raw[:].rearrange("p (a c) -> p a c", a=2), w4_words.bitcast(I32).rearrange("a p c -> p a c"))
+
+        tab_s = held([P, T], U8, "tab_s", TABS_AT)
+        nc.sync.dma_start(tab_s[ROWS_AT:P, :].bitcast(I32), tab_scales.bitcast(I32).rearrange("a q c -> q a c"))
+        tab_w = [held([P, T], I32, "tab_w0", TAB0_AT)]
+        nc.sync.dma_start(tab_w[0][:], tab_words[0].rearrange("p t i -> p (t i)").bitcast(I32))
+
+        decay_col = held([P, 4], F32, "decay_col")
+        drive_col = held([P, 4], F32, "drive_col")
+        peak_run = held([P, 2, 8], F32, "peak_run")
+        peak_col = peak_run[:, :, 0:8:2]
+        with nc.allow_non_contiguous_dma(reason="one value a partition"):
+            nc.scalar.dma_start(decay_col[:], decay.rearrange("(m p) -> p m", p=P))
+        for d in range(2):
+            nc.gpsimd.dma_start(peak_run[d:P:2, :, 0:7], peak.rearrange("(b g e) -> g b e", b=2, e=8)[:, :, d : d + 7])
+        with nc.allow_non_contiguous_dma(reason="one value a partition"):
+            nc.gpsimd.dma_start(drive_col[:], drive.rearrange("(m p) -> p m", p=P))
+
+        zeros = held([P, 32], F32, "zeros", W4_AT - 64)
+        nc.vector.memset(zeros[:], 0.0)
+        w4_s_raw = held([P, 2 * H], U8, "w4_s_raw")
+        nc.vector.memset(w4_s_raw[:].bitcast(I32), 0)
+        zero_in = held([P, 32], F32, "zero_in")
+        nc.vector.tensor_copy(zero_in[:], zeros[:])
+        zero_bias = held([P, 32], F32, "zero_bias")
+        nc.scalar.activation(zero_bias[:], zero_in[:], ACT.Tanh)
         for q in range(4):
             nc.sync.dma_start(
                 w4_s_raw[32 * q : 32 * q + 4, :].bitcast(I32).rearrange("p (a c) -> p a c", a=2),
                 w4_scales[:, 4 * q : 4 * q + 4, :].bitcast(I32).rearrange("a r c -> r a c"),
             )
-        nc.sync.dma_start(tab_w[1], tab_words[1].rearrange("p t i -> p (t i)").bitcast(I32))
+        w4_raw = held([P, H], I32, "w4_raw", W4_AT)
+        nc.sync.dma_start(w4_raw[:].rearrange("p (a c) -> p a c", a=2), w4_words.bitcast(I32).rearrange("a p c -> p a c"))
+        tab_w.append(held([P, T], I32, "tab_w1", TAB1_AT))
+        nc.sync.dma_start(tab_w[1][:], tab_words[1].rearrange("p t i -> p (t i)").bitcast(I32))
+        nc.vector.memset(tab_s[0:ROWS_AT, :].bitcast(I32), 0)
+        planes = held([P, 2 * S], U8, "planes")
+        nc.vector.memset(planes[:].bitcast(I32), 0)
 
-        nc.gpsimd.dma_start(rows[4:8, 0:P], decay.rearrange("(m p) -> m p", p=P))
-        nc.gpsimd.dma_start(rows[0:4, 0 : 2 * P].rearrange("t (bg e) -> t bg e", e=8), peak.rearrange("(bg t e) -> t bg e", t=4, e=8))
-        identity = held([P, P], F32, "identity")
-        make_identity(nc, identity[:])
-        nc.gpsimd.dma_start(rows[0:4, 2 * P : 3 * P], drive.rearrange("(m p) -> m p", p=P))
-        turned = psum_bank(7)
-        for block in range(2):
-            nc.tensor.transpose(turned[:, block * P : (block + 1) * P], rows[:, block * P : (block + 1) * P], identity[:])
-        per_partition = held([P, 2, 8], F32, "per_partition")
-        nc.scalar.copy(per_partition[:], turned[:, 0 : 2 * P].rearrange("p (block c) -> p block c", block=2)[:, :, 0:8])
-        peak_col = per_partition[:, :, 0:4]
-        decay_col = per_partition[:, 0, 4:8]
-        widths = (S, S, S, S)
-        decay_wide = [held([P, widths[m]], F32, "decay_wide%d" % m) for m in range(4)]
-        for m in range(4):
-            nc.scalar.copy(decay_wide[m][:], decay_col[:, m : m + 1].to_broadcast([P, widths[m]]))
-
-        g_tile = {}
-
-        def load_g(m, room):
-            g_tile[m] = held([P, T], F32, "g_tile%d" % m, room)
-            nc.sync.dma_start(g_tile[m][:], gT[P * m : P * (m + 1), :])
-
+        gathered_s = held([P, S], U8, "gathered_s")
+        nc.vector.tensor_copy(gathered_s[:], listed(tab_s[:], whole))
+        for q in range(4):
+            nc.sync.dma_start(
+                planes[32 * q : 32 * q + 4, :].bitcast(I32).rearrange("p (a c) -> p a c", a=2),
+                gathered_s[ROWS_AT + 8 * q : ROWS_AT + 8 * q + 8, :].bitcast(I32),
+            )
         v_w0 = held([P, S], U32, "v_w0")
-        nc.vector.tensor_copy(v_w0[:], listed(tab_w[0].bitcast(U32), (0, S)))
-        gathered_s = {}
+        nc.vector.tensor_copy(v_w0[:], listed(tab_w[0][:].bitcast(U32), whole))
 
-        def gather_scales(part, room, queue, pieces):
-            gathered_s[part] = held([P, part[1]], U8, "gathered_s%d" % part[0], room)
-            nc.vector.tensor_copy(gathered_s[part][:], listed(tab_s, part))
-            for first, count in pieces:
-                queue.dma_start(
-                    moved_s[part][first : first + count, :].bitcast(I32), gathered_s[part][first + 4 : first + 4 + count, :].bitcast(I32)
-                )
-
-        gather_scales(early, TAB0_AT, nc.sync, ((0, 64), (64, 32), (96, 4)))
-
-        def entries_of(tiles, part):
-            whole = early if part[0] < late[0] else late
-            return tiles[whole][:, part[0] - whole[0] : part[0] - whole[0] + part[1]]
-
-        load_g(0, G_AT[0])
-
-        w4_w = held([P, H], I32, "w4_w")
-        nc.vector.tensor_copy(
-            w4_w[:].rearrange("p (ab t g w) -> p ab t g w", t=4, g=16, w=4),
-            w4_raw[:].rearrange("p (ab g t w) -> p ab t g w", t=4, g=16, w=4),
-        )
         w4_s = held([P, 2 * H], U8, "w4_s")
-        nc.vector.tensor_copy(
-            w4_s[:].bitcast(I32).rearrange("p (ab t g w) -> p ab t g w", t=4, g=16, w=2),
-            w4_s_raw.bitcast(I32).rearrange("p (ab g t w) -> p ab t g w", t=4, g=16, w=2),
+        nc.scalar.copy(
+            w4_s[:].bitcast(U16).rearrange("p (ab t g) -> p ab t g", ab=4, t=4),
+            w4_s_raw[:].bitcast(U16).rearrange("p (ab g t) -> p ab t g", ab=4, t=4),
         )
-        w4_bytes = w4_w[:].bitcast(U8)
-        gather_scales(late, W4S_AT, nc.sync, ((0, 64), (64, 32), (96, 4)))
+        w4_w = [held([P, H // 2], U32, "w4_w%d" % b) for b in range(2)]
+        for b in range(2):
+            nc.scalar.copy(
+                w4_w[b][:].rearrange("p (a t g) -> p a t g", a=2, t=4),
+                w4_raw[:].bitcast(U32).rearrange("p (a b g t) -> p b a t g", a=2, b=2, t=4)[:, b],
+            )
         v_w1 = {part: held([P, part[1]], U32, "v_w1_%d" % part[0]) for part in (early, late)}
         for part in (early, late):
-            nc.vector.tensor_copy(v_w1[part][:], listed(tab_w[1].bitcast(U32), part))
+            nc.vector.tensor_copy(v_w1[part][:], listed(tab_w[1][:].bitcast(U32), part))
 
-        w2_rows = w2.rearrange("(b g t e) n -> b t g e n", b=2, t=4, e=8)
-        w2_raw = {}
+        decay_wide = [held([P, S], F32, "decay_wide%d" % m) for m in range(4)]
+        for m in range(4):
+            nc.scalar.copy(decay_wide[m][:], decay_col[:, m : m + 1].to_broadcast([P, S]))
 
-        def load_w2(half, rooms):
+        w2_rows = w2.rearrange("(b g t d) n -> b d g t n", b=2, t=4, d=2)
+        w2_raw, g_tile = {}, {}
+
+        def load_w2(half):
+            w2_raw[half] = held([P, 2, 4, HALF], F32, "w2_raw%d" % half, W2_AT[half])
             for b in range(2):
-                w2_raw[half, b] = held([P, 4, HALF], F32, "w2_raw%d_%d" % (half, b), rooms[b])
-                for t in range(4):
-                    nc.sync.dma_start(w2_raw[half, b][:, t, :], w2_rows[b, t][:, :, half * HALF : (half + 1) * HALF])
+                for d in range(2):
+                    nc.sync.dma_start(w2_raw[half][d:P:2, b], w2_rows[b, d][:, :, half * HALF : (half + 1) * HALF])
 
-        load_w2(0, (W2_AT[0], W2_AT[1]))
-        load_g(1, G_AT[1])
-        load_w2(1, (W2_AT[2], W2_AT[3]))
-        load_g(2, G_AT[2])
-        load_g(3, G_AT[3])
+        def load_g(m):
+            g_tile[m] = held([P, T], F32, "g_tile%d" % m, G_AT[m])
+            nc.sync.dma_start(g_tile[m][:], gT[P * m : P * (m + 1), :])
 
         picked = {}
 
         def gather_g(m, room=None):
             picked[m] = held([P, S], F32, "picked%d" % m, room)
-            for first in range(0, S, widths[m]):
-                part = (first, widths[m])
-                nc.vector.tensor_tensor(picked[m][:, columns_of(part)], listed(g_tile[m][:], part), decay_wide[m][:], ALU.mult)
+            nc.vector.tensor_tensor(picked[m][:], listed(g_tile[m][:], whole), decay_wide[m][:], ALU.mult)
+
+        def moving_words(a, part):
+            if a == 0:
+                return v_w0[:, columns_of(part)]
+            home = early if part[0] < late[0] else late
+            return v_w1[home][:, part[0] - home[0] : part[0] - home[0] + part[1]]
 
         def first_product(bank, b, spans, order=(1, 0)):
             steps = [(a,) + span for a in order for span in spans]
             for s, (a, t, part, bank_col) in enumerate(steps):
+                word_col = a * PASS + t * P
                 w4_col = a * H + b * PASS + t * P
                 nc.tensor.matmul_mx(
                     out=bank[:, bank_col : bank_col + part[1]],
-                    lhsT=w4_bytes[:, 2 * w4_col : 2 * (w4_col + P)].bitcast(FP4X4),
+                    lhsT=w4_w[b][:].bitcast(U8)[:, 2 * word_col : 2 * (word_col + P)].bitcast(FP4X4),
                     lhsT_scale=w4_s[:, w4_col : w4_col + P],
-                    rhs=(v_w0[:, columns_of(part)] if a == 0 else entries_of(v_w1, part)).bitcast(FP8X4),
-                    rhs_scale=entries_of(gathered_s if a == 0 else moved_s, part),
+                    rhs=moving_words(a, part).bitcast(FP8X4),
+                    rhs_scale=planes[:, a * S + part[0] : a * S + part[0] + part[1]],
                     start=(s == 0),
                     stop=(s == len(steps) - 1),
                 )
 
-        PIECE = 4 * QUARTER
         grouped, words, scales = {}, {}, {}
 
         def open_round(q, room=None, words_room=None):
-            pieces = 4 if q == 0 else 2
+            pieces = 2
             grouped[q] = held([P, pieces * PIECE], BF16, "grouped%d" % q, room)
             words[q] = held([P, pieces * QUARTER], U32, "words%d" % q, words_room)
             scales[q] = held([P, pieces * QUARTER], U8, "scales%d" % q)
@@ -209,38 +182,37 @@ def tile_list_place_cell_replay_kernel(tc, tab_words, tab_scales, offs, w4_words
         def quantize(q):
             nc.vector.quantize_mx(out=words[q][:].bitcast(FP8X4), scales=scales[q][:], in_=grouped[q][:])
 
-        def piece_with_vector(q, passes, banks):
-            rate = held([P, passes, PIECE], F32, "rate%d" % q)
-            for b in range(passes):
-                for u in range(2):
-                    bank = psum_bank(banks[2 * b + u])
-                    first_product(bank, b, [(t, (q * QUARTER + u * P, P), t * P) for t in range(4)], (0, 1) if q == 0 else (1, 0))
-                    nc.scalar.activation(
-                        rate[:, b, u * BANK : (u + 1) * BANK].rearrange("p (j t) -> p j t", t=4),
-                        bank[:].rearrange("p (t j) -> p j t", t=4),
-                        ACT.Tanh,
-                    )
+        def piece_with_vector(q, b, banks, room=None):
+            rate = held([P, PIECE], F32, "rate%d_%d" % (q, b), room)
+            for u in range(2):
+                bank = psum_bank(banks[u])
+                first_product(bank, b, [(t, (q * QUARTER + u * P, P), t * P) for t in range(4)], (0, 1) if q == 0 else (1, 0))
+                nc.scalar.activation(
+                    rate[:, u * BANK : (u + 1) * BANK].rearrange("p (j t) -> p j t", t=4),
+                    bank[:].rearrange("p (t j) -> p j t", t=4),
+                    ACT.Tanh,
+                    bias=zero_bias[:, 0:1],
+                )
             nc.vector.tensor_tensor(
-                grouped[q][:, 0 : passes * PIECE].rearrange("p (b j t) -> p b j t", b=passes, t=4),
-                rate[:].rearrange("p b (j t) -> p b j t", t=4),
-                peak_col[:, 0:passes, :].unsqueeze(2).to_broadcast([P, passes, QUARTER, 4]),
+                grouped[q][:, b * PIECE : (b + 1) * PIECE].rearrange("p (j t) -> p j t", t=4),
+                rate[:].rearrange("p (j t) -> p j t", t=4),
+                peak_col[:, b, :].unsqueeze(1).to_broadcast([P, QUARTER, 4]),
                 ALU.mult,
             )
 
         rounded = {}
 
         def scale_on_scalar(q, b, u, number, room=None):
-            first, count = quarters(q)
             if u == 0:
                 rounded[q, b] = held([P, PIECE], BF16, "rounded%d_%d" % (q, b))
             bank = psum_bank(number)
-            first_product(bank, b, [(2 * u + d, (first + j, P), d * count + j) for d in range(2) for j in range(0, count, P)])
+            first_product(bank, b, [(2 * u + d, quarters(q), d * QUARTER) for d in range(2)])
             values = held([P, BANK], F32, "saturated%d_%d_%d" % (q, b, u), room)
-            nc.scalar.activation(values[:], bank[:], ACT.Tanh)
+            nc.scalar.activation(values[:], bank[:], ACT.Tanh, bias=zero_bias[:, 0:1])
             for d in range(2):
                 t = 2 * u + d
                 nc.scalar.activation(
-                    rounded[q, b][:, t * count : (t + 1) * count], values[:, d * count : (d + 1) * count], ACT.Copy, scale=peak_col[:, b, t : t + 1]
+                    rounded[q, b][:, t * QUARTER : (t + 1) * QUARTER], values[:, d * QUARTER : (d + 1) * QUARTER], ACT.Copy, scale=peak_run[:, b, 2 * t : 2 * t + 1]
                 )
 
         def side_by_side(q, b):
@@ -249,38 +221,50 @@ def tile_list_place_cell_replay_kernel(tc, tab_words, tab_scales, offs, w4_words
                 rounded[q, b][:].rearrange("p (t c i) -> p c t i", i=4, t=4),
             )
 
-        def round_w2(half):
-            q, first = ((0, 2), (4, 0))[half]
+        def piece_on_scalar(q, b, banks):
+            for u in range(2):
+                scale_on_scalar(q, b, u, banks[u])
+            side_by_side(q, b)
+
+        w2_home = ((4, 0), (5, 0))
+
+        def round_w2(half, copy):
+            q, first = w2_home[half]
             for b in range(2):
-                (nc.vector.tensor_copy if half == 0 else nc.scalar.copy)(
+                copy(
                     grouped[q][:, (first + b) * PIECE : (first + b + 1) * PIECE].rearrange("p (c i t) -> p c t i", i=4, t=4),
-                    w2_raw[half, b][:].rearrange("p t (c i) -> p c t i", i=4),
+                    w2_raw[half][:, b].rearrange("p t (c i) -> p c t i", i=4),
                 )
 
         driven = {}
 
-        def second_product(m, part, number, room=None):
+        def second_product(steps, number, room=None):
             bank = psum_bank(number)
-            w2_round, w2_first = ((0, 2), (4, 0))[m // 2]
-            for u in range(part[1] // QUARTER):
-                q = part[0] // QUARTER + u
-                for b in range(2):
-                    w2_col = (w2_first + b) * QUARTER + (m % 2) * P
-                    nc.tensor.matmul_mx(
-                        out=bank[:, u * QUARTER : (u + 1) * QUARTER],
-                        lhsT=words[w2_round][:, w2_col : w2_col + P].bitcast(FP8X4),
-                        lhsT_scale=scales[w2_round][:, w2_col : w2_col + P],
-                        rhs=words[q][:, b * QUARTER : (b + 1) * QUARTER].bitcast(FP8X4),
-                        rhs_scale=scales[q][:, b * QUARTER : (b + 1) * QUARTER],
-                        start=(b == 0),
-                        stop=(b == 1),
-                    )
-            driven[m, part] = held([P, part[1]], F32, "y%d_%d" % (m, part[0]), room)
-            nc.scalar.activation(driven[m, part][:], bank[:, 0 : part[1]], ACT.Identity, bias=drive_col[:, m : m + 1])
+            spans, col = [], 0
+            for m, part in steps:
+                spans.append((m, part, col))
+                for u in range(part[1] // QUARTER):
+                    q = part[0] // QUARTER + u
+                    for b in range(2):
+                        w2_round, w2_first = w2_home[m // 2]
+                        w2_col = (w2_first + b) * QUARTER + (m % 2) * P
+                        nc.tensor.matmul_mx(
+                            out=bank[:, col : col + QUARTER],
+                            lhsT=words[w2_round][:, w2_col : w2_col + P].bitcast(FP8X4),
+                            lhsT_scale=scales[w2_round][:, w2_col : w2_col + P],
+                            rhs=words[q][:, b * QUARTER : (b + 1) * QUARTER].bitcast(FP8X4),
+                            rhs_scale=scales[q][:, b * QUARTER : (b + 1) * QUARTER],
+                            start=(b == 0),
+                            stop=(b == 1),
+                        )
+                    col = col + QUARTER
+            sums = held([P, col], F32, "y%d_%d" % (steps[0][0], steps[0][1][0]), room)
+            for m, part, first in spans:
+                driven[m, part] = sums[:, first : first + part[1]]
+                nc.scalar.activation(driven[m, part], bank[:, first : first + part[1]], ACT.Identity, bias=drive_col[:, m : m + 1])
 
-        def replace(m, part, number, room=None):
-            second_product(m, part, number, room)
-            nc.vector.tensor_tensor(listed(g_tile[m][:], part), picked[m][:, columns_of(part)], driven[m, part][:], ALU.add)
+        def replace(m, part):
+            nc.vector.tensor_tensor(listed(g_tile[m][:], part), picked[m][:, columns_of(part)], driven[m, part], ALU.add)
             finished = part[0] + part[1] == S
             if finished and m < 3:
                 nc.sync.dma_start(out[P * m : P * (m + 1), :], g_tile[m][:])
@@ -289,48 +273,58 @@ def tile_list_place_cell_replay_kernel(tc, tab_words, tab_scales, offs, w4_words
                     columns = slice(half * T // 2, (half + 1) * T // 2)
                     queue.dma_start(out[P * m : P * (m + 1), columns], g_tile[m][:, columns])
 
+        load_g(0)
+        load_w2(0)
+        load_g(1)
+        load_w2(1)
+        load_g(2)
+        load_g(3)
         open_round(0)
         gather_g(0)
-        piece_with_vector(0, 2, (0, 1, 2, 3))
-        open_round(1)
-        piece_with_vector(1, 1, (4, 5))
-        round_w2(0)
-        quantize(0)
-        for u in range(2):
-            scale_on_scalar(1, 1, u, 6 + u)
-        side_by_side(1, 1)
-        quantize(1)
-        gather_g(1, "grouped1")
-        turned = psum_bank(6)
-        nc.tensor.transpose(turned[:, 0:P], rows[:, 2 * P : 3 * P], identity[:])
-        drive_col = held([P, 4], F32, "drive_col")
-        nc.scalar.copy(drive_col[:], turned[:, 0:4])
-        scale_on_scalar(2, 0, 0, 0)
-        scale_on_scalar(2, 0, 1, 1, ROUNDED_AT)
-        replace(0, quarters(0, 2), 4, ROUNDED_AT - 6 * QUARTER)
-        replace(1, quarters(0, 2), 4)
-        open_round(4, ROUNDED_AT + 2 * QUARTER)
-        round_w2(1)
+        piece_with_vector(0, 0, (0, 1))
+        piece_with_vector(0, 1, (2, 3))
+        open_round(4, None, "rate0_0")
+        round_w2(0, nc.vector.tensor_copy)
         quantize(4)
-        gather_g(2, ROUNDED_AT + 2 * QUARTER)
-        open_round(2, W2_AT[3])
-        side_by_side(2, 0)
+        quantize(0)
+        gather_g(1, "rate0_1")
+        open_round(1)
+        piece_on_scalar(1, 0, (4, 5))
+        second_product([(0, quarters(0)), (1, quarters(0))], 0)
+        piece_on_scalar(1, 1, (6, 7))
+        replace(0, quarters(0))
+        replace(1, quarters(0))
+        gather_g(2)
+        quantize(1)
+        gather_g(3, "rounded1_1")
+        open_round(5)
+        round_w2(1, nc.scalar.copy)
+        quantize(5)
+        open_round(2)
         for u in range(2):
-            scale_on_scalar(2, 1, u, u, W2_AT[2] + u * 4 * BANK)
+            scale_on_scalar(2, 0, u, 1 + u)
+        second_product([(0, quarters(1)), (1, quarters(1))], 5, "saturated2_0_1")
+        side_by_side(2, 0)
+        scale_on_scalar(2, 1, 0, 3)
+        second_product([(2, quarters(0, 2))], 6, "saturated2_1_0")
+        scale_on_scalar(2, 1, 1, 4)
         side_by_side(2, 1)
+        replace(0, quarters(1))
+        replace(1, quarters(1))
+        replace(2, quarters(0, 2))
         quantize(2)
-        gather_g(3)
+        second_product([(3, quarters(0, 2))], 7, "rounded2_1")
+        replace(3, quarters(0, 2))
         open_round(3)
         for u in range(2):
             scale_on_scalar(3, 0, u, u)
-        replace(2, quarters(0, 2), 6, "saturated3_0_1")
+        second_product([(0, quarters(2))], 4, "saturated3_0_1")
         side_by_side(3, 0)
-        replace(3, quarters(0, 2), 7, "rounded3_0")
-        for u in range(2):
-            scale_on_scalar(3, 1, u, u)
-        replace(0, quarters(2), 5, "saturated3_1_1")
-        side_by_side(3, 1)
+        replace(0, quarters(2))
+        piece_on_scalar(3, 1, (2, 3))
         quantize(3)
-        replace(1, quarters(2), 6, "rounded3_1")
-        for m, part, number in ((0, quarters(3), 7), (1, quarters(3), 4), (2, quarters(2, 2), 2), (3, quarters(2, 2), 3)):
-            replace(m, part, number)
+        second_product([(1, quarters(2))], 5, "rounded3_1")
+        replace(1, quarters(2))
+        for m, part, number in ((0, quarters(3), 6), (1, quarters(3), 7), (2, quarters(2, 2), 0), (3, quarters(2, 2), 1)):
+            second_product([(m, part)], number)
+            replace(m, part)

@@ -25,12 +25,21 @@ HALF = N // 2
 PIECE = 4 * QUARTER
 ROWS_AT = 96
 TILE = 4 * T
-G_AT = [0, 2 * TILE, 4 * TILE, 5 * TILE]
-W2_AT = [TILE, 3 * TILE]
-TABS_AT = TILE - T // 2
-TAB0_AT = 5 * TILE // 2
-TAB1_AT = 9 * TILE // 2
-W4_AT = TAB1_AT + TILE
+G0_AT = 0
+W4_LATE_AT = TILE
+TABS_AT = W4_LATE_AT - T // 2
+G1_AT = 2 * TILE
+DRIVE_AT = 3 * TILE
+W2_EARLY_AT = DRIVE_AT + 64
+TAB0_AT = DRIVE_AT - TILE // 2
+G2_AT = W2_EARLY_AT + TILE
+G3_AT = G2_AT + TILE
+W2_LATE_AT = G3_AT + TILE
+TAB1_AT = G3_AT - TILE // 8
+W4_EARLY_AT = TAB1_AT + TILE
+G_AT = [G0_AT, G1_AT, G2_AT, G3_AT]
+W2_AT = [W2_EARLY_AT, W2_LATE_AT]
+W4_AT = [W4_EARLY_AT, W4_LATE_AT]
 
 
 def quarters(first, count=1):
@@ -71,17 +80,14 @@ def tile_list_place_cell_replay_kernel(tc, tab_words, tab_scales, offs, w4_words
         nc.sync.dma_start(tab_w[0][:], tab_words[0].rearrange("p t i -> p (t i)").bitcast(I32))
 
         decay_col = held([P, 4], F32, "decay_col")
-        drive_col = held([P, 4], F32, "drive_col")
-        peak_run = held([P, 2, 8], F32, "peak_run")
-        peak_col = peak_run[:, :, 0:8:2]
         with nc.allow_non_contiguous_dma(reason="one value a partition"):
             nc.scalar.dma_start(decay_col[:], decay.rearrange("(m p) -> p m", p=P))
-        for d in range(2):
-            nc.gpsimd.dma_start(peak_run[d:P:2, :, 0:7], peak.rearrange("(b g e) -> g b e", b=2, e=8)[:, :, d : d + 7])
-        with nc.allow_non_contiguous_dma(reason="one value a partition"):
-            nc.gpsimd.dma_start(drive_col[:], drive.rearrange("(m p) -> p m", p=P))
 
-        zeros = held([P, 32], F32, "zeros", W4_AT - 64)
+        peak_run = held([P, 2, 8], F32, "peak_run")
+        for d in range(2):
+            nc.scalar.dma_start(peak_run[d:P:2, :, 0:7], peak.rearrange("(b g e) -> g b e", b=2, e=8)[:, :, d : d + 7])
+
+        zeros = held([P, 32], F32, "zeros", W4_EARLY_AT - 64)
         nc.vector.memset(zeros[:], 0.0)
         w4_s_raw = held([P, 2 * H], U8, "w4_s_raw")
         nc.vector.memset(w4_s_raw[:].bitcast(I32), 0)
@@ -94,10 +100,22 @@ def tile_list_place_cell_replay_kernel(tc, tab_words, tab_scales, offs, w4_words
                 w4_s_raw[32 * q : 32 * q + 4, :].bitcast(I32).rearrange("p (a c) -> p a c", a=2),
                 w4_scales[:, 4 * q : 4 * q + 4, :].bitcast(I32).rearrange("a r c -> r a c"),
             )
-        w4_raw = held([P, H], I32, "w4_raw", W4_AT)
-        nc.sync.dma_start(w4_raw[:].rearrange("p (a c) -> p a c", a=2), w4_words.bitcast(I32).rearrange("a p c -> p a c"))
         tab_w.append(held([P, T], I32, "tab_w1", TAB1_AT))
         nc.sync.dma_start(tab_w[1][:], tab_words[1].rearrange("p t i -> p (t i)").bitcast(I32))
+        w4_raw, w4_w = {}, {}
+
+        def load_w4(b):
+            w4_raw[b] = held([P, 2, H // 4], I32, "w4_raw%d" % b, W4_AT[b])
+            nc.sync.dma_start(w4_raw[b][:], w4_words.bitcast(I32).rearrange("a p (b c) -> b p a c", b=2)[b])
+
+        def deal_w4(b):
+            w4_w[b] = held([P, H // 2], U32, "w4_w%d" % b)
+            nc.scalar.copy(
+                w4_w[b][:].rearrange("p (a t g) -> p a g t", a=2, t=4),
+                w4_raw[b][:].bitcast(U32).rearrange("p a (g t) -> p a g t", t=4),
+            )
+
+        load_w4(0)
         nc.vector.memset(tab_s[0:ROWS_AT, :].bitcast(I32), 0)
         planes = held([P, 2 * S], U8, "planes")
         nc.vector.memset(planes[:].bitcast(I32), 0)
@@ -114,22 +132,23 @@ def tile_list_place_cell_replay_kernel(tc, tab_words, tab_scales, offs, w4_words
 
         w4_s = held([P, 2 * H], U8, "w4_s")
         nc.scalar.copy(
-            w4_s[:].bitcast(U16).rearrange("p (ab t g) -> p ab t g", ab=4, t=4),
-            w4_s_raw[:].bitcast(U16).rearrange("p (ab g t) -> p ab t g", ab=4, t=4),
+            w4_s[:].bitcast(U16).rearrange("p (ab t g) -> p ab g t", ab=4, t=4),
+            w4_s_raw[:].bitcast(U16).rearrange("p (ab g t) -> p ab g t", ab=4, t=4),
         )
-        w4_w = [held([P, H // 2], U32, "w4_w%d" % b) for b in range(2)]
-        for b in range(2):
-            nc.scalar.copy(
-                w4_w[b][:].rearrange("p (a t g) -> p a t g", a=2, t=4),
-                w4_raw[:].bitcast(U32).rearrange("p (a b g t) -> p b a t g", a=2, b=2, t=4)[:, b],
-            )
+        deal_w4(0)
         v_w1 = {part: held([P, part[1]], U32, "v_w1_%d" % part[0]) for part in (early, late)}
         for part in (early, late):
             nc.vector.tensor_copy(v_w1[part][:], listed(tab_w[1][:].bitcast(U32), part))
 
-        decay_wide = [held([P, S], F32, "decay_wide%d" % m) for m in range(4)]
+        gather_parts = [[whole], [whole], [quarters(0, 2), quarters(2, 2)], [whole]]
+        decay_wide = {}
         for m in range(4):
-            nc.scalar.copy(decay_wide[m][:], decay_col[:, m : m + 1].to_broadcast([P, S]))
+            for part in gather_parts[m]:
+                decay_wide[m, part] = held([P, part[1]], F32, "decay_wide%d_%d" % (m, part[0]))
+                nc.scalar.copy(decay_wide[m, part][:], decay_col[:, m : m + 1].to_broadcast([P, part[1]]))
+
+        peak_col = held([P, 2, 4], F32, "peak_col")
+        nc.scalar.copy(peak_col[:], peak_run[:, :, 0:8:2])
 
         w2_rows = w2.rearrange("(b g t d) n -> b d g t n", b=2, t=4, d=2)
         w2_raw, g_tile = {}, {}
@@ -148,7 +167,8 @@ def tile_list_place_cell_replay_kernel(tc, tab_words, tab_scales, offs, w4_words
 
         def gather_g(m, room=None):
             picked[m] = held([P, S], F32, "picked%d" % m, room)
-            nc.vector.tensor_tensor(picked[m][:], listed(g_tile[m][:], whole), decay_wide[m][:], ALU.mult)
+            for part in gather_parts[m]:
+                nc.vector.tensor_tensor(picked[m][:, columns_of(part)], listed(g_tile[m][:], part), decay_wide[m, part][:], ALU.mult)
 
         def moving_words(a, part):
             if a == 0:
@@ -156,7 +176,7 @@ def tile_list_place_cell_replay_kernel(tc, tab_words, tab_scales, offs, w4_words
             home = early if part[0] < late[0] else late
             return v_w1[home][:, part[0] - home[0] : part[0] - home[0] + part[1]]
 
-        def first_product(bank, b, spans, order=(1, 0)):
+        def first_product(bank, b, spans, order=(1, 0), opens=True, closes=True):
             steps = [(a,) + span for a in order for span in spans]
             for s, (a, t, part, bank_col) in enumerate(steps):
                 word_col = a * PASS + t * P
@@ -167,14 +187,14 @@ def tile_list_place_cell_replay_kernel(tc, tab_words, tab_scales, offs, w4_words
                     lhsT_scale=w4_s[:, w4_col : w4_col + P],
                     rhs=moving_words(a, part).bitcast(FP8X4),
                     rhs_scale=planes[:, a * S + part[0] : a * S + part[0] + part[1]],
-                    start=(s == 0),
-                    stop=(s == len(steps) - 1),
+                    start=(opens and s == 0),
+                    stop=(closes and s == len(steps) - 1),
                 )
 
         grouped, words, scales = {}, {}, {}
 
         def open_round(q, room=None, words_room=None):
-            pieces = 2
+            pieces = 4 if q < 2 else 2
             grouped[q] = held([P, pieces * PIECE], BF16, "grouped%d" % q, room)
             words[q] = held([P, pieces * QUARTER], U32, "words%d" % q, words_room)
             scales[q] = held([P, pieces * QUARTER], U8, "scales%d" % q)
@@ -184,9 +204,12 @@ def tile_list_place_cell_replay_kernel(tc, tab_words, tab_scales, offs, w4_words
 
         def piece_with_vector(q, b, banks, room=None):
             rate = held([P, PIECE], F32, "rate%d_%d" % (q, b), room)
+            tiles = [psum_bank(number) for number in banks]
+            for a in range(2):
+                for u in range(2):
+                    first_product(tiles[u], b, [(t, (q * QUARTER + u * P, P), t * P) for t in range(4)], (a,), a == 0, a == 1)
             for u in range(2):
-                bank = psum_bank(banks[u])
-                first_product(bank, b, [(t, (q * QUARTER + u * P, P), t * P) for t in range(4)], (0, 1) if q == 0 else (1, 0))
+                bank = tiles[u]
                 nc.scalar.activation(
                     rate[:, u * BANK : (u + 1) * BANK].rearrange("p (j t) -> p j t", t=4),
                     bank[:].rearrange("p (t j) -> p j t", t=4),
@@ -212,7 +235,7 @@ def tile_list_place_cell_replay_kernel(tc, tab_words, tab_scales, offs, w4_words
             for d in range(2):
                 t = 2 * u + d
                 nc.scalar.activation(
-                    rounded[q, b][:, t * QUARTER : (t + 1) * QUARTER], values[:, d * QUARTER : (d + 1) * QUARTER], ACT.Copy, scale=peak_run[:, b, 2 * t : 2 * t + 1]
+                    rounded[q, b][:, t * QUARTER : (t + 1) * QUARTER], values[:, d * QUARTER : (d + 1) * QUARTER], ACT.Copy, scale=peak_col[:, b, t : t + 1]
                 )
 
         def side_by_side(q, b):
@@ -221,20 +244,19 @@ def tile_list_place_cell_replay_kernel(tc, tab_words, tab_scales, offs, w4_words
                 rounded[q, b][:].rearrange("p (t c i) -> p c t i", i=4, t=4),
             )
 
-        def piece_on_scalar(q, b, banks):
+        def piece_on_scalar(q, b, banks, rooms=(None, None)):
             for u in range(2):
-                scale_on_scalar(q, b, u, banks[u])
+                scale_on_scalar(q, b, u, banks[u], rooms[u])
             side_by_side(q, b)
 
-        w2_home = ((4, 0), (5, 0))
+        w2_home = ((0, 2), (1, 2))
 
         def round_w2(half, copy):
             q, first = w2_home[half]
-            for b in range(2):
-                copy(
-                    grouped[q][:, (first + b) * PIECE : (first + b + 1) * PIECE].rearrange("p (c i t) -> p c t i", i=4, t=4),
-                    w2_raw[half][:, b].rearrange("p t (c i) -> p c t i", i=4),
-                )
+            copy(
+                grouped[q][:, first * PIECE : (first + 2) * PIECE].rearrange("p (b c i t) -> p b c t i", b=2, i=4, t=4),
+                w2_raw[half][:].rearrange("p b t (c i) -> p b c t i", i=4),
+            )
 
         driven = {}
 
@@ -274,57 +296,62 @@ def tile_list_place_cell_replay_kernel(tc, tab_words, tab_scales, offs, w4_words
                     queue.dma_start(out[P * m : P * (m + 1), columns], g_tile[m][:, columns])
 
         load_g(0)
-        load_w2(0)
+        load_w4(1)
+        deal_w4(1)
         load_g(1)
-        load_w2(1)
+        load_w2(0)
+        drive_col = held([P, 4], F32, "drive_col", DRIVE_AT)
+        with nc.allow_non_contiguous_dma(reason="one value a partition"):
+            nc.sync.dma_start(drive_col[:], drive.rearrange("(m p) -> p m", p=P))
         load_g(2)
         load_g(3)
-        open_round(0)
+        load_w2(1)
         gather_g(0)
-        piece_with_vector(0, 0, (0, 1))
+        gather_g(1)
+        open_round(0, "decay_wide1_0")
+        piece_with_vector(0, 0, (0, 1), W4_LATE_AT)
         piece_with_vector(0, 1, (2, 3))
-        open_round(4, None, "rate0_0")
         round_w2(0, nc.vector.tensor_copy)
-        quantize(4)
         quantize(0)
-        gather_g(1, "rate0_1")
+        gather_g(2, W2_AT[0])
         open_round(1)
-        piece_on_scalar(1, 0, (4, 5))
-        second_product([(0, quarters(0)), (1, quarters(0))], 0)
-        piece_on_scalar(1, 1, (6, 7))
+        piece_on_scalar(1, 1, (4, 5))
+        piece_on_scalar(1, 0, (2, 3))
+        second_product([(0, quarters(0)), (1, quarters(0))], 0, "decay_wide2_0")
         replace(0, quarters(0))
         replace(1, quarters(0))
-        gather_g(2)
-        quantize(1)
-        gather_g(3, "rounded1_1")
-        open_round(5)
         round_w2(1, nc.scalar.copy)
-        quantize(5)
+        quantize(1)
+        first_room, second_room = W2_AT[1] + TILE // 2, W2_AT[1] + 3 * TILE // 4
         open_round(2)
-        for u in range(2):
-            scale_on_scalar(2, 0, u, 1 + u)
-        second_product([(0, quarters(1)), (1, quarters(1))], 5, "saturated2_0_1")
+        scale_on_scalar(2, 0, 0, 1, W2_AT[1])
+        gather_g(3, W2_AT[1])
+        scale_on_scalar(2, 0, 1, 2, second_room)
         side_by_side(2, 0)
-        scale_on_scalar(2, 1, 0, 3)
-        second_product([(2, quarters(0, 2))], 6, "saturated2_1_0")
-        scale_on_scalar(2, 1, 1, 4)
+        second_product([(2, quarters(0, 2))], 5, "rounded2_0")
+        scale_on_scalar(2, 1, 0, 3, first_room)
+        second_product([(0, quarters(1))], 6, first_room)
+        scale_on_scalar(2, 1, 1, 4, second_room)
         side_by_side(2, 1)
-        replace(0, quarters(1))
-        replace(1, quarters(1))
         replace(2, quarters(0, 2))
+        replace(0, quarters(1))
         quantize(2)
         second_product([(3, quarters(0, 2))], 7, "rounded2_1")
         replace(3, quarters(0, 2))
         open_round(3)
-        for u in range(2):
-            scale_on_scalar(3, 0, u, u)
-        second_product([(0, quarters(2))], 4, "saturated3_0_1")
+        scale_on_scalar(3, 0, 0, 1, second_room)
+        scale_on_scalar(3, 0, 1, 2)
         side_by_side(3, 0)
+        second_product([(1, quarters(1, 2))], 0, "rounded3_0")
+        replace(1, quarters(1, 2))
+        scale_on_scalar(3, 1, 0, 3, second_room)
+        second_product([(0, quarters(2))], 5, second_room)
         replace(0, quarters(2))
-        piece_on_scalar(3, 1, (2, 3))
+        scale_on_scalar(3, 1, 1, 4, "saturated3_0_1")
+        side_by_side(3, 1)
         quantize(3)
-        second_product([(1, quarters(2))], 5, "rounded3_1")
-        replace(1, quarters(2))
-        for m, part, number in ((0, quarters(3), 6), (1, quarters(3), 7), (2, quarters(2, 2), 0), (3, quarters(2, 2), 1)):
+        second_product([(2, quarters(2))], 6, "rounded3_1")
+        replace(2, quarters(2))
+        for m, part, number in ((0, quarters(3), 7), (1, quarters(3), 1), (2, quarters(3), 2), (3, quarters(2, 2), 0)):
             second_product([(m, part)], number)
             replace(m, part)

@@ -29,11 +29,11 @@ G0_AT = 0
 W4_LATE_AT = TILE
 TABS_AT = W4_LATE_AT - T // 2
 G1_AT = 2 * TILE
-DRIVE_AT = 3 * TILE
-W2_EARLY_AT = DRIVE_AT + 64
-TAB0_AT = DRIVE_AT - TILE // 2
+W2_EARLY_AT = 3 * TILE
+TAB0_AT = W2_EARLY_AT - TILE // 2
 G2_AT = W2_EARLY_AT + TILE
-G3_AT = G2_AT + TILE
+DRIVE_AT = G2_AT + TILE
+G3_AT = DRIVE_AT + 64
 W2_LATE_AT = G3_AT + TILE
 TAB1_AT = G3_AT - TILE // 8
 W4_EARLY_AT = TAB1_AT + TILE
@@ -72,7 +72,6 @@ def tile_list_place_cell_replay_kernel(tc, tab_words, tab_scales, offs, w4_words
             return slice(part[0], part[0] + part[1])
 
         whole = (0, S)
-        early, late = quarters(0), quarters(1, 3)
 
         tab_s = held([P, T], U8, "tab_s", TABS_AT)
         nc.sync.dma_start(tab_s[ROWS_AT:P, :].bitcast(I32), tab_scales.bitcast(I32).rearrange("a q c -> q a c"))
@@ -136,9 +135,8 @@ def tile_list_place_cell_replay_kernel(tc, tab_words, tab_scales, offs, w4_words
             w4_s_raw[:].bitcast(U16).rearrange("p (ab g t) -> p ab g t", ab=4, t=4),
         )
         deal_w4(0)
-        v_w1 = {part: held([P, part[1]], U32, "v_w1_%d" % part[0]) for part in (early, late)}
-        for part in (early, late):
-            nc.vector.tensor_copy(v_w1[part][:], listed(tab_w[1][:].bitcast(U32), part))
+        v_w1 = held([P, S], U32, "v_w1")
+        nc.vector.tensor_copy(v_w1[:], listed(tab_w[1][:].bitcast(U32), whole))
 
         gather_parts = [[whole], [whole], [quarters(0, 2), quarters(2, 2)], [whole]]
         decay_wide = {}
@@ -171,10 +169,7 @@ def tile_list_place_cell_replay_kernel(tc, tab_words, tab_scales, offs, w4_words
                 nc.vector.tensor_tensor(picked[m][:, columns_of(part)], listed(g_tile[m][:], part), decay_wide[m, part][:], ALU.mult)
 
         def moving_words(a, part):
-            if a == 0:
-                return v_w0[:, columns_of(part)]
-            home = early if part[0] < late[0] else late
-            return v_w1[home][:, part[0] - home[0] : part[0] - home[0] + part[1]]
+            return (v_w0, v_w1)[a][:, columns_of(part)]
 
         def first_product(bank, b, spans, order=(1, 0), opens=True, closes=True):
             steps = [(a,) + span for a in order for span in spans]
@@ -194,7 +189,7 @@ def tile_list_place_cell_replay_kernel(tc, tab_words, tab_scales, offs, w4_words
         grouped, words, scales = {}, {}, {}
 
         def open_round(q, room=None, words_room=None):
-            pieces = 4 if q < 2 else 2
+            pieces = 4 if q == 0 else 2
             grouped[q] = held([P, pieces * PIECE], BF16, "grouped%d" % q, room)
             words[q] = held([P, pieces * QUARTER], U32, "words%d" % q, words_room)
             scales[q] = held([P, pieces * QUARTER], U8, "scales%d" % q)
@@ -223,19 +218,22 @@ def tile_list_place_cell_replay_kernel(tc, tab_words, tab_scales, offs, w4_words
                 ALU.mult,
             )
 
-        rounded = {}
+        rounded, values = {}, {}
 
-        def scale_on_scalar(q, b, u, number, room=None):
-            if u == 0:
-                rounded[q, b] = held([P, PIECE], BF16, "rounded%d_%d" % (q, b))
+        def saturate(q, b, u, number):
             bank = psum_bank(number)
             first_product(bank, b, [(2 * u + d, quarters(q), d * QUARTER) for d in range(2)])
-            values = held([P, BANK], F32, "saturated%d_%d_%d" % (q, b, u), room)
-            nc.scalar.activation(values[:], bank[:], ACT.Tanh, bias=zero_bias[:, 0:1])
-            for d in range(2):
-                t = 2 * u + d
+            values[q, b, u] = held([P, BANK], F32, "saturated%d_%d_%d" % (q, b, u), "saturated%d" % u)
+            nc.scalar.activation(values[q, b, u][:], bank[:], ACT.Tanh, bias=zero_bias[:, 0:1])
+
+        def scale(q, b, room=None):
+            rounded[q, b] = held([P, PIECE], BF16, "rounded%d_%d" % (q, b), room)
+            for t in range(4):
                 nc.scalar.activation(
-                    rounded[q, b][:, t * QUARTER : (t + 1) * QUARTER], values[:, d * QUARTER : (d + 1) * QUARTER], ACT.Copy, scale=peak_col[:, b, t : t + 1]
+                    rounded[q, b][:, t * QUARTER : (t + 1) * QUARTER],
+                    values[q, b, t // 2][:, (t % 2) * QUARTER : (t % 2 + 1) * QUARTER],
+                    ACT.Copy,
+                    scale=peak_col[:, b, t : t + 1],
                 )
 
         def side_by_side(q, b):
@@ -244,12 +242,7 @@ def tile_list_place_cell_replay_kernel(tc, tab_words, tab_scales, offs, w4_words
                 rounded[q, b][:].rearrange("p (t c i) -> p c t i", i=4, t=4),
             )
 
-        def piece_on_scalar(q, b, banks, rooms=(None, None)):
-            for u in range(2):
-                scale_on_scalar(q, b, u, banks[u], rooms[u])
-            side_by_side(q, b)
-
-        w2_home = ((0, 2), (1, 2))
+        w2_home = ((0, 2), (4, 0))
 
         def round_w2(half, copy):
             q, first = w2_home[half]
@@ -260,18 +253,17 @@ def tile_list_place_cell_replay_kernel(tc, tab_words, tab_scales, offs, w4_words
 
         driven = {}
 
-        def second_product(steps, number, room=None):
-            bank = psum_bank(number)
-            spans, col = [], 0
-            for m, part in steps:
-                spans.append((m, part, col))
+        def second_product(steps, room=None):
+            sums = held([P, sum(part[1] for m, part, number, col in steps)], F32, "y%d_%d" % (steps[0][0], steps[0][1][0]), room)
+            banks = {number: psum_bank(number) for number in sorted(set(step[2] for step in steps))}
+            for m, part, number, col in steps:
+                w2_round, w2_first = w2_home[m // 2]
                 for u in range(part[1] // QUARTER):
                     q = part[0] // QUARTER + u
                     for b in range(2):
-                        w2_round, w2_first = w2_home[m // 2]
                         w2_col = (w2_first + b) * QUARTER + (m % 2) * P
                         nc.tensor.matmul_mx(
-                            out=bank[:, col : col + QUARTER],
+                            out=banks[number][:, col + u * QUARTER : col + (u + 1) * QUARTER],
                             lhsT=words[w2_round][:, w2_col : w2_col + P].bitcast(FP8X4),
                             lhsT_scale=scales[w2_round][:, w2_col : w2_col + P],
                             rhs=words[q][:, b * QUARTER : (b + 1) * QUARTER].bitcast(FP8X4),
@@ -279,11 +271,11 @@ def tile_list_place_cell_replay_kernel(tc, tab_words, tab_scales, offs, w4_words
                             start=(b == 0),
                             stop=(b == 1),
                         )
-                    col = col + QUARTER
-            sums = held([P, col], F32, "y%d_%d" % (steps[0][0], steps[0][1][0]), room)
-            for m, part, first in spans:
+            first = 0
+            for m, part, number, col in steps:
                 driven[m, part] = sums[:, first : first + part[1]]
-                nc.scalar.activation(driven[m, part], bank[:, first : first + part[1]], ACT.Identity, bias=drive_col[:, m : m + 1])
+                nc.scalar.activation(driven[m, part], banks[number][:, col : col + part[1]], ACT.Identity, bias=drive_col[:, m : m + 1])
+                first = first + part[1]
 
         def replace(m, part):
             nc.vector.tensor_tensor(listed(g_tile[m][:], part), picked[m][:, columns_of(part)], driven[m, part], ALU.add)
@@ -300,58 +292,66 @@ def tile_list_place_cell_replay_kernel(tc, tab_words, tab_scales, offs, w4_words
         deal_w4(1)
         load_g(1)
         load_w2(0)
+        load_g(2)
+        load_g(3)
         drive_col = held([P, 4], F32, "drive_col", DRIVE_AT)
         with nc.allow_non_contiguous_dma(reason="one value a partition"):
             nc.sync.dma_start(drive_col[:], drive.rearrange("(m p) -> p m", p=P))
-        load_g(2)
-        load_g(3)
         load_w2(1)
         gather_g(0)
-        gather_g(1)
-        open_round(0, "decay_wide1_0")
+        open_round(0, "decay_wide0_0")
         piece_with_vector(0, 0, (0, 1), W4_LATE_AT)
         piece_with_vector(0, 1, (2, 3))
+        gather_g(1)
         round_w2(0, nc.vector.tensor_copy)
         quantize(0)
         gather_g(2, W2_AT[0])
-        open_round(1)
-        piece_on_scalar(1, 1, (4, 5))
-        piece_on_scalar(1, 0, (2, 3))
-        second_product([(0, quarters(0)), (1, quarters(0))], 0, "decay_wide2_0")
-        replace(0, quarters(0))
-        replace(1, quarters(0))
-        round_w2(1, nc.scalar.copy)
+        open_round(1, None, "decay_wide2_0")
+        saturate(1, 1, 0, 4)
+        saturate(1, 1, 1, 5)
+        scale(1, 1)
+        saturate(1, 0, 0, 2)
+        side_by_side(1, 1)
+        saturate(1, 0, 1, 3)
+        scale(1, 0)
+        saturate(2, 0, 0, 4)
+        side_by_side(1, 0)
         quantize(1)
-        first_room, second_room = W2_AT[1] + TILE // 2, W2_AT[1] + 3 * TILE // 4
+        gather_g(3, "rounded1_0")
+        saturate(2, 0, 1, 5)
+        open_round(4)
+        round_w2(1, nc.scalar.copy)
+        quantize(4)
+        second_product([(0, quarters(0, 2), 0, 0)], W2_AT[1] + TILE // 2)
+        replace(0, quarters(0, 2))
         open_round(2)
-        scale_on_scalar(2, 0, 0, 1, W2_AT[1])
-        gather_g(3, W2_AT[1])
-        scale_on_scalar(2, 0, 1, 2, second_room)
+        scale(2, 0, W2_AT[1])
+        saturate(2, 1, 0, 2)
         side_by_side(2, 0)
-        second_product([(2, quarters(0, 2))], 5, "rounded2_0")
-        scale_on_scalar(2, 1, 0, 3, first_room)
-        second_product([(0, quarters(1))], 6, first_room)
-        scale_on_scalar(2, 1, 1, 4, second_room)
-        side_by_side(2, 1)
+        second_product([(1, quarters(0, 2), 1, 0), (2, quarters(0, 2), 6, 0)], W2_AT[1])
+        replace(1, quarters(0, 2))
         replace(2, quarters(0, 2))
-        replace(0, quarters(1))
+        saturate(2, 1, 1, 3)
+        scale(2, 1)
+        saturate(3, 0, 0, 4)
+        side_by_side(2, 1)
         quantize(2)
-        second_product([(3, quarters(0, 2))], 7, "rounded2_1")
+        second_product([(3, quarters(0, 2), 7, 0)], "rounded2_1")
         replace(3, quarters(0, 2))
         open_round(3)
-        scale_on_scalar(3, 0, 0, 1, second_room)
-        scale_on_scalar(3, 0, 1, 2)
+        saturate(3, 0, 1, 5)
+        scale(3, 0)
+        saturate(3, 1, 0, 2)
         side_by_side(3, 0)
-        second_product([(1, quarters(1, 2))], 0, "rounded3_0")
-        replace(1, quarters(1, 2))
-        scale_on_scalar(3, 1, 0, 3, second_room)
-        second_product([(0, quarters(2))], 5, second_room)
+        saturate(3, 1, 1, 3)
+        scale(3, 1)
+        second_product([(0, quarters(2), 0, 0), (1, quarters(2), 0, QUARTER)], "saturated0")
         replace(0, quarters(2))
-        scale_on_scalar(3, 1, 1, 4, "saturated3_0_1")
+        replace(1, quarters(2))
         side_by_side(3, 1)
         quantize(3)
-        second_product([(2, quarters(2))], 6, "rounded3_1")
+        second_product([(2, quarters(2), 1, 0)], "rounded3_1")
         replace(2, quarters(2))
-        for m, part, number in ((0, quarters(3), 7), (1, quarters(3), 1), (2, quarters(3), 2), (3, quarters(2, 2), 0)):
-            second_product([(m, part)], number)
+        for m, part, number in ((0, quarters(3), 6), (1, quarters(3), 7), (2, quarters(3), 4), (3, quarters(2, 2), 5)):
+            second_product([(m, part, number, 0)])
             replace(m, part)

@@ -87,11 +87,11 @@ def tile_list_place_cell_replay_kernel(tc, tab_words, tab_scales, offs, w4_words
             nc.scalar.dma_start(peak_run[d:P:2, :, 0:7], peak.rearrange("(b g e) -> g b e", b=2, e=8)[:, :, d : d + 7])
 
         zeros = held([P, 32], F32, "zeros", W4_EARLY_AT - 64)
-        nc.vector.memset(zeros[:], 0.0)
+        nc.gpsimd.memset(zeros[:], 0.0)
         w4_s_raw = held([P, 2 * H], U8, "w4_s_raw")
-        nc.vector.memset(w4_s_raw[:].bitcast(I32), 0)
+        nc.gpsimd.memset(w4_s_raw[:].bitcast(I32), 0)
         zero_in = held([P, 32], F32, "zero_in")
-        nc.vector.tensor_copy(zero_in[:], zeros[:])
+        nc.gpsimd.tensor_copy(zero_in[:], zeros[:])
         zero_bias = held([P, 32], F32, "zero_bias")
         nc.scalar.activation(zero_bias[:], zero_in[:], ACT.Tanh)
         for q in range(4):
@@ -116,16 +116,34 @@ def tile_list_place_cell_replay_kernel(tc, tab_words, tab_scales, offs, w4_words
 
         load_w4(0)
         nc.vector.memset(tab_s[0:ROWS_AT, :].bitcast(I32), 0)
-        planes = held([P, 2 * S], U8, "planes")
-        nc.vector.memset(planes[:].bitcast(I32), 0)
+        early, late = quarters(0), quarters(1, 3)
+        planes = {part: held([P, 2, part[1]], U8, "planes%d" % part[0]) for part in (early, late)}
+        for part in (early, late):
+            nc.vector.memset(planes[part][:].bitcast(I32), 0)
 
-        gathered_s = held([P, S], U8, "gathered_s")
-        nc.vector.tensor_copy(gathered_s[:], listed(tab_s[:], whole))
-        for q in range(4):
-            nc.sync.dma_start(
-                planes[32 * q : 32 * q + 4, :].bitcast(I32).rearrange("p (a c) -> p a c", a=2),
-                gathered_s[ROWS_AT + 8 * q : ROWS_AT + 8 * q + 8, :].bitcast(I32),
-            )
+        gathered_s, g_tile = {}, {}
+
+        def gather_scales(part):
+            gathered_s[part] = held([P, part[1]], U8, "gathered_s%d" % part[0])
+            nc.vector.tensor_copy(gathered_s[part][:], listed(tab_s[:], part))
+
+        def move_scales(part):
+            for q in range(4):
+                nc.sync.dma_start(
+                    planes[part][32 * q : 32 * q + 4].bitcast(I32),
+                    gathered_s[part][ROWS_AT + 8 * q : ROWS_AT + 8 * q + 8, :].bitcast(I32),
+                )
+
+        def load_g(m):
+            g_tile[m] = held([P, T], F32, "g_tile%d" % m, G_AT[m])
+            nc.sync.dma_start(g_tile[m][:], gT[P * m : P * (m + 1), :])
+
+        gather_scales(early)
+        move_scales(early)
+        gather_scales(late)
+        load_g(0)
+        load_w4(1)
+        move_scales(late)
         v_w0 = held([P, S], U32, "v_w0")
         nc.vector.tensor_copy(v_w0[:], listed(tab_w[0][:].bitcast(U32), whole))
 
@@ -149,17 +167,13 @@ def tile_list_place_cell_replay_kernel(tc, tab_words, tab_scales, offs, w4_words
         nc.scalar.copy(peak_col[:], peak_run[:, :, 0:8:2])
 
         w2_rows = w2.rearrange("(b g t d) n -> b d g t n", b=2, t=4, d=2)
-        w2_raw, g_tile = {}, {}
+        w2_raw = {}
 
         def load_w2(half):
             w2_raw[half] = held([P, 2, 4, HALF], F32, "w2_raw%d" % half, W2_AT[half])
             for b in range(2):
                 for d in range(2):
                     nc.sync.dma_start(w2_raw[half][d:P:2, b], w2_rows[b, d][:, :, half * HALF : (half + 1) * HALF])
-
-        def load_g(m):
-            g_tile[m] = held([P, T], F32, "g_tile%d" % m, G_AT[m])
-            nc.sync.dma_start(g_tile[m][:], gT[P * m : P * (m + 1), :])
 
         picked = {}
 
@@ -171,6 +185,10 @@ def tile_list_place_cell_replay_kernel(tc, tab_words, tab_scales, offs, w4_words
         def moving_words(a, part):
             return (v_w0, v_w1)[a][:, columns_of(part)]
 
+        def moving_scales(a, part):
+            home = early if part[0] < late[0] else late
+            return planes[home][:, a, part[0] - home[0] : part[0] - home[0] + part[1]]
+
         def first_product(bank, b, spans, order=(1, 0), opens=True, closes=True):
             steps = [(a,) + span for a in order for span in spans]
             for s, (a, t, part, bank_col) in enumerate(steps):
@@ -181,7 +199,7 @@ def tile_list_place_cell_replay_kernel(tc, tab_words, tab_scales, offs, w4_words
                     lhsT=w4_w[b][:].bitcast(U8)[:, 2 * word_col : 2 * (word_col + P)].bitcast(FP4X4),
                     lhsT_scale=w4_s[:, w4_col : w4_col + P],
                     rhs=moving_words(a, part).bitcast(FP8X4),
-                    rhs_scale=planes[:, a * S + part[0] : a * S + part[0] + part[1]],
+                    rhs_scale=moving_scales(a, part),
                     start=(opens and s == 0),
                     stop=(closes and s == len(steps) - 1),
                 )
@@ -287,8 +305,6 @@ def tile_list_place_cell_replay_kernel(tc, tab_words, tab_scales, offs, w4_words
                     columns = slice(half * T // 2, (half + 1) * T // 2)
                     queue.dma_start(out[P * m : P * (m + 1), columns], g_tile[m][:, columns])
 
-        load_g(0)
-        load_w4(1)
         deal_w4(1)
         load_g(1)
         load_w2(0)

@@ -23,6 +23,7 @@ GROUP = 16
 QUARTER = S // 4
 HALF = N // 2
 PIECE = 4 * QUARTER
+TANH_STEPS = H * S // (P * BANK)
 ROWS_AT = 96
 TILE = 4 * T
 G0_AT = 0
@@ -86,13 +87,13 @@ def tile_list_place_cell_replay_kernel(tc, tab_words, tab_scales, offs, w4_words
         for d in range(2):
             nc.scalar.dma_start(peak_run[d:P:2, :, 0:7], peak.rearrange("(b g e) -> g b e", b=2, e=8)[:, :, d : d + 7])
 
-        zeros = held([P, 32], F32, "zeros", W4_EARLY_AT - 64)
+        zeros = placed.tile([P, TANH_STEPS], F32, name="zeros", offset=W4_EARLY_AT - 2 * TANH_STEPS)
         nc.gpsimd.memset(zeros[:], 0.0)
         w4_s_raw = held([P, 2 * H], U8, "w4_s_raw")
         nc.gpsimd.memset(w4_s_raw[:].bitcast(I32), 0)
-        zero_in = held([P, 32], F32, "zero_in")
+        zero_in = held([P, TANH_STEPS], F32, "zero_in")
         nc.gpsimd.tensor_copy(zero_in[:], zeros[:])
-        zero_bias = held([P, 32], F32, "zero_bias")
+        zero_bias = held([P, TANH_STEPS], F32, "zero_bias")
         nc.scalar.activation(zero_bias[:], zero_in[:], ACT.Tanh)
         for q in range(4):
             nc.sync.dma_start(
@@ -215,6 +216,10 @@ def tile_list_place_cell_replay_kernel(tc, tab_words, tab_scales, offs, w4_words
         def quantize(q):
             nc.vector.quantize_mx(out=words[q][:].bitcast(FP8X4), scales=scales[q][:], in_=grouped[q][:])
 
+        def bias_of(q, b, u):
+            step = 4 * q + 2 * b + u
+            return zero_bias[:, step : step + 1]
+
         def piece_with_vector(q, b, banks, room=None):
             rate = held([P, PIECE], F32, "rate%d_%d" % (q, b), room)
             tiles = [psum_bank(number) for number in banks]
@@ -227,7 +232,7 @@ def tile_list_place_cell_replay_kernel(tc, tab_words, tab_scales, offs, w4_words
                     rate[:, u * BANK : (u + 1) * BANK].rearrange("p (j t) -> p j t", t=4),
                     bank[:].rearrange("p (t j) -> p j t", t=4),
                     ACT.Tanh,
-                    bias=zero_bias[:, 0:1],
+                    bias=bias_of(q, b, u),
                 )
             nc.vector.tensor_tensor(
                 grouped[q][:, b * PIECE : (b + 1) * PIECE].rearrange("p (j t) -> p j t", t=4),
@@ -242,7 +247,7 @@ def tile_list_place_cell_replay_kernel(tc, tab_words, tab_scales, offs, w4_words
             bank = psum_bank(number)
             first_product(bank, b, [(2 * u + d, quarters(q), d * QUARTER) for d in range(2)])
             values[q, b, u] = held([P, BANK], F32, "saturated%d_%d_%d" % (q, b, u), "saturated%d" % u)
-            nc.scalar.activation(values[q, b, u][:], bank[:], ACT.Tanh, bias=zero_bias[:, 0:1])
+            nc.scalar.activation(values[q, b, u][:], bank[:], ACT.Tanh, bias=bias_of(q, b, u))
 
         def scale(q, b, room=None):
             rounded[q, b] = held([P, PIECE], BF16, "rounded%d_%d" % (q, b), room)
@@ -262,12 +267,13 @@ def tile_list_place_cell_replay_kernel(tc, tab_words, tab_scales, offs, w4_words
 
         w2_home = ((0, 2), (4, 0))
 
-        def round_w2(half, copy):
+        def round_w2(half, copy, passes):
             q, first = w2_home[half]
-            copy(
-                grouped[q][:, first * PIECE : (first + 2) * PIECE].rearrange("p (b c i t) -> p b c t i", b=2, i=4, t=4),
-                w2_raw[half][:].rearrange("p b t (c i) -> p b c t i", i=4),
-            )
+            for b in range(0, 2, passes):
+                copy(
+                    grouped[q][:, (first + b) * PIECE : (first + b + passes) * PIECE].rearrange("p (b c i t) -> p b c t i", b=passes, i=4, t=4),
+                    w2_raw[half][:, b : b + passes].rearrange("p b t (c i) -> p b c t i", i=4),
+                )
 
         driven = {}
 
@@ -310,16 +316,16 @@ def tile_list_place_cell_replay_kernel(tc, tab_words, tab_scales, offs, w4_words
         load_w2(0)
         load_g(2)
         load_g(3)
+        load_w2(1)
         drive_col = held([P, 4], F32, "drive_col", DRIVE_AT)
         with nc.allow_non_contiguous_dma(reason="one value a partition"):
             nc.sync.dma_start(drive_col[:], drive.rearrange("(m p) -> p m", p=P))
-        load_w2(1)
         gather_g(0)
         open_round(0, "decay_wide0_0")
         piece_with_vector(0, 0, (0, 1), W4_LATE_AT)
         piece_with_vector(0, 1, (2, 3))
         gather_g(1)
-        round_w2(0, nc.vector.tensor_copy)
+        round_w2(0, nc.vector.tensor_copy, 2)
         quantize(0)
         gather_g(2, W2_AT[0])
         open_round(1, None, "decay_wide2_0")
@@ -336,7 +342,7 @@ def tile_list_place_cell_replay_kernel(tc, tab_words, tab_scales, offs, w4_words
         gather_g(3, "rounded1_0")
         saturate(2, 0, 1, 5)
         open_round(4)
-        round_w2(1, nc.scalar.copy)
+        round_w2(1, nc.scalar.copy, 1)
         quantize(4)
         second_product([(0, quarters(0, 2), 0, 0)], W2_AT[1] + TILE // 2)
         replace(0, quarters(0, 2))

@@ -157,7 +157,7 @@ def tile_list_place_cell_replay_kernel(tc, tab_words, tab_scales, offs, w4_words
         v_w1 = held([P, S], U32, "v_w1")
         nc.vector.tensor_copy(v_w1[:], listed(tab_w[1][:].bitcast(U32), whole))
 
-        gather_parts = [[whole], [whole], [quarters(0, 2), quarters(2, 2)], [whole]]
+        gather_parts = [[whole], [whole], [whole], [quarters(0, 2), quarters(2, 2)]]
         decay_wide = {}
         for m in range(4):
             for part in gather_parts[m]:
@@ -243,10 +243,10 @@ def tile_list_place_cell_replay_kernel(tc, tab_words, tab_scales, offs, w4_words
 
         rounded, values = {}, {}
 
-        def saturate(q, b, u, number):
+        def saturate(q, b, u, number, room=None):
             bank = psum_bank(number)
             first_product(bank, b, [(2 * u + d, quarters(q), d * QUARTER) for d in range(2)])
-            values[q, b, u] = held([P, BANK], F32, "saturated%d_%d_%d" % (q, b, u), "saturated%d" % u)
+            values[q, b, u] = held([P, BANK], F32, "saturated%d_%d_%d" % (q, b, u), room or "saturated%d" % u)
             nc.scalar.activation(values[q, b, u][:], bank[:], ACT.Tanh, bias=bias_of(q, b, u))
 
         def scale(q, b, room=None):
@@ -323,13 +323,17 @@ def tile_list_place_cell_replay_kernel(tc, tab_words, tab_scales, offs, w4_words
         gather_g(0)
         open_round(0, "decay_wide0_0")
         piece_with_vector(0, 0, (0, 1), W4_LATE_AT)
-        piece_with_vector(0, 1, (2, 3))
+        saturate(0, 1, 0, 2)
+        saturate(0, 1, 1, 3)
+        scale(0, 1)
+        saturate(1, 1, 0, 4)
+        side_by_side(0, 1)
         gather_g(1)
         round_w2(0, nc.vector.tensor_copy, 2)
         quantize(0)
         gather_g(2, W2_AT[0])
-        open_round(1, None, "decay_wide2_0")
-        saturate(1, 1, 0, 4)
+        gather_g(3)
+        open_round(1, None, "decay_wide3_0")
         saturate(1, 1, 1, 5)
         scale(1, 1)
         saturate(1, 0, 0, 2)
@@ -339,21 +343,24 @@ def tile_list_place_cell_replay_kernel(tc, tab_words, tab_scales, offs, w4_words
         saturate(2, 0, 0, 4)
         side_by_side(1, 0)
         quantize(1)
-        gather_g(3, "rounded1_0")
-        saturate(2, 0, 1, 5)
+        second_product([(0, quarters(0), 0, 0), (1, quarters(0), 0, QUARTER)], "rounded1_0")
+        replace(0, quarters(0))
+        replace(1, quarters(0))
         open_round(4)
         round_w2(1, nc.scalar.copy, 1)
         quantize(4)
-        second_product([(0, quarters(0, 2), 0, 0)], W2_AT[1] + TILE // 2)
-        replace(0, quarters(0, 2))
+        second_product([(0, quarters(1), 1, 0), (1, quarters(1), 1, QUARTER)], W2_AT[1] + TILE // 2)
+        replace(0, quarters(1))
+        replace(1, quarters(1))
+        late_room = W2_AT[1] + 3 * TILE // 4
+        saturate(2, 0, 1, 5, late_room)
         open_round(2)
         scale(2, 0, W2_AT[1])
         saturate(2, 1, 0, 2)
         side_by_side(2, 0)
-        second_product([(1, quarters(0, 2), 1, 0), (2, quarters(0, 2), 6, 0)], W2_AT[1])
-        replace(1, quarters(0, 2))
+        second_product([(2, quarters(0, 2), 6, 0)], W2_AT[1])
         replace(2, quarters(0, 2))
-        saturate(2, 1, 1, 3)
+        saturate(2, 1, 1, 3, late_room)
         scale(2, 1)
         saturate(3, 0, 0, 4)
         side_by_side(2, 1)
@@ -361,15 +368,15 @@ def tile_list_place_cell_replay_kernel(tc, tab_words, tab_scales, offs, w4_words
         second_product([(3, quarters(0, 2), 7, 0)], "rounded2_1")
         replace(3, quarters(0, 2))
         open_round(3)
-        saturate(3, 0, 1, 5)
+        saturate(3, 0, 1, 5, late_room)
         scale(3, 0)
         saturate(3, 1, 0, 2)
         side_by_side(3, 0)
-        saturate(3, 1, 1, 3)
-        scale(3, 1)
-        second_product([(0, quarters(2), 0, 0), (1, quarters(2), 0, QUARTER)], "saturated0")
+        saturate(3, 1, 1, 3, late_room)
+        second_product([(0, quarters(2), 0, 0), (1, quarters(2), 0, QUARTER)], "rounded3_0")
         replace(0, quarters(2))
         replace(1, quarters(2))
+        scale(3, 1)
         side_by_side(3, 1)
         quantize(3)
         second_product([(2, quarters(2), 1, 0)], "rounded3_1")

from contextlib import ExitStack

import concourse.mybir as mybir

K, H, N, T, S = 1024, 1024, 512, 2048, 1024
FLOPS = 2 * K * H * S + 2 * H * N * S

F32 = mybir.dt.float32
BF16 = mybir.dt.bfloat16
I32 = mybir.dt.int32
U32 = mybir.dt.uint32
U16 = mybir.dt.uint16
U8 = mybir.dt.uint8
FP8X4 = mybir.dt.float8_e4m3fn_x4
FP4X4 = mybir.dt.float4_e2m1fn_x4
ACT = mybir.ActivationFunctionType
ALU = mybir.AluOpType

P = 128
PASS = 512
BANK = 512
GROUP = 16
QUARTER = S // 4
HALF = N // 2
PIECE = 4 * QUARTER
TANH_STEPS = H * S // (P * BANK)
ROWS_AT = 96
TILE = 4 * T
G0_AT = 0
W4_LATE_AT = TILE
TABS_AT = W4_LATE_AT - T // 2
G1_AT = 2 * TILE
W2_EARLY_AT = 3 * TILE
TAB0_AT = W2_EARLY_AT - TILE // 2
G2_AT = W2_EARLY_AT + TILE
DRIVE_AT = G2_AT + TILE
G3_AT = DRIVE_AT + 64
W2_LATE_AT = G3_AT + TILE
TAB1_AT = G3_AT - TILE // 8
W4_EARLY_AT = TAB1_AT + TILE
G_AT = [G0_AT, G1_AT, G2_AT, G3_AT]
W2_AT = [W2_EARLY_AT, W2_LATE_AT]
W4_AT = [W4_EARLY_AT, W4_LATE_AT]


def quarters(first, count=1):
    return (first * QUARTER, count * QUARTER)


def tile_list_place_cell_replay_kernel(tc, tab_words, tab_scales, offs, w4_words, w4_scales, peak, w2, drive, decay, gT, out):
    nc = tc.nc
    with ExitStack() as ctx:
        keep = ctx.enter_context(tc.tile_pool(name="keep", bufs=1))
        placed = ctx.enter_context(tc.tile_pool(name="placed", bufs=1))
        psum = ctx.enter_context(tc.psum_pool(name="psum", bufs=1))

        def held(shape, dtype, name, room=None):
            if isinstance(room, int):
                return placed.tile(shape, dtype, name=name, align_bytes=64, offset=room)
            return keep.tile(shape, dtype, name=name, tag=room or name, align_bytes=64)

        def psum_bank(number):
            return psum.tile([P, BANK], F32, name="bank%d" % number)

        offsets = keep.tile([P, S // GROUP], U16, name="offsets")
        nc.sync.dma_start(offsets[:], offs)

        def listed(window, part):
            first, count = part
            return window.indirect(offsets[:, first // GROUP : (first + count) // GROUP])

        def columns_of(part):
            return slice(part[0], part[0] + part[1])

        whole = (0, S)

        tab_s = held([P, T], U8, "tab_s", TABS_AT)
        nc.sync.dma_start(tab_s[ROWS_AT:P, :].bitcast(I32), tab_scales.bitcast(I32).rearrange("a q c -> q a c"))
        tab_w = [held([P, T], I32, "tab_w0", TAB0_AT)]
        nc.sync.dma_start(tab_w[0][:], tab_words[0].rearrange("p t i -> p (t i)").bitcast(I32))

        decay_col = held([P, 4], F32, "decay_col")
        with nc.allow_non_contiguous_dma(reason="one value a partition"):
            nc.scalar.dma_start(decay_col[:], decay.rearrange("(m p) -> p m", p=P))

        peak_run = held([P, 2, 8], F32, "peak_run")
        for d in range(2):
            nc.scalar.dma_start(peak_run[d:P:2, :, 0:7], peak.rearrange("(b g e) -> g b e", b=2, e=8)[:, :, d : d + 7])

        zeros = placed.tile([P, TANH_STEPS], F32, name="zeros", offset=W4_EARLY_AT - 2 * TANH_STEPS)
        nc.gpsimd.memset(zeros[:], 0.0)
        w4_s_raw = held([P, 2 * H], U8, "w4_s_raw")
        nc.gpsimd.memset(w4_s_raw[:].bitcast(I32), 0)
        zero_in = held([P, TANH_STEPS], F32, "zero_in")
        nc.gpsimd.tensor_copy(zero_in[:], zeros[:])
        zero_bias = held([P, TANH_STEPS], F32, "zero_bias")
        nc.scalar.activation(zero_bias[:], zero_in[:], ACT.Tanh)
        for q in range(4):
            nc.sync.dma_start(
                w4_s_raw[32 * q : 32 * q + 4, :].bitcast(I32).rearrange("p (a c) -> p a c", a=2),
                w4_scales[:, 4 * q : 4 * q + 4, :].bitcast(I32).rearrange("a r c -> r a c"),
            )
        tab_w.append(held([P, T], I32, "tab_w1", TAB1_AT))
        nc.sync.dma_start(tab_w[1][:], tab_words[1].rearrange("p t i -> p (t i)").bitcast(I32))
        w4_raw, w4_w = {}, {}

        def load_w4(b):
            w4_raw[b] = held([P, 2, H // 4], I32, "w4_raw%d" % b, W4_AT[b])
            nc.sync.dma_start(w4_raw[b][:], w4_words.bitcast(I32).rearrange("a p (b c) -> b p a c", b=2)[b])

        def deal_w4(b):
            w4_w[b] = held([P, H // 2], U32, "w4_w%d" % b)
            nc.scalar.copy(
                w4_w[b][:].rearrange("p (a t g) -> p a g t", a=2, t=4),
                w4_raw[b][:].bitcast(U32).rearrange("p a (g t) -> p a g t", t=4),
            )

        load_w4(0)
        nc.vector.memset(tab_s[0:ROWS_AT, :].bitcast(I32), 0)
        early, late = quarters(0), quarters(1, 3)
        planes = {part: held([P, 2, part[1]], U8, "planes%d" % part[0]) for part in (early, late)}
        for part in (early, late):
            nc.vector.memset(planes[part][:].bitcast(I32), 0)

        gathered_s, g_tile = {}, {}

        def gather_scales(part):
            gathered_s[part] = held([P, part[1]], U8, "gathered_s%d" % part[0])
            nc.vector.tensor_copy(gathered_s[part][:], listed(tab_s[:], part))

        def move_scales(part):
            for q in range(4):
                nc.sync.dma_start(
                    planes[part][32 * q : 32 * q + 4].bitcast(I32),
                    gathered_s[part][ROWS_AT + 8 * q : ROWS_AT + 8 * q + 8, :].bitcast(I32),
                )

        def load_g(m):
            g_tile[m] = held([P, T], F32, "g_tile%d" % m, G_AT[m])
            nc.sync.dma_start(g_tile[m][:], gT[P * m : P * (m + 1), :])

        gather_scales(early)
        move_scales(early)
        gather_scales(late)
        load_g(0)
        load_w4(1)
        move_scales(late)
        v_w0 = held([P, S], U32, "v_w0")
        nc.vector.tensor_copy(v_w0[:], listed(tab_w[0][:].bitcast(U32), whole))

        w4_s = held([P, 2 * H], U8, "w4_s")
        nc.scalar.copy(
            w4_s[:].bitcast(U16).rearrange("p (ab t g) -> p ab g t", ab=4, t=4),
            w4_s_raw[:].bitcast(U16).rearrange("p (ab g t) -> p ab g t", ab=4, t=4),
        )
        deal_w4(0)
        v_w1 = held([P, S], U32, "v_w1")
        nc.vector.tensor_copy(v_w1[:], listed(tab_w[1][:].bitcast(U32), whole))

        gather_parts = [[whole], [whole], [whole], [quarters(0, 2), quarters(2, 2)]]
        decay_wide = {}
        for m in range(4):
            for part in gather_parts[m]:
                decay_wide[m, part] = held([P, part[1]], F32, "decay_wide%d_%d" % (m, part[0]))
                nc.scalar.copy(decay_wide[m, part][:], decay_col[:, m : m + 1].to_broadcast([P, part[1]]))

        peak_col = held([P, 2, 4], F32, "peak_col")
        nc.scalar.copy(peak_col[:], peak_run[:, :, 0:8:2])

        w2_rows = w2.rearrange("(b g t d) n -> b d g t n", b=2, t=4, d=2)
        w2_raw = {}

        def load_w2(half):
            w2_raw[half] = held([P, 2, 4, HALF], F32, "w2_raw%d" % half, W2_AT[half])
            for b in range(2):
                for d in range(2):
                    nc.sync.dma_start(w2_raw[half][d:P:2, b], w2_rows[b, d][:, :, half * HALF : (half + 1) * HALF])

        picked = {}

        def gather_g(m, room=None):
            picked[m] = held([P, S], F32, "picked%d" % m, room)
            for part in gather_parts[m]:
                nc.vector.tensor_tensor(picked[m][:, columns_of(part)], listed(g_tile[m][:], part), decay_wide[m, part][:], ALU.mult)

        def moving_words(a, part):
            return (v_w0, v_w1)[a][:, columns_of(part)]

        def moving_scales(a, part):
            home = early if part[0] < late[0] else late
            return planes[home][:, a, part[0] - home[0] : part[0] - home[0] + part[1]]

        def first_product(bank, b, spans, order=(1, 0), opens=True, closes=True):
            steps = [(a,) + span for a in order for span in spans]
            for s, (a, t, part, bank_col) in enumerate(steps):
                word_col = a * PASS + t * P
                w4_col = a * H + b * PASS + t * P
                nc.tensor.matmul_mx(
                    out=bank[:, bank_col : bank_col + part[1]],
                    lhsT=w4_w[b][:].bitcast(U8)[:, 2 * word_col : 2 * (word_col + P)].bitcast(FP4X4),
                    lhsT_scale=w4_s[:, w4_col : w4_col + P],
                    rhs=moving_words(a, part).bitcast(FP8X4),
                    rhs_scale=moving_scales(a, part),
                    start=(opens and s == 0),
                    stop=(closes and s == len(steps) - 1),
                )

        grouped, words, scales = {}, {}, {}

        def open_round(q, room=None, words_room=None):
            pieces = 4 if q == 0 else 2
            grouped[q] = held([P, pieces * PIECE], BF16, "grouped%d" % q, room)
            words[q] = held([P, pieces * QUARTER], U32, "words%d" % q, words_room)
            scales[q] = held([P, pieces * QUARTER], U8, "scales%d" % q)

        def quantize(q):
            nc.vector.quantize_mx(out=words[q][:].bitcast(FP8X4), scales=scales[q][:], in_=grouped[q][:])

        def bias_of(q, b, u):
            step = 4 * q + 2 * b + u
            return zero_bias[:, step : step + 1]

        def piece_with_vector(q, b, banks, room=None):
            rate = held([P, PIECE], F32, "rate%d_%d" % (q, b), room)
            tiles = [psum_bank(number) for number in banks]
            for a in range(2):
                for u in range(2):
                    first_product(tiles[u], b, [(t, (q * QUARTER + u * P, P), t * P) for t in range(4)], (a,), a == 0, a == 1)
            for u in range(2):
                bank = tiles[u]
                nc.scalar.activation(
                    rate[:, u * BANK : (u + 1) * BANK].rearrange("p (j t) -> p j t", t=4),
                    bank[:].rearrange("p (t j) -> p j t", t=4),
                    ACT.Tanh,
                    bias=bias_of(q, b, u),
                )
            nc.vector.tensor_tensor(
                grouped[q][:, b * PIECE : (b + 1) * PIECE].rearrange("p (j t) -> p j t", t=4),
                rate[:].rearrange("p (j t) -> p j t", t=4),
                peak_col[:, b, :].unsqueeze(1).to_broadcast([P, QUARTER, 4]),
                ALU.mult,
            )

        rounded, values = {}, {}

        def saturate(q, b, u, number, room=None):
            bank = psum_bank(number)
            first_product(bank, b, [(2 * u + d, quarters(q), d * QUARTER) for d in range(2)])
            values[q, b, u] = held([P, BANK], F32, "saturated%d_%d_%d" % (q, b, u), room or "saturated%d" % u)
            nc.scalar.activation(values[q, b, u][:], bank[:], ACT.Tanh, bias=bias_of(q, b, u))

        def scale(q, b, room=None):
            rounded[q, b] = held([P, PIECE], BF16, "rounded%d_%d" % (q, b), room)
            for t in range(4):
                nc.scalar.activation(
                    rounded[q, b][:, t * QUARTER : (t + 1) * QUARTER],
                    values[q, b, t // 2][:, (t % 2) * QUARTER : (t % 2 + 1) * QUARTER],
                    ACT.Copy,
                    scale=peak_col[:, b, t : t + 1],
                )

        def side_by_side(q, b):
            nc.scalar.copy(
                grouped[q][:, b * PIECE : (b + 1) * PIECE].rearrange("p (c i t) -> p c t i", i=4, t=4),
                rounded[q, b][:].rearrange("p (t c i) -> p c t i", i=4, t=4),
            )

        w2_home = ((0, 2), (4, 0))

        def round_w2(half, copy, passes):
            q, first = w2_home[half]
            for b in range(0, 2, passes):
                copy(
                    grouped[q][:, (first + b) * PIECE : (first + b + passes) * PIECE].rearrange("p (b c i t) -> p b c t i", b=passes, i=4, t=4),
                    w2_raw[half][:, b : b + passes].rearrange("p b t (c i) -> p b c t i", i=4),
                )

        driven = {}

        def second_product(steps, room=None):
            sums = held([P, sum(part[1] for m, part, number, col in steps)], F32, "y%d_%d" % (steps[0][0], steps[0][1][0]), room)
            banks = {number: psum_bank(number) for number in sorted(set(step[2] for step in steps))}
            for m, part, number, col in steps:
                w2_round, w2_first = w2_home[m // 2]
                for u in range(part[1] // QUARTER):
                    q = part[0] // QUARTER + u
                    for b in range(2):
                        w2_col = (w2_first + b) * QUARTER + (m % 2) * P
                        nc.tensor.matmul_mx(
                            out=banks[number][:, col + u * QUARTER : col + (u + 1) * QUARTER],
                            lhsT=words[w2_round][:, w2_col : w2_col + P].bitcast(FP8X4),
                            lhsT_scale=scales[w2_round][:, w2_col : w2_col + P],
                            rhs=words[q][:, b * QUARTER : (b + 1) * QUARTER].bitcast(FP8X4),
                            rhs_scale=scales[q][:, b * QUARTER : (b + 1) * QUARTER],
                            start=(b == 0),
                            stop=(b == 1),
                        )
            first = 0
            for m, part, number, col in steps:
                driven[m, part] = sums[:, first : first + part[1]]
                nc.scalar.activation(driven[m, part], banks[number][:, col : col + part[1]], ACT.Identity, bias=drive_col[:, m : m + 1])
                first = first + part[1]

        def replace(m, part):
            nc.vector.tensor_tensor(listed(g_tile[m][:], part), picked[m][:, columns_of(part)], driven[m, part], ALU.add)
            finished = part[0] + part[1] == S
            if finished and m < 3:
                nc.sync.dma_start(out[P * m : P * (m + 1), :], g_tile[m][:])
            elif finished:
                for half, queue in enumerate((nc.sync, nc.scalar)):
                    columns = slice(half * T // 2, (half + 1) * T // 2)
                    queue.dma_start(out[P * m : P * (m + 1), columns], g_tile[m][:, columns])

        deal_w4(1)
        load_g(1)
        load_w2(0)
        load_g(2)
        load_g(3)
        load_w2(1)
        drive_col = held([P, 4], F32, "drive_col", DRIVE_AT)
        with nc.allow_non_contiguous_dma(reason="one value a partition"):
            nc.sync.dma_start(drive_col[:], drive.rearrange("(m p) -> p m", p=P))
        gather_g(0)
        open_round(0, "decay_wide0_0")
        piece_with_vector(0, 0, (0, 1), W4_LATE_AT)
        saturate(0, 1, 0, 2)
        saturate(0, 1, 1, 3)
        scale(0, 1)
        saturate(1, 1, 0, 4)
        side_by_side(0, 1)
        gather_g(1)
        round_w2(0, nc.vector.tensor_copy, 2)
        quantize(0)
        gather_g(2, W2_AT[0])
        gather_g(3)
        open_round(1, None, "decay_wide3_0")
        saturate(1, 1, 1, 5)
        scale(1, 1)
        saturate(1, 0, 0, 2)
        side_by_side(1, 1)
        saturate(1, 0, 1, 3)
        scale(1, 0)
        saturate(2, 0, 0, 4)
        side_by_side(1, 0)
        quantize(1)
        second_product([(0, quarters(0), 0, 0), (1, quarters(0), 0, QUARTER)], "rounded1_0")
        replace(0, quarters(0))
        replace(1, quarters(0))
        open_round(4)
        round_w2(1, nc.scalar.copy, 1)
        quantize(4)
        second_product([(0, quarters(1), 1, 0), (1, quarters(1), 1, QUARTER)], W2_AT[1] + TILE // 2)
        replace(0, quarters(1))
        replace(1, quarters(1))
        late_room = W2_AT[1] + 3 * TILE // 4
        saturate(2, 0, 1, 5, late_room)
        open_round(2)
        scale(2, 0, W2_AT[1])
        saturate(2, 1, 0, 2)
        side_by_side(2, 0)
        second_product([(2, quarters(0, 2), 6, 0)], W2_AT[1])
        replace(2, quarters(0, 2))
        saturate(2, 1, 1, 3, late_room)
        scale(2, 1)
        saturate(3, 0, 0, 4)
        side_by_side(2, 1)
        quantize(2)
        second_product([(3, quarters(0, 2), 7, 0)], "rounded2_1")
        replace(3, quarters(0, 2))
        open_round(3)
        saturate(3, 0, 1, 5, late_room)
        scale(3, 0)
        saturate(3, 1, 0, 2)
        side_by_side(3, 0)
        saturate(3, 1, 1, 3, late_room)
        second_product([(0, quarters(2), 0, 0), (1, quarters(2), 0, QUARTER)], "rounded3_0")
        replace(0, quarters(2))
        replace(1, quarters(2))
        scale(3, 1)
        side_by_side(3, 1)
        quantize(3)
        second_product([(2, quarters(2), 1, 0)], "rounded3_1")
        replace(2, quarters(2))
        for m, part, number in ((0, quarters(3), 6), (1, quarters(3), 7), (2, quarters(3), 4), (3, quarters(2, 2), 5)):
            second_product([(m, part, number, 0)])
            replace(m, part)
